import numpy as np
import ml_dtypes


def mxq(x, axis, fmt="e4m3"):
    dtype, down = {"e4m3": (ml_dtypes.float8_e4m3fn, 7), "e5m2": (ml_dtypes.float8_e5m2, 14)}[fmt]
    v = np.moveaxis(np.asarray(x, np.float32).astype(ml_dtypes.bfloat16).astype(np.float64), axis, -1)
    blocks = v.reshape(v.shape[:-1] + (-1, 32))
    amax = np.abs(blocks).max(-1, keepdims=True)
    byte = np.maximum(np.where(amax > 0, np.frexp(amax)[1] - 1 + 127, 0) - down, 1)
    scale = np.exp2(byte - 127.0)
    codes = (blocks / scale).astype(np.float32).astype(dtype).astype(np.float64)
    return np.moveaxis((codes * scale).reshape(v.shape), -1, axis)


WIDE = False


def mx_kscale(k):
    if not WIDE:
        return np.ones(k)
    levels = np.array([10, -10, 5, -5, 0])
    if k % 512:
        return np.exp2(np.random.permutation(np.resize(levels, k // 32))).repeat(32)
    a = np.empty((k // 512, 16))
    for p in range(k // 512):
        a[p, :8] = np.random.permutation(np.resize(levels, 8))
        for g in range(8):
            far = levels[np.abs(levels - a[p, g]) >= 10]
            a[p, g + 8] = far[np.random.randint(len(far))]
    return np.exp2(a.ravel()).repeat(32)


BF16 = ml_dtypes.bfloat16


def bf(x):
    return np.asarray(x, np.float32).astype(BF16)


def f64(x):
    return np.asarray(x).astype(np.float64)


E2M1 = np.array([0.0, 0.5, 1.0, 1.5, 2.0, 3.0, 4.0, 6.0, -0.0, -0.5, -1.0, -1.5, -2.0, -3.0, -4.0, -6.0])


def pack_weight(w, fmt):
    k, n = w.shape
    w = f64(bf(w)).reshape(k // 32, 32, n)
    amax = np.abs(w).max(1)
    if fmt == "e4m3":
        byte = np.frexp(amax)[1] - 1 + 127 - 7
    else:
        mant, ex = np.frexp(amax / 6.0)
        byte = np.where(mant > 0.5, ex, ex - 1) + 127
    byte = np.clip(np.where(amax > 0, byte, 1), 1, 254)
    scaled = (w * np.exp2(127.0 - byte)[:, None, :]).reshape(k, n).astype(np.float32)
    by_word = np.ascontiguousarray(scaled.reshape(k // 512, 128, 4, n).transpose(0, 1, 3, 2))
    if fmt == "e4m3":
        words = by_word.astype(ml_dtypes.float8_e4m3fn).view(np.uint8)
    else:
        c = by_word.astype(ml_dtypes.float4_e2m1fn).view(np.uint8) & 0xF
        words = c[..., 0::2] | (c[..., 1::2] << 4)
    return np.ascontiguousarray(words), np.ascontiguousarray(byte.astype(np.uint8).reshape(k // 512, 16, n))


def unpack_weight(words, scales, fmt):
    g, p, n, _ = words.shape
    if fmt == "e4m3":
        vals = np.ascontiguousarray(words).view(ml_dtypes.float8_e4m3fn).astype(np.float64)
    else:
        nib = np.empty((g, p, n, 4), np.uint8)
        nib[..., 0::2] = words & 0xF
        nib[..., 1::2] = words >> 4
        vals = E2M1[nib]
    vals = vals * np.repeat(np.exp2(scales.astype(np.float64) - 127.0), 8, axis=1)[..., None]
    return vals.transpose(0, 1, 3, 2).reshape(g * 512, n)
def pack4(w):
    words, scales = pack_weight(w, "e2m1")
    return words.reshape(words.shape[0], 128, -1), scales


def unpack4(words, scales):
    return unpack_weight(words.reshape(words.shape[0], 128, -1, 2), scales, "e2m1")


M, K, N = 2048, 1024, 1024

FLOOR = 0.25


def setup_inputs():
    s = mx_kscale(K)
    patches = np.random.standard_normal((M, K)) * s
    d_row = np.random.standard_normal((K, N)) / np.sqrt(K) / s[:, None]
    d_col = np.random.standard_normal((K, N)) / np.sqrt(K) / s[:, None]
    d_col_words, d_col_scales = pack4(d_col)
    return {"patches": bf(patches),
            "d_row": bf(d_row),
            "d_col_words": d_col_words,
            "d_col_scales": d_col_scales}


def reference(patches, d_row, d_col_words, d_col_scales):
    x = mxq(f64(patches), 1, "e4m3")
    wr = mxq(f64(d_row), 0, "e4m3")
    wc = unpack4(d_col_words, d_col_scales)
    gr = x @ wr
    gc = x @ wc
    diagonal = gr + gc
    magnitude = np.sqrt(gr * gr + gc * gc + FLOOR * FLOOR)
    return magnitude, diagonal

@@ -1,0 +1,325 @@
+from contextlib import ExitStack
+
+import concourse.mybir as mybir
+from concourse.masks import make_identity
+
+F32 = mybir.dt.float32
+BF16 = mybir.dt.bfloat16
+U32 = mybir.dt.uint32
+I32 = mybir.dt.int32
+U8 = mybir.dt.uint8
+FP8X4 = mybir.dt.float8_e4m3fn_x4
+FP4X4 = mybir.dt.float4_e2m1fn_x4
+ACT = mybir.ActivationFunctionType
+ALU = mybir.AluOpType
+
+M, K, N = 2048, 1024, 1024
+P = 128
+PACK = 4
+K_PASS = P * PACK
+PASSES = K // K_PASS
+HALF = 512
+TILES = M // P
+FLOOR_SQUARED = 0.0625
+FLOPS = 2 * 2 * M * K * N
+S_COLS = 256
+GCB, GRB = 3, 3
+L, R, W = slice(0, HALF), slice(HALF, N), slice(0, N)
+
+
+def tile_patch_gradient_magnitude_s1_kernel(tc, patches, d_row, d_col_words, d_col_scales, out_0, out_1):
+    nc = tc.nc
+    with ExitStack() as ctx:
+        keep = ctx.enter_context(tc.tile_pool(name="keep", bufs=1))
+        stage = ctx.enter_context(tc.tile_pool(name="stage", bufs=3))
+        work = ctx.enter_context(tc.tile_pool(name="work", bufs=5))
+        outs = ctx.enter_context(tc.tile_pool(name="outs", bufs=5))
+        psum = ctx.enter_context(tc.psum_pool(name="psum", bufs=3))
+        psum_t = ctx.enter_context(tc.psum_pool(name="psum_t", bufs=2))
+
+        ident = keep.tile([P, P], F32)
+        one = keep.tile([P, 1], F32)
+        warm = keep.tile([P, 1], F32)
+        x_raw = keep.tile([P, TILES, K], BF16, align_bytes=64)
+        dr_raw = keep.tile([P, PASSES, 2, PACK, HALF], BF16, align_bytes=64)
+        dr_grouped = keep.tile([P, PASSES, 2, HALF, PACK], BF16, align_bytes=64)
+        dr_codes = keep.tile([P, PASSES, N], U32, align_bytes=64)
+        dr_scales = keep.tile([P, PASSES, N], U8, align_bytes=64)
+        dc_words = keep.tile([P, PASSES, 2 * N], U8, align_bytes=64)
+        dc_scales = keep.tile([P, PASSES, N], U8, align_bytes=64)
+
+        x_codes, x_scales, x_turned, x_grouped = {}, {}, {}, {}
+        gc_bank, gr_bank, gc_sb, gc_sq, gr_sq, total, diag, mag = {}, {}, {}, {}, {}, {}, {}, {}
+        engines = {"S": nc.scalar, "V": nc.vector, "G": nc.gpsimd}
+
+        def pair_rows(tensor, m):
+            first = m // 2 * 2 * P
+            return tensor[first : first + 2 * P, :].rearrange("(p a) k -> p a k", a=2)
+
+        def load_x(m, count):
+            nc.sync.dma_start(out=x_raw[:, m : m + count, :], in_=pair_rows(patches, m)[:, m % 2 : m % 2 + count, :])
+
+        def load_d_row(g, h):
+            rows = d_row[g * K_PASS : (g + 1) * K_PASS, h * HALF : (h + 1) * HALF]
+            nc.sync.dma_start(out=dr_raw[:, g, h, :, :], in_=rows.rearrange("(p j) w -> p j w", j=PACK))
+
+        def load_words(g):
+            nc.sync.dma_start(out=dc_words[:, g, :].bitcast(I32), in_=d_col_words[g].bitcast(I32))
+
+        def load_scales():
+            for q in range(4):
+                nc.sync.dma_start(
+                    out=dc_scales[32 * q : 32 * q + 4, :, :].bitcast(I32),
+                    in_=d_col_scales[:, 4 * q : 4 * q + 4, :].rearrange("g r n -> r g n").bitcast(I32),
+                )
+
+        def turn(m):
+            xt = psum_t.tile([P, PASSES, 2, P], F32)
+            words = x_raw[:, m, :].bitcast(F32)
+            for g in range(PASSES):
+                for u in range(2):
+                    nc.tensor.transpose(xt[:, g, u, :], words[:, 256 * g + u : 256 * (g + 1) : 2], ident[:])
+            x_turned[m] = xt
+
+        def copy_x(m, e):
+            if m // 2 not in x_grouped:
+                grouped = stage.tile([P, 2, PASSES, P, PACK], BF16, align_bytes=64)
+                codes = stage.tile([P, 2, PASSES * P], U32, align_bytes=64)
+                scales = stage.tile([P, 2, PASSES * P], U8, align_bytes=64)
+                x_grouped[m // 2], x_codes[m // 2], x_scales[m // 2] = grouped, codes, scales
+            dst = x_grouped[m // 2][:, m % 2, :, :, :].bitcast(F32)
+            src = x_turned[m][:].rearrange("p g u r -> p g r u")
+            if e == "S":
+                nc.scalar.copy(out=dst, in_=src)
+            else:
+                nc.vector.tensor_copy(out=dst, in_=src)
+
+        def quant_x(m, count=1):
+            pair, a, b = m // 2, m % 2, m % 2 + count
+            nc.vector.quantize_mx(
+                out=x_codes[pair][:, a:b, :].rearrange("p a w -> p (a w)").bitcast(FP8X4),
+                scales=x_scales[pair][:, a:b, :].rearrange("p a w -> p (a w)"),
+                in_=x_grouped[pair][:, a:b, :, :, :].rearrange("p a g r t -> p (a g r t)"),
+            )
+
+        def inter(g, h, e="S"):
+            dst = dr_grouped[:, g, h, :, :].rearrange("p (c i) t -> p c t i", i=4)
+            src = dr_raw[:, g, h, :, :].rearrange("p t (c i) -> p c t i", i=4)
+            cut = S_COLS // 4
+            if e == "S":
+                nc.scalar.copy(out=dst[:, :cut], in_=src[:, :cut])
+            else:
+                nc.gpsimd.tensor_scalar(out=dst[:, :cut], in0=src[:, :cut], scalar1=1.0, scalar2=0.0, op0=ALU.mult, op1=ALU.add)
+            nc.vector.tensor_copy(out=dst[:, cut:], in_=src[:, cut:])
+
+        def quant_d(g, h):
+            cols = slice(h * HALF, (h + 1) * HALF)
+            nc.vector.quantize_mx(
+                out=dr_codes[:, g, cols].bitcast(FP8X4),
+                scales=dr_scales[:, g, cols],
+                in_=dr_grouped[:, g, h, :, :].rearrange("p n t -> p (n t)"),
+            )
+
+        def product(acc, m, words, scales):
+            for g in range(PASSES):
+                rows = slice(g * P, (g + 1) * P)
+                nc.tensor.matmul_mx(
+                    out=acc[:],
+                    lhsT=x_codes[m // 2][:, m % 2, rows].bitcast(FP8X4),
+                    lhsT_scale=x_scales[m // 2][:, m % 2, rows],
+                    rhs=words(g),
+                    rhs_scale=scales[g],
+                    start=(g == 0),
+                    stop=(g == PASSES - 1),
+                )
+
+        def mm_gc(m, h):
+            acc_c = psum.tile([P, HALF], F32, bufs=GCB)
+            cols = slice(h * HALF, (h + 1) * HALF)
+            product(acc_c, m, lambda g: dc_words[:, g, 2 * h * HALF : 2 * (h + 1) * HALF].bitcast(FP4X4), [dc_scales[:, g, cols] for g in range(PASSES)])
+            gc_bank[m, h] = acc_c
+
+        def mm_gr(m, h):
+            acc_r = psum.tile([P, HALF], F32, bufs=GRB)
+            cols = slice(h * HALF, (h + 1) * HALF)
+            product(acc_r, m, lambda g: dr_codes[:, g, cols].bitcast(FP8X4), [dr_scales[:, g, cols] for g in range(PASSES)])
+            gr_bank[m, h] = acc_r
+
+        def copy_gc(m, h):
+            if m not in gc_sb:
+                gc = work.tile([P, N], F32)
+                gc_sb[m] = gc
+            nc.vector.tensor_copy(out=gc_sb[m][:, h * HALF : (h + 1) * HALF], in_=gc_bank[m, h][:])
+
+        def square_gc(m, cols, e="S"):
+            if m not in gc_sq:
+                gc2 = work.tile([P, N], F32)
+                gc_sq[m] = gc2
+            gc = gc_sb[m][:, cols]
+            if e == "S":
+                nc.scalar.activation(out=gc_sq[m][:, cols], in_=gc, func=ACT.Square)
+            else:
+                engines[e].tensor_tensor(out=gc_sq[m][:, cols], in0=gc, in1=gc, op=ALU.mult)
+
+        def diagonal(m, h):
+            if m not in diag:
+                dg = outs.tile([P, N], F32)
+                diag[m] = dg
+            cols = slice(h * HALF, (h + 1) * HALF)
+            nc.vector.tensor_tensor(out=diag[m][:, cols], in0=gr_bank[m, h][:], in1=gc_sb[m][:, cols], op=ALU.add)
+            if m == TILES - 1:
+                nc.sync.dma_start(out=pair_rows(out_1, m)[:, m % 2, cols], in_=diag[m][:, cols])
+            elif h == 1:
+                nc.sync.dma_start(out=pair_rows(out_1, m)[:, m % 2, :], in_=diag[m][:])
+
+        def square_gr(m, h):
+            if m not in gr_sq:
+                gr2 = work.tile([P, N], F32)
+                gr_sq[m] = gr2
+            nc.scalar.activation(out=gr_sq[m][:, h * HALF : (h + 1) * HALF], in_=gr_bank[m, h][:], func=ACT.Square)
+
+        def add_squares(m, cols, e="G"):
+            if m not in total:
+                sm = work.tile([P, N], F32)
+                total[m] = sm
+            engines[e].tensor_tensor(out=total[m][:, cols], in0=gr_sq[m][:, cols], in1=gc_sq[m][:, cols], op=ALU.add)
+
+        def root(m, cols):
+            if m not in mag:
+                mg = outs.tile([P, N], F32)
+                mag[m] = mg
+            nc.scalar.activation(out=mag[m][:, cols], in_=total[m][:, cols], func=ACT.Sqrt, bias=FLOOR_SQUARED)
+            nc.sync.dma_start(out=pair_rows(out_0, m)[:, m % 2, cols], in_=mag[m][:, cols])
+
+        nc.vector.memset(dc_scales[:].rearrange("p g n -> p (g n)").bitcast(I32), 0)
+        nc.gpsimd.memset(one[:], 1.0)
+        make_identity(nc, ident[:])
+
+        with tc.manual_schedule():
+            load_x(0, 1)
+            load_d_row(1, 0)
+            load_scales()
+            load_d_row(0, 0)
+            load_x(1, 1)
+            load_words(0)
+            load_words(1)
+            load_d_row(0, 1)
+            load_d_row(1, 1)
+            load_x(2, 2)
+            load_x(12, 2)
+            load_x(4, 2)
+            load_x(14, 2)
+            load_x(8, 2)
+            load_x(10, 2)
+            load_x(6, 2)
+            nc.scalar.activation(out=warm[:], in_=one[:], func=ACT.Sqrt, bias=FLOOR_SQUARED)
+            turn(0)
+            turn(1)
+            inter(1, 0, "S")
+            copy_x(0, "V")
+            inter(0, 0, "S")
+            copy_x(1, "S")
+            quant_x(0)
+            quant_d(1, 0)
+            mm_gc(0, 0)
+            mm_gc(0, 1)
+            quant_d(0, 0)
+            quant_x(1)
+            copy_gc(0, 0)
+            inter(0, 1, "S")
+            copy_gc(0, 1)
+            mm_gc(1, 0)
+            inter(1, 1, "S")
+            quant_d(0, 1)
+            mm_gr(1, 0)
+            mm_gr(0, 0)
+            turn(3)
+            square_gr(1, 0)
+            turn(2)
+            quant_d(1, 1)
+            mm_gr(0, 1)
+            square_gc(0, L, "S")
+            copy_x(3, "S")
+            copy_x(2, "S")
+            square_gr(0, 1)
+            copy_gc(1, 0)
+            mm_gc(1, 1)
+            square_gc(0, R, "G")
+            diagonal(0, 0)
+            square_gr(0, 0)
+            diagonal(1, 0)
+            square_gc(1, L, "S")
+            quant_x(2, 2)
+            copy_gc(1, 1)
+            add_squares(0, W, "G")
+            mm_gr(1, 1)
+            diagonal(0, 1)
+            square_gc(1, R, "S")
+            for m in range(2, TILES - 2, 2):
+                square_gr(m - 1, 1)
+                mm_gc(m, 1)
+                mm_gc(m, 0)
+                mm_gr(m, 1)
+                copy_gc(m, 1)
+                square_gr(m, 1)
+                mm_gr(m, 0)
+                turn(m + 2)
+                copy_gc(m, 0)
+                turn(m + 3)
+                diagonal(m - 1, 1)
+                diagonal(m, 0)
+                copy_x(m + 2, "V")
+                mm_gr(m + 1, 0)
+                root(m - 2, W)
+                square_gc(m, W, "S")
+                mm_gc(m + 1, 0)
+                copy_x(m + 3, "V")
+                diagonal(m, 1)
+                mm_gc(m + 1, 1)
+                quant_x(m + 2, 2)
+                square_gr(m, 0)
+                copy_gc(m + 1, 0)
+                add_squares(m - 1, W, "G")
+                copy_gc(m + 1, 1)
+                square_gr(m + 1, 0)
+                root(m - 1, W)
+                diagonal(m + 1, 0)
+                add_squares(m, W, "G")
+                square_gc(m + 1, R, "G")
+                square_gc(m + 1, L, "S")
+                mm_gr(m + 1, 1)
+            mm_gr(14, 0)
+            square_gr(13, 1)
+            mm_gc(14, 0)
+            mm_gc(14, 1)
+            copy_gc(14, 0)
+            diagonal(13, 1)
+            add_squares(13, W, "G")
+            square_gr(14, 0)
+            mm_gr(14, 1)
+            copy_gc(14, 1)
+            root(12, W)
+            mm_gc(15, 0)
+            mm_gc(15, 1)
+            diagonal(14, 0)
+            square_gr(14, 1)
+            copy_gc(15, 0)
+            mm_gr(15, 1)
+            mm_gr(15, 0)
+            square_gc(14, W, "S")
+            copy_gc(15, 1)
+            diagonal(14, 1)
+            square_gc(15, L, "S")
+            square_gr(15, 0)
+            diagonal(15, 1)
+            add_squares(14, L, "V")
+            add_squares(14, R, "V")
+            root(13, W)
+            square_gr(15, 1)
+            add_squares(15, L, "V")
+            square_gc(15, R, "V")
+            root(14, W)
+            add_squares(15, R, "V")
+            diagonal(15, 0)
+            root(15, L)
+            root(15, R)

@@ -20,11 +20,21 @@ K_PASS = P * PACK
 PASSES = K // K_PASS
 HALF = 512
 TILES = M // P
+QUAD = 4
 FLOOR_SQUARED = 0.0625
 FLOPS = 2 * 2 * M * K * N
-S_COLS = 256
-GCB, GRB = 3, 3
-L, R, W = slice(0, HALF), slice(HALF, N), slice(0, N)
+WORK_BUFS = 4
+OUT_BUFS = 5
+V_SQ = 592
+V_SQ0 = 512
+V_SQH = 128
+S_COLS = 192
+S_COLS_R = 0
+HS = 3
+HS1 = 2
+FIRST = 8
+X_AHEAD = 6
+LATE = 10
 
 
 def tile_patch_gradient_magnitude_s1_kernel(tc, patches, d_row, d_col_words, d_col_scales, out_0, out_1):
@@ -32,39 +42,40 @@ def tile_patch_gradient_magnitude_s1_kernel(tc, patches, d_row, d_col_words, d_c
     with ExitStack() as ctx:
         keep = ctx.enter_context(tc.tile_pool(name="keep", bufs=1))
         stage = ctx.enter_context(tc.tile_pool(name="stage", bufs=3))
-        work = ctx.enter_context(tc.tile_pool(name="work", bufs=5))
-        outs = ctx.enter_context(tc.tile_pool(name="outs", bufs=5))
-        psum = ctx.enter_context(tc.psum_pool(name="psum", bufs=3))
-        psum_t = ctx.enter_context(tc.psum_pool(name="psum_t", bufs=2))
+        work = ctx.enter_context(tc.tile_pool(name="work", bufs=WORK_BUFS))
+        outs = ctx.enter_context(tc.tile_pool(name="outs", bufs=OUT_BUFS))
+        psum = ctx.enter_context(tc.psum_pool(name="psum", bufs=8))
 
         ident = keep.tile([P, P], F32)
         one = keep.tile([P, 1], F32)
         warm = keep.tile([P, 1], F32)
         x_raw = keep.tile([P, TILES, K], BF16, align_bytes=64)
+        x_codes = keep.tile([P, TILES, PASSES * P], U32, align_bytes=64)
+        x_scales = keep.tile([P, TILES, PASSES * P], U8, align_bytes=64)
         dr_raw = keep.tile([P, PASSES, 2, PACK, HALF], BF16, align_bytes=64)
-        dr_grouped = keep.tile([P, PASSES, 2, HALF, PACK], BF16, align_bytes=64)
+        dr_grouped = keep.tile([P, PASSES, N, PACK], BF16, align_bytes=64)
         dr_codes = keep.tile([P, PASSES, N], U32, align_bytes=64)
         dr_scales = keep.tile([P, PASSES, N], U8, align_bytes=64)
-        dc_words = keep.tile([P, PASSES, 2 * N], U8, align_bytes=64)
+        dc_words = keep.tile([P, 2, PASSES, 2 * HALF], U8, align_bytes=64)
         dc_scales = keep.tile([P, PASSES, N], U8, align_bytes=64)
 
-        x_codes, x_scales, x_turned, x_grouped = {}, {}, {}, {}
-        gc_bank, gr_bank, gc_sb, gc_sq, gr_sq, total, diag, mag = {}, {}, {}, {}, {}, {}, {}, {}
-        engines = {"S": nc.scalar, "V": nc.vector, "G": nc.gpsimd}
+        x_turned, x_grouped = {}, {}
+        gc_bank, gr_bank, gc_sb, gc_sq, gr_sq, diag, mag = {}, {}, {}, {}, {}, {}, {}
 
-        def pair_rows(tensor, m):
-            first = m // 2 * 2 * P
-            return tensor[first : first + 2 * P, :].rearrange("(p a) k -> p a k", a=2)
+        def quad_rows(tensor, m):
+            first = m // QUAD * QUAD * P
+            return tensor[first : first + QUAD * P, :].rearrange("(p a) k -> p a k", a=QUAD)
 
         def load_x(m, count):
-            nc.sync.dma_start(out=x_raw[:, m : m + count, :], in_=pair_rows(patches, m)[:, m % 2 : m % 2 + count, :])
+            nc.sync.dma_start(out=x_raw[:, m : m + count, :], in_=quad_rows(patches, m)[:, m % QUAD : m % QUAD + count, :])
 
         def load_d_row(g, h):
             rows = d_row[g * K_PASS : (g + 1) * K_PASS, h * HALF : (h + 1) * HALF]
             nc.sync.dma_start(out=dr_raw[:, g, h, :, :], in_=rows.rearrange("(p j) w -> p j w", j=PACK))
 
-        def load_words(g):
-            nc.sync.dma_start(out=dc_words[:, g, :].bitcast(I32), in_=d_col_words[g].bitcast(I32))
+        def load_words(h):
+            half = slice(2 * h * HALF, 2 * (h + 1) * HALF)
+            nc.sync.dma_start(out=dc_words[:, h, :, :].bitcast(I32), in_=d_col_words[:, :, half].rearrange("g p w -> p g w").bitcast(I32))
 
         def load_scales():
             for q in range(4):
@@ -74,19 +85,17 @@ def tile_patch_gradient_magnitude_s1_kernel(tc, patches, d_row, d_col_words, d_c
                 )
 
         def turn(m):
-            xt = psum_t.tile([P, PASSES, 2, P], F32)
+            bank = psum.tile([P, PASSES, 2, P], F32, tag="bank")
             words = x_raw[:, m, :].bitcast(F32)
             for g in range(PASSES):
                 for u in range(2):
-                    nc.tensor.transpose(xt[:, g, u, :], words[:, 256 * g + u : 256 * (g + 1) : 2], ident[:])
-            x_turned[m] = xt
+                    nc.tensor.transpose(bank[:, g, u, :], words[:, 256 * g + u : 256 * (g + 1) : 2], ident[:])
+            x_turned[m] = bank
 
         def copy_x(m, e):
             if m // 2 not in x_grouped:
                 grouped = stage.tile([P, 2, PASSES, P, PACK], BF16, align_bytes=64)
-                codes = stage.tile([P, 2, PASSES * P], U32, align_bytes=64)
-                scales = stage.tile([P, 2, PASSES * P], U8, align_bytes=64)
-                x_grouped[m // 2], x_codes[m // 2], x_scales[m // 2] = grouped, codes, scales
+                x_grouped[m // 2] = grouped
             dst = x_grouped[m // 2][:, m % 2, :, :, :].bitcast(F32)
             src = x_turned[m][:].rearrange("p g u r -> p g r u")
             if e == "S":
@@ -94,232 +103,257 @@ def tile_patch_gradient_magnitude_s1_kernel(tc, patches, d_row, d_col_words, d_c
             else:
                 nc.vector.tensor_copy(out=dst, in_=src)
 
-        def quant_x(m, count=1):
-            pair, a, b = m // 2, m % 2, m % 2 + count
+        def quant_x(m, count):
             nc.vector.quantize_mx(
-                out=x_codes[pair][:, a:b, :].rearrange("p a w -> p (a w)").bitcast(FP8X4),
-                scales=x_scales[pair][:, a:b, :].rearrange("p a w -> p (a w)"),
-                in_=x_grouped[pair][:, a:b, :, :, :].rearrange("p a g r t -> p (a g r t)"),
+                out=x_codes[:, m : m + count, :].rearrange("p a w -> p (a w)").bitcast(FP8X4),
+                scales=x_scales[:, m : m + count, :].rearrange("p a w -> p (a w)"),
+                in_=x_grouped[m // 2][:, m % 2 : m % 2 + count, :, :, :].rearrange("p a g r t -> p (a g r t)"),
             )
 
-        def inter(g, h, e="S"):
-            dst = dr_grouped[:, g, h, :, :].rearrange("p (c i) t -> p c t i", i=4)
-            src = dr_raw[:, g, h, :, :].rearrange("p t (c i) -> p c t i", i=4)
-            cut = S_COLS // 4
+        def inter(g, h, lo, hi, e):
+            dst = dr_grouped[:, g, h * HALF + lo : h * HALF + hi, :].rearrange("p (c i) t -> p c t i", i=4)
+            src = dr_raw[:, g, h, :, lo:hi].rearrange("p t (c i) -> p c t i", i=4)
             if e == "S":
-                nc.scalar.copy(out=dst[:, :cut], in_=src[:, :cut])
+                nc.scalar.copy(out=dst, in_=src)
             else:
-                nc.gpsimd.tensor_scalar(out=dst[:, :cut], in0=src[:, :cut], scalar1=1.0, scalar2=0.0, op0=ALU.mult, op1=ALU.add)
-            nc.vector.tensor_copy(out=dst[:, cut:], in_=src[:, cut:])
+                nc.vector.tensor_copy(out=dst, in_=src)
 
         def quant_d(g, h):
             cols = slice(h * HALF, (h + 1) * HALF)
             nc.vector.quantize_mx(
                 out=dr_codes[:, g, cols].bitcast(FP8X4),
                 scales=dr_scales[:, g, cols],
-                in_=dr_grouped[:, g, h, :, :].rearrange("p n t -> p (n t)"),
+                in_=dr_grouped[:, g, cols, :].rearrange("p n t -> p (n t)"),
             )
 
-        def product(acc, m, words, scales):
+        def product(m, words, scales):
+            bank = psum.tile([P, HALF], F32, tag="bank")
             for g in range(PASSES):
                 rows = slice(g * P, (g + 1) * P)
                 nc.tensor.matmul_mx(
-                    out=acc[:],
-                    lhsT=x_codes[m // 2][:, m % 2, rows].bitcast(FP8X4),
-                    lhsT_scale=x_scales[m // 2][:, m % 2, rows],
-                    rhs=words(g),
+                    out=bank[:],
+                    lhsT=x_codes[:, m, rows].bitcast(FP8X4),
+                    lhsT_scale=x_scales[:, m, rows],
+                    rhs=words[g],
                     rhs_scale=scales[g],
                     start=(g == 0),
                     stop=(g == PASSES - 1),
                 )
+            return bank
 
-        def mm_gc(m, h):
-            acc_c = psum.tile([P, HALF], F32, bufs=GCB)
+        def unit(s, j):
+            if s < FIRST:
+                return 2 * (s % (FIRST // 2)) + j, s // (FIRST // 2)
+            return s, j
+
+        def step_rows(tensor, s, lo, hi):
+            m, h = unit(s, lo)
+            rows = quad_rows(tensor, m)
+            if s < FIRST:
+                return rows[:, m % QUAD : m % QUAD + hi - lo, h * HALF : (h + 1) * HALF]
+            return rows[:, m % QUAD, lo * HALF : hi * HALF].rearrange("p (j n) -> p j n", n=HALF)
+
+        def mm_gc(s, j):
+            m, h = unit(s, j)
             cols = slice(h * HALF, (h + 1) * HALF)
-            product(acc_c, m, lambda g: dc_words[:, g, 2 * h * HALF : 2 * (h + 1) * HALF].bitcast(FP4X4), [dc_scales[:, g, cols] for g in range(PASSES)])
-            gc_bank[m, h] = acc_c
+            words = [dc_words[:, h, g, :].bitcast(FP4X4) for g in range(PASSES)]
+            gc_bank[s, j] = product(m, words, [dc_scales[:, g, cols] for g in range(PASSES)])
 
-        def mm_gr(m, h):
-            acc_r = psum.tile([P, HALF], F32, bufs=GRB)
+        def mm_gr(s, j):
+            m, h = unit(s, j)
             cols = slice(h * HALF, (h + 1) * HALF)
-            product(acc_r, m, lambda g: dr_codes[:, g, cols].bitcast(FP8X4), [dr_scales[:, g, cols] for g in range(PASSES)])
-            gr_bank[m, h] = acc_r
+            words = [dr_codes[:, g, cols].bitcast(FP8X4) for g in range(PASSES)]
+            gr_bank[s, j] = product(m, words, [dr_scales[:, g, cols] for g in range(PASSES)])
 
-        def copy_gc(m, h):
-            if m not in gc_sb:
+        def copy_gc(s, j, e="V"):
+            if s not in gc_sb:
                 gc = work.tile([P, N], F32)
-                gc_sb[m] = gc
-            nc.vector.tensor_copy(out=gc_sb[m][:, h * HALF : (h + 1) * HALF], in_=gc_bank[m, h][:])
-
-        def square_gc(m, cols, e="S"):
-            if m not in gc_sq:
-                gc2 = work.tile([P, N], F32)
-                gc_sq[m] = gc2
-            gc = gc_sb[m][:, cols]
+                gc_sb[s] = gc
+            dst = gc_sb[s][:, j * HALF : (j + 1) * HALF]
             if e == "S":
-                nc.scalar.activation(out=gc_sq[m][:, cols], in_=gc, func=ACT.Square)
+                nc.scalar.copy(out=dst, in_=gc_bank[s, j][:])
             else:
-                engines[e].tensor_tensor(out=gc_sq[m][:, cols], in0=gc, in1=gc, op=ALU.mult)
+                nc.vector.tensor_copy(out=dst, in_=gc_bank[s, j][:])
 
-        def diagonal(m, h):
-            if m not in diag:
+        def square_gc(s, lo, hi, e):
+            if hi <= lo:
+                return
+            if s not in gc_sq:
+                gc2 = work.tile([P, N], F32)
+                gc_sq[s] = gc2
+            gc, dst = gc_sb[s][:, lo:hi], gc_sq[s][:, lo:hi]
+            if e == "S":
+                nc.scalar.activation(out=dst, in_=gc, func=ACT.Square)
+            elif e == "V":
+                for j in range(2):
+                    a, b = max(lo, j * HALF), min(hi, (j + 1) * HALF)
+                    if a < b:
+                        nc.vector.tensor_tensor(out=gc_sq[s][:, a:b], in0=gc_bank[s, j][:, a - j * HALF : b - j * HALF], in1=gc_sb[s][:, a:b], op=ALU.mult)
+            else:
+                nc.gpsimd.tensor_tensor(out=dst, in0=gc, in1=gc, op=ALU.mult)
+
+        def store(tensor, tile, s, lo, hi):
+            nc.sync.dma_start(out=step_rows(tensor, s, lo, hi), in_=tile[:, lo * HALF : hi * HALF].rearrange("p (j n) -> p j n", n=HALF))
+
+        def diagonal(s, j, first=None):
+            if s not in diag:
                 dg = outs.tile([P, N], F32)
-                diag[m] = dg
-            cols = slice(h * HALF, (h + 1) * HALF)
-            nc.vector.tensor_tensor(out=diag[m][:, cols], in0=gr_bank[m, h][:], in1=gc_sb[m][:, cols], op=ALU.add)
-            if m == TILES - 1:
-                nc.sync.dma_start(out=pair_rows(out_1, m)[:, m % 2, cols], in_=diag[m][:, cols])
-            elif h == 1:
-                nc.sync.dma_start(out=pair_rows(out_1, m)[:, m % 2, :], in_=diag[m][:])
+                diag[s] = dg
+            cols = slice(j * HALF, (j + 1) * HALF)
+            nc.vector.tensor_tensor(out=diag[s][:, cols], in0=gr_bank[s, j][:], in1=gc_sb[s][:, cols], op=ALU.add)
+            if first is not None:
+                store(out_1, diag[s], s, first, j + 1)
 
-        def square_gr(m, h):
-            if m not in gr_sq:
+        def square_gr(s, j):
+            if s not in gr_sq:
                 gr2 = work.tile([P, N], F32)
-                gr_sq[m] = gr2
-            nc.scalar.activation(out=gr_sq[m][:, h * HALF : (h + 1) * HALF], in_=gr_bank[m, h][:], func=ACT.Square)
+                gr_sq[s] = gr2
+            nc.scalar.activation(out=gr_sq[s][:, j * HALF : (j + 1) * HALF], in_=gr_bank[s, j][:], func=ACT.Square)
 
-        def add_squares(m, cols, e="G"):
-            if m not in total:
-                sm = work.tile([P, N], F32)
-                total[m] = sm
-            engines[e].tensor_tensor(out=total[m][:, cols], in0=gr_sq[m][:, cols], in1=gc_sq[m][:, cols], op=ALU.add)
+        def add_squares(s, lo, hi, e):
+            engine = nc.gpsimd if e == "G" else nc.vector
+            cols = slice(lo * HALF, hi * HALF)
+            engine.tensor_tensor(out=gr_sq[s][:, cols], in0=gr_sq[s][:, cols], in1=gc_sq[s][:, cols], op=ALU.add)
 
-        def root(m, cols):
-            if m not in mag:
+        def root(s, lo, hi):
+            if s not in mag:
                 mg = outs.tile([P, N], F32)
-                mag[m] = mg
-            nc.scalar.activation(out=mag[m][:, cols], in_=total[m][:, cols], func=ACT.Sqrt, bias=FLOOR_SQUARED)
-            nc.sync.dma_start(out=pair_rows(out_0, m)[:, m % 2, cols], in_=mag[m][:, cols])
+                mag[s] = mg
+            cols = slice(lo * HALF, hi * HALF)
+            nc.scalar.activation(out=mag[s][:, cols], in_=gr_sq[s][:, cols], func=ACT.Sqrt, bias=FLOOR_SQUARED)
+            if s == TILES - 1:
+                store(out_0, mag[s], s, lo, hi)
+            elif hi == 2:
+                store(out_0, mag[s], s, 0, 2)
+
+        def group_d(g, h, s_cols):
+            if s_cols:
+                inter(g, h, 0, s_cols, "S")
+            inter(g, h, s_cols, HALF, "V")
 
         nc.vector.memset(dc_scales[:].rearrange("p g n -> p (g n)").bitcast(I32), 0)
         nc.gpsimd.memset(one[:], 1.0)
         make_identity(nc, ident[:])
 
         with tc.manual_schedule():
-            load_x(0, 1)
-            load_d_row(1, 0)
-            load_scales()
+            load_x(0, 2)
             load_d_row(0, 0)
-            load_x(1, 1)
+            load_scales()
             load_words(0)
-            load_words(1)
-            load_d_row(0, 1)
-            load_d_row(1, 1)
+            load_d_row(1, 0)
             load_x(2, 2)
-            load_x(12, 2)
+            load_d_row(0, 1)
             load_x(4, 2)
-            load_x(14, 2)
-            load_x(8, 2)
-            load_x(10, 2)
+            load_d_row(1, 1)
             load_x(6, 2)
+            load_words(1)
+            load_x(8, QUAD)
+            load_x(12, QUAD)
             nc.scalar.activation(out=warm[:], in_=one[:], func=ACT.Sqrt, bias=FLOOR_SQUARED)
             turn(0)
             turn(1)
-            inter(1, 0, "S")
             copy_x(0, "V")
-            inter(0, 0, "S")
+            group_d(0, 0, S_COLS)
             copy_x(1, "S")
-            quant_x(0)
-            quant_d(1, 0)
+            quant_x(0, 1)
             mm_gc(0, 0)
-            mm_gc(0, 1)
             quant_d(0, 0)
-            quant_x(1)
-            copy_gc(0, 0)
-            inter(0, 1, "S")
-            copy_gc(0, 1)
-            mm_gc(1, 0)
-            inter(1, 1, "S")
-            quant_d(0, 1)
-            mm_gr(1, 0)
-            mm_gr(0, 0)
-            turn(3)
-            square_gr(1, 0)
+            quant_x(1, 1)
+            mm_gc(0, 1)
+            group_d(1, 0, S_COLS)
             turn(2)
-            quant_d(1, 1)
+            turn(3)
+            copy_gc(0, 0)
+            quant_d(1, 0)
+            mm_gr(0, 0)
             mm_gr(0, 1)
-            square_gc(0, L, "S")
+            copy_gc(0, 1, "S")
+            copy_x(2, "V")
+            square_gc(0, 0, N, "S")
             copy_x(3, "S")
-            copy_x(2, "S")
-            square_gr(0, 1)
-            copy_gc(1, 0)
-            mm_gc(1, 1)
-            square_gc(0, R, "G")
-            diagonal(0, 0)
-            square_gr(0, 0)
-            diagonal(1, 0)
-            square_gc(1, L, "S")
+            group_d(0, 1, 0)
             quant_x(2, 2)
-            copy_gc(1, 1)
-            add_squares(0, W, "G")
+            turn(4)
+            turn(5)
+            mm_gc(1, 0)
+            mm_gc(1, 1)
+            square_gr(0, 0)
+            square_gr(0, 1)
+            add_squares(0, 0, 2, "G")
+            diagonal(0, 0)
+            mm_gr(1, 0)
+            diagonal(0, 1, 0)
             mm_gr(1, 1)
-            diagonal(0, 1)
-            square_gc(1, R, "S")
-            for m in range(2, TILES - 2, 2):
-                square_gr(m - 1, 1)
-                mm_gc(m, 1)
-                mm_gc(m, 0)
-                mm_gr(m, 1)
-                copy_gc(m, 1)
-                square_gr(m, 1)
-                mm_gr(m, 0)
-                turn(m + 2)
-                copy_gc(m, 0)
-                turn(m + 3)
-                diagonal(m - 1, 1)
-                diagonal(m, 0)
-                copy_x(m + 2, "V")
-                mm_gr(m + 1, 0)
-                root(m - 2, W)
-                square_gc(m, W, "S")
-                mm_gc(m + 1, 0)
-                copy_x(m + 3, "V")
-                diagonal(m, 1)
-                mm_gc(m + 1, 1)
-                quant_x(m + 2, 2)
-                square_gr(m, 0)
-                copy_gc(m + 1, 0)
-                add_squares(m - 1, W, "G")
-                copy_gc(m + 1, 1)
-                square_gr(m + 1, 0)
-                root(m - 1, W)
-                diagonal(m + 1, 0)
-                add_squares(m, W, "G")
-                square_gc(m + 1, R, "G")
-                square_gc(m + 1, L, "S")
-                mm_gr(m + 1, 1)
-            mm_gr(14, 0)
-            square_gr(13, 1)
-            mm_gc(14, 0)
-            mm_gc(14, 1)
-            copy_gc(14, 0)
-            diagonal(13, 1)
-            add_squares(13, W, "G")
-            square_gr(14, 0)
-            mm_gr(14, 1)
-            copy_gc(14, 1)
-            root(12, W)
-            mm_gc(15, 0)
-            mm_gc(15, 1)
-            diagonal(14, 0)
-            square_gr(14, 1)
-            copy_gc(15, 0)
-            mm_gr(15, 1)
-            mm_gr(15, 0)
-            square_gc(14, W, "S")
-            copy_gc(15, 1)
-            diagonal(14, 1)
-            square_gc(15, L, "S")
-            square_gr(15, 0)
-            diagonal(15, 1)
-            add_squares(14, L, "V")
-            add_squares(14, R, "V")
-            root(13, W)
-            square_gr(15, 1)
-            add_squares(15, L, "V")
-            square_gc(15, R, "V")
-            root(14, W)
-            add_squares(15, R, "V")
-            diagonal(15, 0)
-            root(15, L)
-            root(15, R)
+            copy_x(4, "S")
+            copy_x(5, "S")
+            copy_gc(1, 0, "S")
+            copy_gc(1, 1)
+            turn(6)
+            turn(7)
+            quant_x(4, 2)
+            quant_d(0, 1)
+            mm_gc(2, 0)
+            square_gr(1, 0)
+            square_gr(1, 1)
+            square_gc(1, 0, N - V_SQH, "S")
+            copy_x(6, "S")
+            copy_x(7, "S")
+            diagonal(1, 0)
+            mm_gr(2, 0)
+            group_d(1, 1, S_COLS_R)
+            diagonal(1, 1, 0)
+            mm_gc(2, 1)
+            mm_gr(2, 1)
+            quant_d(1, 1)
+            square_gc(1, N - V_SQH, N, "V")
+            quant_x(6, 2)
+            add_squares(1, 0, 2, "G")
+            turn(8)
+            rooted = 0
+            for s in range(2, TILES):
+                nxt = s + 1 < TILES
+                last = s == TILES - 1
+                m = s + X_AHEAD
+                late = s >= LATE
+                v_sq = V_SQ if m < TILES else V_SQ0
+                if s == LATE + 1:
+                    v_sq = N
+                if nxt:
+                    mm_gc(s + 1, 0)
+                copy_gc(s, 0, "S" if s < HS else "V")
+                square_gr(s, 0)
+                if nxt:
+                    mm_gr(s + 1, 0)
+                copy_gc(s, 1, "S" if s < HS1 else "V")
+                square_gr(s, 1)
+                diagonal(s, 0, 0 if last else None)
+                if nxt:
+                    mm_gc(s + 1, 1)
+                if m < TILES:
+                    copy_x(m, "S")
+                square_gc(s, 0, N - v_sq, "S")
+                if late and v_sq <= HALF:
+                    add_squares(s, 0, 1, "G")
+                diagonal(s, 1, 1 if last else 0)
+                while rooted < s - 1:
+                    root(rooted, 0, 2)
+                    rooted = rooted + 1
+                if s > LATE:
+                    root(s - 1, 0, 1)
+                    root(s - 1, 1, 2)
+                    rooted = s
+                if nxt:
+                    mm_gr(s + 1, 1)
+                if m + 1 < TILES:
+                    turn(m + 1)
+                square_gc(s, N - v_sq, N, "V")
+                if m < TILES:
+                    quant_x(m, 1)
+                if not late:
+                    add_squares(s, 0, 2, "G")
+                else:
+                    if v_sq > HALF:
+                        add_squares(s, 0, 1, "G")
+                    add_squares(s, 1, 2, "V" if last else "G")
+            root(TILES - 1, 0, 1)
+            root(TILES - 1, 1, 2)

@@ -25,16 +25,18 @@ FLOOR_SQUARED = 0.0625
 FLOPS = 2 * 2 * M * K * N
 WORK_BUFS = 4
 OUT_BUFS = 5
-V_SQ = 592
+V_SQ = 736
 V_SQ0 = 512
+G_SQ = 0
 V_SQH = 128
 S_COLS = 192
 S_COLS_R = 0
 HS = 3
 HS1 = 2
 FIRST = 8
-X_AHEAD = 6
-LATE = 10
+X_FROM = 2
+X_EVERY = 3
+LATE = 12
 
 
 def tile_patch_gradient_magnitude_s1_kernel(tc, patches, d_row, d_col_words, d_col_scales, out_0, out_1):
@@ -115,6 +117,8 @@ def tile_patch_gradient_magnitude_s1_kernel(tc, patches, d_row, d_col_words, d_c
             src = dr_raw[:, g, h, :, lo:hi].rearrange("p t (c i) -> p c t i", i=4)
             if e == "S":
                 nc.scalar.copy(out=dst, in_=src)
+            elif e == "G":
+                nc.gpsimd.tensor_scalar(out=dst, in0=src, scalar1=1.0, scalar2=0.0, op0=ALU.mult, op1=ALU.add)
             else:
                 nc.vector.tensor_copy(out=dst, in_=src)
 
@@ -308,14 +312,24 @@ def tile_patch_gradient_magnitude_s1_kernel(tc, patches, d_row, d_col_words, d_c
             square_gc(1, N - V_SQH, N, "V")
             quant_x(6, 2)
             add_squares(1, 0, 2, "G")
-            turn(8)
+            def x_pair(s):
+                if s >= X_FROM and (s - X_FROM) % X_EVERY == 0:
+                    m = FIRST + 2 * ((s - X_FROM) // X_EVERY)
+                    if m < TILES:
+                        return [m, m + 1]
+                return []
+
+
+            for m in x_pair(2):
+                turn(m)
             rooted = 0
             for s in range(2, TILES):
                 nxt = s + 1 < TILES
                 last = s == TILES - 1
-                m = s + X_AHEAD
+                tiles = x_pair(s)
                 late = s >= LATE
-                v_sq = V_SQ if m < TILES else V_SQ0
+                v_sq = V_SQ if tiles else V_SQ0
+                g_sq = G_SQ if tiles else 0
                 if s == LATE + 1:
                     v_sq = N
                 if nxt:
@@ -327,11 +341,12 @@ def tile_patch_gradient_magnitude_s1_kernel(tc, patches, d_row, d_col_words, d_c
                 copy_gc(s, 1, "S" if s < HS1 else "V")
                 square_gr(s, 1)
                 diagonal(s, 0, 0 if last else None)
+                for m in tiles:
+                    copy_x(m, "S")
                 if nxt:
                     mm_gc(s + 1, 1)
-                if m < TILES:
-                    copy_x(m, "S")
-                square_gc(s, 0, N - v_sq, "S")
+                square_gc(s, 0, g_sq, "G")
+                square_gc(s, g_sq, N - v_sq, "S")
                 if late and v_sq <= HALF:
                     add_squares(s, 0, 1, "G")
                 diagonal(s, 1, 1 if last else 0)
@@ -344,11 +359,11 @@ def tile_patch_gradient_magnitude_s1_kernel(tc, patches, d_row, d_col_words, d_c
                     rooted = s
                 if nxt:
                     mm_gr(s + 1, 1)
-                if m + 1 < TILES:
-                    turn(m + 1)
                 square_gc(s, N - v_sq, N, "V")
-                if m < TILES:
-                    quant_x(m, 1)
+                for m in x_pair(s + 1):
+                    turn(m)
+                if tiles:
+                    quant_x(tiles[0], 2)
                 if not late:
                     add_squares(s, 0, 2, "G")
                 else:

@@ -23,20 +23,15 @@ TILES = M // P
 QUAD = 4
 FLOOR_SQUARED = 0.0625
 FLOPS = 2 * 2 * M * K * N
-WORK_BUFS = 4
-OUT_BUFS = 5
 V_SQ = 736
 V_SQ0 = 512
-G_SQ = 0
 V_SQH = 128
 S_COLS = 192
-S_COLS_R = 0
-HS = 3
-HS1 = 2
-FIRST = 8
+S_COLS_R = 128
+FIRST = 4
 X_FROM = 2
-X_EVERY = 3
-LATE = 12
+X_EVERY = 2
+LATE = 13
 
 
 def tile_patch_gradient_magnitude_s1_kernel(tc, patches, d_row, d_col_words, d_col_scales, out_0, out_1):
@@ -44,8 +39,8 @@ def tile_patch_gradient_magnitude_s1_kernel(tc, patches, d_row, d_col_words, d_c
     with ExitStack() as ctx:
         keep = ctx.enter_context(tc.tile_pool(name="keep", bufs=1))
         stage = ctx.enter_context(tc.tile_pool(name="stage", bufs=3))
-        work = ctx.enter_context(tc.tile_pool(name="work", bufs=WORK_BUFS))
-        outs = ctx.enter_context(tc.tile_pool(name="outs", bufs=OUT_BUFS))
+        work = ctx.enter_context(tc.tile_pool(name="work", bufs=4))
+        outs = ctx.enter_context(tc.tile_pool(name="outs", bufs=TILES))
         psum = ctx.enter_context(tc.psum_pool(name="psum", bufs=8))
 
         ident = keep.tile([P, P], F32)
@@ -54,15 +49,13 @@ def tile_patch_gradient_magnitude_s1_kernel(tc, patches, d_row, d_col_words, d_c
         x_raw = keep.tile([P, TILES, K], BF16, align_bytes=64)
         x_codes = keep.tile([P, TILES, PASSES * P], U32, align_bytes=64)
         x_scales = keep.tile([P, TILES, PASSES * P], U8, align_bytes=64)
-        dr_raw = keep.tile([P, PASSES, 2, PACK, HALF], BF16, align_bytes=64)
-        dr_grouped = keep.tile([P, PASSES, N, PACK], BF16, align_bytes=64)
         dr_codes = keep.tile([P, PASSES, N], U32, align_bytes=64)
         dr_scales = keep.tile([P, PASSES, N], U8, align_bytes=64)
         dc_words = keep.tile([P, 2, PASSES, 2 * HALF], U8, align_bytes=64)
         dc_scales = keep.tile([P, PASSES, N], U8, align_bytes=64)
 
-        x_turned, x_grouped = {}, {}
-        gc_bank, gr_bank, gc_sb, gc_sq, gr_sq, diag, mag = {}, {}, {}, {}, {}, {}, {}
+        x_turned, x_grouped, dr_raw, dr_grouped = {}, {}, {}, {}
+        gc_bank, gr_bank, gc_sb, gc_sq, gr_sq, diag = {}, {}, {}, {}, {}, {}
 
         def quad_rows(tensor, m):
             first = m // QUAD * QUAD * P
@@ -73,7 +66,9 @@ def tile_patch_gradient_magnitude_s1_kernel(tc, patches, d_row, d_col_words, d_c
 
         def load_d_row(g, h):
             rows = d_row[g * K_PASS : (g + 1) * K_PASS, h * HALF : (h + 1) * HALF]
-            nc.sync.dma_start(out=dr_raw[:, g, h, :, :], in_=rows.rearrange("(p j) w -> p j w", j=PACK))
+            raw = outs.tile([P, PACK, HALF], BF16, tag="diag", align_bytes=64)
+            dr_raw[g, h] = raw
+            nc.sync.dma_start(out=raw[:], in_=rows.rearrange("(p j) w -> p j w", j=PACK))
 
         def load_words(h):
             half = slice(2 * h * HALF, 2 * (h + 1) * HALF)
@@ -113,8 +108,11 @@ def tile_patch_gradient_magnitude_s1_kernel(tc, patches, d_row, d_col_words, d_c
             )
 
         def inter(g, h, lo, hi, e):
-            dst = dr_grouped[:, g, h * HALF + lo : h * HALF + hi, :].rearrange("p (c i) t -> p c t i", i=4)
-            src = dr_raw[:, g, h, :, lo:hi].rearrange("p t (c i) -> p c t i", i=4)
+            if (g, h) not in dr_grouped:
+                grouped = outs.tile([P, HALF, PACK], BF16, tag="diag", align_bytes=64)
+                dr_grouped[g, h] = grouped
+            dst = dr_grouped[g, h][:, lo:hi, :].rearrange("p (c i) t -> p c t i", i=4)
+            src = dr_raw[g, h][:, :, lo:hi].rearrange("p t (c i) -> p c t i", i=4)
             if e == "S":
                 nc.scalar.copy(out=dst, in_=src)
             elif e == "G":
@@ -127,7 +125,7 @@ def tile_patch_gradient_magnitude_s1_kernel(tc, patches, d_row, d_col_words, d_c
             nc.vector.quantize_mx(
                 out=dr_codes[:, g, cols].bitcast(FP8X4),
                 scales=dr_scales[:, g, cols],
-                in_=dr_grouped[:, g, cols, :].rearrange("p n t -> p (n t)"),
+                in_=dr_grouped[g, h][:].rearrange("p n t -> p (n t)"),
             )
 
         def product(m, words, scales):
@@ -171,7 +169,7 @@ def tile_patch_gradient_magnitude_s1_kernel(tc, patches, d_row, d_col_words, d_c
 
         def copy_gc(s, j, e="V"):
             if s not in gc_sb:
-                gc = work.tile([P, N], F32)
+                gc = work.tile([P, N], F32, bufs=3)
                 gc_sb[s] = gc
             dst = gc_sb[s][:, j * HALF : (j + 1) * HALF]
             if e == "S":
@@ -199,18 +197,18 @@ def tile_patch_gradient_magnitude_s1_kernel(tc, patches, d_row, d_col_words, d_c
         def store(tensor, tile, s, lo, hi):
             nc.sync.dma_start(out=step_rows(tensor, s, lo, hi), in_=tile[:, lo * HALF : hi * HALF].rearrange("p (j n) -> p j n", n=HALF))
 
-        def diagonal(s, j, first=None):
+        def diagonal(s, j, stored=None):
             if s not in diag:
-                dg = outs.tile([P, N], F32)
+                dg = outs.tile([P, N], F32, tag="diag", align_bytes=64)
                 diag[s] = dg
             cols = slice(j * HALF, (j + 1) * HALF)
             nc.vector.tensor_tensor(out=diag[s][:, cols], in0=gr_bank[s, j][:], in1=gc_sb[s][:, cols], op=ALU.add)
-            if first is not None:
-                store(out_1, diag[s], s, first, j + 1)
+            if stored is not None:
+                store(out_1, diag[s], s, stored[0], stored[1])
 
         def square_gr(s, j):
             if s not in gr_sq:
-                gr2 = work.tile([P, N], F32)
+                gr2 = outs.tile([P, N], F32)
                 gr_sq[s] = gr2
             nc.scalar.activation(out=gr_sq[s][:, j * HALF : (j + 1) * HALF], in_=gr_bank[s, j][:], func=ACT.Square)
 
@@ -220,15 +218,12 @@ def tile_patch_gradient_magnitude_s1_kernel(tc, patches, d_row, d_col_words, d_c
             engine.tensor_tensor(out=gr_sq[s][:, cols], in0=gr_sq[s][:, cols], in1=gc_sq[s][:, cols], op=ALU.add)
 
         def root(s, lo, hi):
-            if s not in mag:
-                mg = outs.tile([P, N], F32)
-                mag[s] = mg
             cols = slice(lo * HALF, hi * HALF)
-            nc.scalar.activation(out=mag[s][:, cols], in_=gr_sq[s][:, cols], func=ACT.Sqrt, bias=FLOOR_SQUARED)
+            nc.scalar.activation(out=gr_sq[s][:, cols], in_=gr_sq[s][:, cols], func=ACT.Sqrt, bias=FLOOR_SQUARED)
             if s == TILES - 1:
-                store(out_0, mag[s], s, lo, hi)
+                store(out_0, gr_sq[s], s, lo, hi)
             elif hi == 2:
-                store(out_0, mag[s], s, 0, 2)
+                store(out_0, gr_sq[s], s, 0, 2)
 
         def group_d(g, h, s_cols):
             if s_cols:
@@ -247,10 +242,10 @@ def tile_patch_gradient_magnitude_s1_kernel(tc, patches, d_row, d_col_words, d_c
             load_d_row(1, 0)
             load_x(2, 2)
             load_d_row(0, 1)
-            load_x(4, 2)
             load_d_row(1, 1)
-            load_x(6, 2)
             load_words(1)
+            load_x(4, 2)
+            load_x(6, 2)
             load_x(8, QUAD)
             load_x(12, QUAD)
             nc.scalar.activation(out=warm[:], in_=one[:], func=ACT.Sqrt, bias=FLOOR_SQUARED)
@@ -273,44 +268,35 @@ def tile_patch_gradient_magnitude_s1_kernel(tc, patches, d_row, d_col_words, d_c
             mm_gr(0, 1)
             copy_gc(0, 1, "S")
             copy_x(2, "V")
-            square_gc(0, 0, N, "S")
+            square_gc(0, 0, HALF, "S")
             copy_x(3, "S")
             group_d(0, 1, 0)
             quant_x(2, 2)
-            turn(4)
-            turn(5)
             mm_gc(1, 0)
             mm_gc(1, 1)
+            mm_gr(1, 0)
+            mm_gr(1, 1)
             square_gr(0, 0)
             square_gr(0, 1)
-            add_squares(0, 0, 2, "G")
-            diagonal(0, 0)
-            mm_gr(1, 0)
-            diagonal(0, 1, 0)
-            mm_gr(1, 1)
-            copy_x(4, "S")
-            copy_x(5, "S")
-            copy_gc(1, 0, "S")
-            copy_gc(1, 1)
-            turn(6)
-            turn(7)
-            quant_x(4, 2)
+            square_gc(0, HALF, N - V_SQH, "S")
             quant_d(0, 1)
+            group_d(1, 1, S_COLS_R)
+            square_gc(0, N - V_SQH, N, "V")
+            quant_d(1, 1)
+            add_squares(0, 0, 2, "G")
+            copy_gc(1, 0, "S")
+            copy_gc(1, 1, "S")
+            diagonal(0, 0)
+            mm_gc(2, 1)
             mm_gc(2, 0)
+            diagonal(0, 1, (0, 2))
+            mm_gr(2, 0)
             square_gr(1, 0)
             square_gr(1, 1)
-            square_gc(1, 0, N - V_SQH, "S")
-            copy_x(6, "S")
-            copy_x(7, "S")
+            square_gc(1, 0, N, "S")
             diagonal(1, 0)
-            mm_gr(2, 0)
-            group_d(1, 1, S_COLS_R)
-            diagonal(1, 1, 0)
-            mm_gc(2, 1)
             mm_gr(2, 1)
-            quant_d(1, 1)
-            square_gc(1, N - V_SQH, N, "V")
-            quant_x(6, 2)
+            diagonal(1, 1, (0, 2))
             add_squares(1, 0, 2, "G")
             def x_pair(s):
                 if s >= X_FROM and (s - X_FROM) % X_EVERY == 0:
@@ -322,53 +308,49 @@ def tile_patch_gradient_magnitude_s1_kernel(tc, patches, d_row, d_col_words, d_c
 
             for m in x_pair(2):
                 turn(m)
-            rooted = 0
             for s in range(2, TILES):
                 nxt = s + 1 < TILES
                 last = s == TILES - 1
                 tiles = x_pair(s)
-                late = s >= LATE
                 v_sq = V_SQ if tiles else V_SQ0
-                g_sq = G_SQ if tiles else 0
-                if s == LATE + 1:
+                if s == LATE:
                     v_sq = N
                 if nxt:
-                    mm_gc(s + 1, 0)
-                copy_gc(s, 0, "S" if s < HS else "V")
-                square_gr(s, 0)
+                    mm_gc(s + 1, 1)
+                copy_gc(s, 0)
                 if nxt:
-                    mm_gr(s + 1, 0)
-                copy_gc(s, 1, "S" if s < HS1 else "V")
+                    mm_gc(s + 1, 0)
+                copy_gc(s, 1)
                 square_gr(s, 1)
-                diagonal(s, 0, 0 if last else None)
+                square_gr(s, 0)
                 for m in tiles:
                     copy_x(m, "S")
+                if s < LATE and not tiles:
+                    root(s - 2, 0, 2)
+                square_gc(s, v_sq, N, "S")
+                square_gc(s, 0, HALF, "V")
+                diagonal(s, 0, (0, 1) if last else None)
                 if nxt:
-                    mm_gc(s + 1, 1)
-                square_gc(s, 0, g_sq, "G")
-                square_gc(s, g_sq, N - v_sq, "S")
-                if late and v_sq <= HALF:
-                    add_squares(s, 0, 1, "G")
-                diagonal(s, 1, 1 if last else 0)
-                while rooted < s - 1:
-                    root(rooted, 0, 2)
-                    rooted = rooted + 1
-                if s > LATE:
-                    root(s - 1, 0, 1)
-                    root(s - 1, 1, 2)
-                    rooted = s
+                    mm_gr(s + 1, 0)
+                if s == LATE:
+                    square_gc(s, HALF, v_sq, "V")
+                if s >= LATE and not last:
+                    add_squares(s, 0, 2, "G")
+                diagonal(s, 1, (1, 2) if last else (0, 2))
                 if nxt:
                     mm_gr(s + 1, 1)
-                square_gc(s, N - v_sq, N, "V")
+                if s < LATE:
+                    square_gc(s, HALF, v_sq, "V")
+                    if tiles:
+                        quant_x(tiles[0], 2)
+                    add_squares(s, 0, 2, "G")
+                if tiles or s == LATE:
+                    root(s - 2, 0, 2)
+                if s >= LATE:
+                    root(s - 1, 0, 2)
                 for m in x_pair(s + 1):
                     turn(m)
-                if tiles:
-                    quant_x(tiles[0], 2)
-                if not late:
-                    add_squares(s, 0, 2, "G")
-                else:
-                    if v_sq > HALF:
-                        add_squares(s, 0, 1, "G")
-                    add_squares(s, 1, 2, "V" if last else "G")
+            add_squares(TILES - 1, 0, 1, "V")
+            add_squares(TILES - 1, 1, 2, "V")
             root(TILES - 1, 0, 1)
             root(TILES - 1, 1, 2)

@@ -23,22 +23,19 @@ TILES = M // P
 QUAD = 4
 FLOOR_SQUARED = 0.0625
 FLOPS = 2 * 2 * M * K * N
-V_SQ = 736
-V_SQ0 = 512
+S_SQ = 304
+S_SQ0 = 512
 V_SQH = 128
 S_COLS = 192
-S_COLS_R = 128
+S_COLS_R = 192
 FIRST = 4
-X_FROM = 2
-X_EVERY = 2
-LATE = 13
 
 
 def tile_patch_gradient_magnitude_s1_kernel(tc, patches, d_row, d_col_words, d_col_scales, out_0, out_1):
     nc = tc.nc
     with ExitStack() as ctx:
         keep = ctx.enter_context(tc.tile_pool(name="keep", bufs=1))
-        stage = ctx.enter_context(tc.tile_pool(name="stage", bufs=3))
+        stage = ctx.enter_context(tc.tile_pool(name="stage", bufs=2))
         work = ctx.enter_context(tc.tile_pool(name="work", bufs=4))
         outs = ctx.enter_context(tc.tile_pool(name="outs", bufs=TILES))
         psum = ctx.enter_context(tc.psum_pool(name="psum", bufs=8))
@@ -169,7 +166,7 @@ def tile_patch_gradient_magnitude_s1_kernel(tc, patches, d_row, d_col_words, d_c
 
         def copy_gc(s, j, e="V"):
             if s not in gc_sb:
-                gc = work.tile([P, N], F32, bufs=3)
+                gc = work.tile([P, N], F32)
                 gc_sb[s] = gc
             dst = gc_sb[s][:, j * HALF : (j + 1) * HALF]
             if e == "S":
@@ -186,11 +183,13 @@ def tile_patch_gradient_magnitude_s1_kernel(tc, patches, d_row, d_col_words, d_c
             gc, dst = gc_sb[s][:, lo:hi], gc_sq[s][:, lo:hi]
             if e == "S":
                 nc.scalar.activation(out=dst, in_=gc, func=ACT.Square)
+            elif e == "W":
+                nc.vector.tensor_tensor(out=dst, in0=gc, in1=gc, op=ALU.mult)
             elif e == "V":
                 for j in range(2):
                     a, b = max(lo, j * HALF), min(hi, (j + 1) * HALF)
                     if a < b:
-                        nc.vector.tensor_tensor(out=gc_sq[s][:, a:b], in0=gc_bank[s, j][:, a - j * HALF : b - j * HALF], in1=gc_sb[s][:, a:b], op=ALU.mult)
+                        nc.vector.tensor_tensor(out=gc_sq[s][:, a:b], in0=gc_sb[s][:, a:b], in1=gc_bank[s, j][:, a - j * HALF : b - j * HALF], op=ALU.mult)
             else:
                 nc.gpsimd.tensor_tensor(out=dst, in0=gc, in1=gc, op=ALU.mult)
 
@@ -202,7 +201,7 @@ def tile_patch_gradient_magnitude_s1_kernel(tc, patches, d_row, d_col_words, d_c
                 dg = outs.tile([P, N], F32, tag="diag", align_bytes=64)
                 diag[s] = dg
             cols = slice(j * HALF, (j + 1) * HALF)
-            nc.vector.tensor_tensor(out=diag[s][:, cols], in0=gr_bank[s, j][:], in1=gc_sb[s][:, cols], op=ALU.add)
+            nc.vector.tensor_tensor(out=diag[s][:, cols], in0=gc_sb[s][:, cols], in1=gr_bank[s, j][:], op=ALU.add)
             if stored is not None:
                 store(out_1, diag[s], s, stored[0], stored[1])
 
@@ -217,13 +216,11 @@ def tile_patch_gradient_magnitude_s1_kernel(tc, patches, d_row, d_col_words, d_c
             cols = slice(lo * HALF, hi * HALF)
             engine.tensor_tensor(out=gr_sq[s][:, cols], in0=gr_sq[s][:, cols], in1=gc_sq[s][:, cols], op=ALU.add)
 
-        def root(s, lo, hi):
+        def root(s, lo, hi, stored=None):
             cols = slice(lo * HALF, hi * HALF)
             nc.scalar.activation(out=gr_sq[s][:, cols], in_=gr_sq[s][:, cols], func=ACT.Sqrt, bias=FLOOR_SQUARED)
-            if s == TILES - 1:
-                store(out_0, gr_sq[s], s, lo, hi)
-            elif hi == 2:
-                store(out_0, gr_sq[s], s, 0, 2)
+            if stored is not None:
+                store(out_0, gr_sq[s], s, stored[0], stored[1])
 
         def group_d(g, h, s_cols):
             if s_cols:
@@ -262,16 +259,17 @@ def tile_patch_gradient_magnitude_s1_kernel(tc, patches, d_row, d_col_words, d_c
             group_d(1, 0, S_COLS)
             turn(2)
             turn(3)
-            copy_gc(0, 0)
+            copy_gc(0, 0, "S")
             quant_d(1, 0)
             mm_gr(0, 0)
             mm_gr(0, 1)
             copy_gc(0, 1, "S")
-            copy_x(2, "V")
             square_gc(0, 0, HALF, "S")
+            copy_x(2, "V")
             copy_x(3, "S")
-            group_d(0, 1, 0)
+            inter(0, 1, 0, HALF // 2, "V")
             quant_x(2, 2)
+            inter(0, 1, HALF // 2, HALF, "V")
             mm_gc(1, 0)
             mm_gc(1, 1)
             mm_gr(1, 0)
@@ -279,6 +277,7 @@ def tile_patch_gradient_magnitude_s1_kernel(tc, patches, d_row, d_col_words, d_c
             square_gr(0, 0)
             square_gr(0, 1)
             square_gc(0, HALF, N - V_SQH, "S")
+            diagonal(0, 0)
             quant_d(0, 1)
             group_d(1, 1, S_COLS_R)
             square_gc(0, N - V_SQH, N, "V")
@@ -286,71 +285,75 @@ def tile_patch_gradient_magnitude_s1_kernel(tc, patches, d_row, d_col_words, d_c
             add_squares(0, 0, 2, "G")
             copy_gc(1, 0, "S")
             copy_gc(1, 1, "S")
-            diagonal(0, 0)
             mm_gc(2, 1)
             mm_gc(2, 0)
             diagonal(0, 1, (0, 2))
-            mm_gr(2, 0)
+            mm_gr(2, 1)
             square_gr(1, 0)
             square_gr(1, 1)
             square_gc(1, 0, N, "S")
             diagonal(1, 0)
-            mm_gr(2, 1)
+            mm_gr(2, 0)
             diagonal(1, 1, (0, 2))
             add_squares(1, 0, 2, "G")
             def x_pair(s):
-                if s >= X_FROM and (s - X_FROM) % X_EVERY == 0:
-                    m = FIRST + 2 * ((s - X_FROM) // X_EVERY)
-                    if m < TILES:
-                        return [m, m + 1]
-                return []
+                return [s + 2, s + 3] if s % 2 == 0 and s + 2 < TILES else []
 
 
-            for m in x_pair(2):
+            for m in x_pair(2)[::-1]:
                 turn(m)
-            for s in range(2, TILES):
-                nxt = s + 1 < TILES
-                last = s == TILES - 1
+            last = TILES - 1
+            for s in range(2, last - 1):
                 tiles = x_pair(s)
-                v_sq = V_SQ if tiles else V_SQ0
-                if s == LATE:
-                    v_sq = N
-                if nxt:
-                    mm_gc(s + 1, 1)
+                s_sq = S_SQ if tiles else S_SQ0
+                mm_gc(s + 1, 1)
                 copy_gc(s, 0)
-                if nxt:
-                    mm_gc(s + 1, 0)
+                mm_gc(s + 1, 0)
                 copy_gc(s, 1)
-                square_gr(s, 1)
                 square_gr(s, 0)
+                square_gr(s, 1)
                 for m in tiles:
                     copy_x(m, "S")
-                if s < LATE and not tiles:
-                    root(s - 2, 0, 2)
-                square_gc(s, v_sq, N, "S")
-                square_gc(s, 0, HALF, "V")
-                diagonal(s, 0, (0, 1) if last else None)
-                if nxt:
-                    mm_gr(s + 1, 0)
-                if s == LATE:
-                    square_gc(s, HALF, v_sq, "V")
-                if s >= LATE and not last:
+                square_gc(s, 0, s_sq, "S")
+                diagonal(s, 0)
+                mm_gr(s + 1, 1)
+                square_gc(s, HALF, N, "V")
+                if not tiles:
                     add_squares(s, 0, 2, "G")
-                diagonal(s, 1, (1, 2) if last else (0, 2))
-                if nxt:
-                    mm_gr(s + 1, 1)
-                if s < LATE:
-                    square_gc(s, HALF, v_sq, "V")
-                    if tiles:
-                        quant_x(tiles[0], 2)
+                root(s - 2, 0, 2, (0, 2))
+                diagonal(s, 1, (0, 2))
+                mm_gr(s + 1, 0)
+                if tiles:
+                    square_gc(s, s_sq, HALF, "W")
+                    quant_x(tiles[0], 2)
                     add_squares(s, 0, 2, "G")
-                if tiles or s == LATE:
-                    root(s - 2, 0, 2)
-                if s >= LATE:
-                    root(s - 1, 0, 2)
-                for m in x_pair(s + 1):
+                for m in x_pair(s + 1)[::-1]:
                     turn(m)
-            add_squares(TILES - 1, 0, 1, "V")
-            add_squares(TILES - 1, 1, 2, "V")
-            root(TILES - 1, 0, 1)
-            root(TILES - 1, 1, 2)
+            s = last - 1
+            mm_gc(last, 1)
+            copy_gc(s, 0)
+            mm_gc(last, 0)
+            copy_gc(s, 1)
+            root(s - 2, 0, 2, (0, 2))
+            square_gr(s, 0)
+            square_gr(s, 1)
+            square_gc(s, 0, N, "V")
+            add_squares(s, 0, 2, "G")
+            diagonal(s, 0)
+            mm_gr(last, 1)
+            diagonal(s, 1, (0, 2))
+            mm_gr(last, 0)
+            root(s - 1, 0, 2, (0, 2))
+            copy_gc(last, 0)
+            copy_gc(last, 1)
+            square_gr(last, 0)
+            square_gr(last, 1)
+            square_gc(last, 0, HALF, "S")
+            diagonal(last, 0, (0, 1))
+            square_gc(last, HALF, N, "V")
+            diagonal(last, 1, (1, 2))
+            root(s, 0, 2, (0, 2))
+            add_squares(last, 0, 1, "V")
+            add_squares(last, 1, 2, "V")
+            root(last, 0, 1, (0, 1))
+            root(last, 1, 2, (1, 2))

@@ -23,12 +23,13 @@ TILES = M // P
 QUAD = 4
 FLOOR_SQUARED = 0.0625
 FLOPS = 2 * 2 * M * K * N
-S_SQ = 304
+S_SQ = 288
 S_SQ0 = 512
 V_SQH = 128
 S_COLS = 192
-S_COLS_R = 192
+S_COLS_R = 160
 FIRST = 4
+V_SQ1 = 128
 
 
 def tile_patch_gradient_magnitude_s1_kernel(tc, patches, d_row, d_col_words, d_col_scales, out_0, out_1):
@@ -274,6 +275,8 @@ def tile_patch_gradient_magnitude_s1_kernel(tc, patches, d_row, d_col_words, d_c
             mm_gc(1, 1)
             mm_gr(1, 0)
             mm_gr(1, 1)
+            turn(4)
+            turn(5)
             square_gr(0, 0)
             square_gr(0, 1)
             square_gc(0, HALF, N - V_SQH, "S")
@@ -285,54 +288,60 @@ def tile_patch_gradient_magnitude_s1_kernel(tc, patches, d_row, d_col_words, d_c
             add_squares(0, 0, 2, "G")
             copy_gc(1, 0, "S")
             copy_gc(1, 1, "S")
-            mm_gc(2, 1)
             mm_gc(2, 0)
+            mm_gc(2, 1)
             diagonal(0, 1, (0, 2))
-            mm_gr(2, 1)
+            mm_gr(2, 0)
             square_gr(1, 0)
             square_gr(1, 1)
-            square_gc(1, 0, N, "S")
+            copy_x(4, "S")
+            copy_x(5, "S")
+            square_gc(1, 0, N - V_SQ1, "S")
             diagonal(1, 0)
-            mm_gr(2, 0)
+            mm_gr(2, 1)
             diagonal(1, 1, (0, 2))
+            copy_gc(2, 0)
+            copy_gc(2, 1)
+            square_gc(1, N - V_SQ1, N, "W")
+            quant_x(4, 2)
             add_squares(1, 0, 2, "G")
             def x_pair(s):
-                return [s + 2, s + 3] if s % 2 == 0 and s + 2 < TILES else []
+                return [s + 3, s + 4] if s % 2 == 1 and s + 3 < TILES else []
 
 
-            for m in x_pair(2)[::-1]:
-                turn(m)
             last = TILES - 1
             for s in range(2, last - 1):
                 tiles = x_pair(s)
                 s_sq = S_SQ if tiles else S_SQ0
-                mm_gc(s + 1, 1)
-                copy_gc(s, 0)
                 mm_gc(s + 1, 0)
-                copy_gc(s, 1)
+                if s > 2:
+                    copy_gc(s, 0)
+                if s > 2 and x_pair(s - 1):
+                    square_gc(s - 1, S_SQ, HALF, "W")
+                    quant_x(x_pair(s - 1)[0], 2)
+                    add_squares(s - 1, 0, 2, "G")
+                mm_gr(s + 1, 0)
+                if s > 2:
+                    copy_gc(s, 1)
                 square_gr(s, 0)
                 square_gr(s, 1)
                 for m in tiles:
                     copy_x(m, "S")
                 square_gc(s, 0, s_sq, "S")
                 diagonal(s, 0)
-                mm_gr(s + 1, 1)
+                mm_gc(s + 1, 1)
                 square_gc(s, HALF, N, "V")
                 if not tiles:
                     add_squares(s, 0, 2, "G")
-                root(s - 2, 0, 2, (0, 2))
                 diagonal(s, 1, (0, 2))
-                mm_gr(s + 1, 0)
-                if tiles:
-                    square_gc(s, s_sq, HALF, "W")
-                    quant_x(tiles[0], 2)
-                    add_squares(s, 0, 2, "G")
-                for m in x_pair(s + 1)[::-1]:
+                root(s - 2, 0, 2, (0, 2))
+                mm_gr(s + 1, 1)
+                for m in x_pair(s + 1):
                     turn(m)
             s = last - 1
-            mm_gc(last, 1)
-            copy_gc(s, 0)
             mm_gc(last, 0)
+            copy_gc(s, 0)
+            mm_gr(last, 0)
             copy_gc(s, 1)
             root(s - 2, 0, 2, (0, 2))
             square_gr(s, 0)
@@ -340,9 +349,9 @@ def tile_patch_gradient_magnitude_s1_kernel(tc, patches, d_row, d_col_words, d_c
             square_gc(s, 0, N, "V")
             add_squares(s, 0, 2, "G")
             diagonal(s, 0)
-            mm_gr(last, 1)
+            mm_gc(last, 1)
             diagonal(s, 1, (0, 2))
-            mm_gr(last, 0)
+            mm_gr(last, 1)
             root(s - 1, 0, 2, (0, 2))
             copy_gc(last, 0)
             copy_gc(last, 1)

@@ -23,7 +23,7 @@ TILES = M // P
 QUAD = 4
 FLOOR_SQUARED = 0.0625
 FLOPS = 2 * 2 * M * K * N
-S_SQ = 288
+S_SQ = 304
 S_SQ0 = 512
 V_SQH = 128
 S_COLS = 192
@@ -268,12 +268,14 @@ def tile_patch_gradient_magnitude_s1_kernel(tc, patches, d_row, d_col_words, d_c
             square_gc(0, 0, HALF, "S")
             copy_x(2, "V")
             copy_x(3, "S")
-            inter(0, 1, 0, HALF // 2, "V")
-            quant_x(2, 2)
-            inter(0, 1, HALF // 2, HALF, "V")
+            inter(0, 1, 0, P, "V")
+            quant_x(2, 1)
+            inter(0, 1, P, 2 * P, "V")
+            quant_x(3, 1)
+            inter(0, 1, 2 * P, HALF, "V")
             mm_gc(1, 0)
-            mm_gc(1, 1)
             mm_gr(1, 0)
+            mm_gc(1, 1)
             mm_gr(1, 1)
             turn(4)
             turn(5)

@@ -24,7 +24,6 @@ QUAD = 4
 FLOOR_SQUARED = 0.0625
 FLOPS = 2 * 2 * M * K * N
 S_SQ = 304
-S_SQ0 = 512
 V_SQH = 128
 S_COLS = 192
 S_COLS_R = 160
@@ -250,12 +249,14 @@ def tile_patch_gradient_magnitude_s1_kernel(tc, patches, d_row, d_col_words, d_c
             turn(0)
             turn(1)
             copy_x(0, "V")
-            group_d(0, 0, S_COLS)
-            copy_x(1, "S")
+            inter(0, 0, 0, S_COLS, "S")
+            inter(0, 0, S_COLS, S_COLS + P, "V")
             quant_x(0, 1)
+            inter(0, 0, S_COLS + P, HALF, "V")
+            copy_x(1, "S")
             mm_gc(0, 0)
-            quant_d(0, 0)
             quant_x(1, 1)
+            quant_d(0, 0)
             mm_gc(0, 1)
             group_d(1, 0, S_COLS)
             turn(2)
@@ -314,11 +315,11 @@ def tile_patch_gradient_magnitude_s1_kernel(tc, patches, d_row, d_col_words, d_c
             last = TILES - 1
             for s in range(2, last - 1):
                 tiles = x_pair(s)
-                s_sq = S_SQ if tiles else S_SQ0
+                s_sq = S_SQ if tiles else HALF
                 mm_gc(s + 1, 0)
                 if s > 2:
                     copy_gc(s, 0)
-                if s > 2 and x_pair(s - 1):
+                if s > 2 and x_pair(s - 1) and x_pair(s + 1):
                     square_gc(s - 1, S_SQ, HALF, "W")
                     quant_x(x_pair(s - 1)[0], 2)
                     add_squares(s - 1, 0, 2, "G")
@@ -336,6 +337,10 @@ def tile_patch_gradient_magnitude_s1_kernel(tc, patches, d_row, d_col_words, d_c
                 if not tiles:
                     add_squares(s, 0, 2, "G")
                 diagonal(s, 1, (0, 2))
+                if tiles and not x_pair(s + 2):
+                    square_gc(s, S_SQ, HALF, "W")
+                    quant_x(tiles[0], 2)
+                    add_squares(s, 0, 2, "G")
                 root(s - 2, 0, 2, (0, 2))
                 mm_gr(s + 1, 1)
                 for m in x_pair(s + 1):

@@ -49,7 +49,9 @@ def tile_patch_gradient_magnitude_s1_kernel(tc, patches, d_row, d_col_words, d_c
         dr_codes = keep.tile([P, PASSES, N], U32, align_bytes=64)
         dr_scales = keep.tile([P, PASSES, N], U8, align_bytes=64)
         dc_words = keep.tile([P, 2, PASSES, 2 * HALF], U8, align_bytes=64)
-        dc_scales = keep.tile([P, PASSES, N], U8, align_bytes=64)
+        left_scales = keep.tile([P, PASSES, HALF], U8, align_bytes=64)
+        right_scales = keep.tile([P, PASSES, HALF], U8, align_bytes=64)
+        dc_scales = [left_scales, right_scales]
 
         x_turned, x_grouped, dr_raw, dr_grouped = {}, {}, {}, {}
         gc_bank, gr_bank, gc_sb, gc_sq, gr_sq, diag = {}, {}, {}, {}, {}, {}
@@ -71,11 +73,11 @@ def tile_patch_gradient_magnitude_s1_kernel(tc, patches, d_row, d_col_words, d_c
             half = slice(2 * h * HALF, 2 * (h + 1) * HALF)
             nc.sync.dma_start(out=dc_words[:, h, :, :].bitcast(I32), in_=d_col_words[:, :, half].rearrange("g p w -> p g w").bitcast(I32))
 
-        def load_scales():
+        def load_scales(h):
             for q in range(4):
                 nc.sync.dma_start(
-                    out=dc_scales[32 * q : 32 * q + 4, :, :].bitcast(I32),
-                    in_=d_col_scales[:, 4 * q : 4 * q + 4, :].rearrange("g r n -> r g n").bitcast(I32),
+                    out=dc_scales[h][32 * q : 32 * q + 4, :, :].bitcast(I32),
+                    in_=d_col_scales[:, 4 * q : 4 * q + 4, h * HALF : (h + 1) * HALF].rearrange("g r n -> r g n").bitcast(I32),
                 )
 
         def turn(m):
@@ -154,9 +156,8 @@ def tile_patch_gradient_magnitude_s1_kernel(tc, patches, d_row, d_col_words, d_c
 
         def mm_gc(s, j):
             m, h = unit(s, j)
-            cols = slice(h * HALF, (h + 1) * HALF)
             words = [dc_words[:, h, g, :].bitcast(FP4X4) for g in range(PASSES)]
-            gc_bank[s, j] = product(m, words, [dc_scales[:, g, cols] for g in range(PASSES)])
+            gc_bank[s, j] = product(m, words, [dc_scales[h][:, g, :] for g in range(PASSES)])
 
         def mm_gr(s, j):
             m, h = unit(s, j)
@@ -227,19 +228,21 @@ def tile_patch_gradient_magnitude_s1_kernel(tc, patches, d_row, d_col_words, d_c
                 inter(g, h, 0, s_cols, "S")
             inter(g, h, s_cols, HALF, "V")
 
-        nc.vector.memset(dc_scales[:].rearrange("p g n -> p (g n)").bitcast(I32), 0)
+        for plane in dc_scales:
+            nc.vector.memset(plane[:].rearrange("p g n -> p (g n)").bitcast(I32), 0)
         nc.gpsimd.memset(one[:], 1.0)
         make_identity(nc, ident[:])
 
         with tc.manual_schedule():
             load_x(0, 2)
             load_d_row(0, 0)
-            load_scales()
+            load_scales(0)
             load_words(0)
             load_d_row(1, 0)
             load_x(2, 2)
             load_d_row(0, 1)
             load_d_row(1, 1)
+            load_scales(1)
             load_words(1)
             load_x(4, 2)
             load_x(6, 2)

@@ -316,7 +316,7 @@ def tile_patch_gradient_magnitude_s1_kernel(tc, patches, d_row, d_col_words, d_c
 
 
             last = TILES - 1
-            for s in range(2, last - 1):
+            for s in range(2, 11):
                 tiles = x_pair(s)
                 s_sq = S_SQ if tiles else HALF
                 mm_gc(s + 1, 0)
@@ -348,31 +348,52 @@ def tile_patch_gradient_magnitude_s1_kernel(tc, patches, d_row, d_col_words, d_c
                 mm_gr(s + 1, 1)
                 for m in x_pair(s + 1):
                     turn(m)
-            s = last - 1
-            mm_gc(last, 0)
+            s = 11
+            mm_gc(s + 1, 0)
             copy_gc(s, 0)
-            mm_gr(last, 0)
+            mm_gr(s + 1, 0)
             copy_gc(s, 1)
-            root(s - 2, 0, 2, (0, 2))
             square_gr(s, 0)
             square_gr(s, 1)
-            square_gc(s, 0, N, "V")
-            add_squares(s, 0, 2, "G")
+            copy_x(14, "S")
+            copy_x(15, "V")
+            square_gc(s, 0, S_SQ, "S")
+            square_gc(s, HALF, N, "V")
             diagonal(s, 0)
-            mm_gc(last, 1)
+            square_gc(s, S_SQ, HALF, "W")
+            quant_x(14, 2)
+            add_squares(s, 0, 2, "G")
+            mm_gc(s + 1, 1)
+            root(s - 2, 0, 2, (0, 2))
             diagonal(s, 1, (0, 2))
-            mm_gr(last, 1)
             root(s - 1, 0, 2, (0, 2))
+            mm_gr(s + 1, 1)
+            for s in (12, 13, 14):
+                mm_gc(s + 1, 0)
+                copy_gc(s, 0)
+                mm_gr(s + 1, 0)
+                copy_gc(s, 1)
+                square_gr(s, 0)
+                square_gr(s, 1)
+                square_gc(s, 0, HALF, "V")
+                square_gc(s, HALF, N, "S")
+                add_squares(s, 0, 2, "G")
+                mm_gc(s + 1, 1)
+                diagonal(s, 0, (0, 1) if s == 14 else None)
+                diagonal(s, 1, (1, 2) if s == 14 else (0, 2))
+                root(s - 1, 0, 2, (0, 2))
+                mm_gr(s + 1, 1)
             copy_gc(last, 0)
             copy_gc(last, 1)
             square_gr(last, 0)
             square_gr(last, 1)
-            square_gc(last, 0, HALF, "S")
+            square_gc(last, 0, HALF, "V")
+            square_gc(last, HALF, N, "S")
             diagonal(last, 0, (0, 1))
-            square_gc(last, HALF, N, "V")
             diagonal(last, 1, (1, 2))
-            root(s, 0, 2, (0, 2))
+            root(last - 1, 0, 1, (0, 1))
             add_squares(last, 0, 1, "V")
+            root(last - 1, 1, 2, (1, 2))
             add_squares(last, 1, 2, "V")
             root(last, 0, 1, (0, 1))
             root(last, 1, 2, (1, 2))

@@ -26,7 +26,7 @@ FLOPS = 2 * 2 * M * K * N
 S_SQ = 304
 V_SQH = 128
 S_COLS = 192
-S_COLS_R = 160
+S_COLS_R = 128
 FIRST = 4
 V_SQ1 = 128
 
@@ -379,21 +379,21 @@ def tile_patch_gradient_magnitude_s1_kernel(tc, patches, d_row, d_col_words, d_c
                 square_gc(s, HALF, N, "S")
                 add_squares(s, 0, 2, "G")
                 mm_gc(s + 1, 1)
-                diagonal(s, 0, (0, 1) if s == 14 else None)
-                diagonal(s, 1, (1, 2) if s == 14 else (0, 2))
+                diagonal(s, 0, (0, 1) if s >= 13 else None)
+                diagonal(s, 1, (1, 2) if s >= 13 else (0, 2))
                 root(s - 1, 0, 2, (0, 2))
                 mm_gr(s + 1, 1)
             copy_gc(last, 0)
             copy_gc(last, 1)
-            square_gr(last, 0)
             square_gr(last, 1)
-            square_gc(last, 0, HALF, "V")
             square_gc(last, HALF, N, "S")
             diagonal(last, 0, (0, 1))
+            square_gr(last, 0)
             diagonal(last, 1, (1, 2))
+            square_gc(last, 0, HALF, "V")
             root(last - 1, 0, 1, (0, 1))
-            add_squares(last, 0, 1, "V")
-            root(last - 1, 1, 2, (1, 2))
             add_squares(last, 1, 2, "V")
-            root(last, 0, 1, (0, 1))
+            root(last - 1, 1, 2, (1, 2))
+            add_squares(last, 0, 1, "V")
             root(last, 1, 2, (1, 2))
+            root(last, 0, 1, (0, 1))

@@ -23,7 +23,7 @@ TILES = M // P
 QUAD = 4
 FLOOR_SQUARED = 0.0625
 FLOPS = 2 * 2 * M * K * N
-S_SQ = 304
+S_SQ = 368
 V_SQH = 128
 S_COLS = 192
 S_COLS_R = 128

@@ -23,12 +23,14 @@ TILES = M // P
 QUAD = 4
 FLOOR_SQUARED = 0.0625
 FLOPS = 2 * 2 * M * K * N
-S_SQ = 368
+S_SQ = 432
 V_SQH = 128
 S_COLS = 192
 S_COLS_R = 128
 FIRST = 4
 V_SQ1 = 128
+GATE = 128
+S_ROWS = 72
 
 
 def tile_patch_gradient_magnitude_s1_kernel(tc, patches, d_row, d_col_words, d_col_scales, out_0, out_1):
@@ -88,12 +90,12 @@ def tile_patch_gradient_magnitude_s1_kernel(tc, patches, d_row, d_col_words, d_c
                     nc.tensor.transpose(bank[:, g, u, :], words[:, 256 * g + u : 256 * (g + 1) : 2], ident[:])
             x_turned[m] = bank
 
-        def copy_x(m, e):
+        def copy_x(m, e, lo=0, hi=PASSES, rows=slice(0, P)):
             if m // 2 not in x_grouped:
                 grouped = stage.tile([P, 2, PASSES, P, PACK], BF16, align_bytes=64)
                 x_grouped[m // 2] = grouped
-            dst = x_grouped[m // 2][:, m % 2, :, :, :].bitcast(F32)
-            src = x_turned[m][:].rearrange("p g u r -> p g r u")
+            dst = x_grouped[m // 2][:, m % 2, lo:hi, rows, :].bitcast(F32)
+            src = x_turned[m][:, lo:hi, :, rows].rearrange("p g u r -> p g r u")
             if e == "S":
                 nc.scalar.copy(out=dst, in_=src)
             else:
@@ -318,32 +320,34 @@ def tile_patch_gradient_magnitude_s1_kernel(tc, patches, d_row, d_col_words, d_c
             last = TILES - 1
             for s in range(2, 11):
                 tiles = x_pair(s)
-                s_sq = S_SQ if tiles else HALF
                 mm_gc(s + 1, 0)
                 if s > 2:
-                    copy_gc(s, 0)
-                if s > 2 and x_pair(s - 1) and x_pair(s + 1):
-                    square_gc(s - 1, S_SQ, HALF, "W")
-                    quant_x(x_pair(s - 1)[0], 2)
-                    add_squares(s - 1, 0, 2, "G")
-                mm_gr(s + 1, 0)
-                if s > 2:
                     copy_gc(s, 1)
+                    copy_gc(s, 0, "S")
+                if s > 2 and not tiles:
+                    square_gc(s - 1, N - GATE, N, "W")
+                    quant_x(s + 2, 2)
+                    add_squares(s - 1, 0, 2, "G")
+                mm_gc(s + 1, 1)
                 square_gr(s, 0)
                 square_gr(s, 1)
-                for m in tiles:
-                    copy_x(m, "S")
-                square_gc(s, 0, s_sq, "S")
-                diagonal(s, 0)
-                mm_gc(s + 1, 1)
-                square_gc(s, HALF, N, "V")
+                if s == 2:
+                    square_gc(s, 0, HALF, "S")
+                    diagonal(s, 0)
+                else:
+                    square_gc(s, 0, HALF, "V")
+                square_gc(s, HALF, N - GATE if tiles else N, "V")
                 if not tiles:
                     add_squares(s, 0, 2, "G")
+                mm_gr(s + 1, 0)
+                if tiles:
+                    copy_x(tiles[0], "S")
+                    copy_x(tiles[1], "S", 0, PASSES, slice(0, S_ROWS))
+                if s > 2:
+                    diagonal(s, 0)
                 diagonal(s, 1, (0, 2))
-                if tiles and not x_pair(s + 2):
-                    square_gc(s, S_SQ, HALF, "W")
-                    quant_x(tiles[0], 2)
-                    add_squares(s, 0, 2, "G")
+                if tiles:
+                    copy_x(tiles[1], "V", 0, PASSES, slice(S_ROWS, P))
                 root(s - 2, 0, 2, (0, 2))
                 mm_gr(s + 1, 1)
                 for m in x_pair(s + 1):

@@ -23,14 +23,21 @@ TILES = M // P
 QUAD = 4
 FLOOR_SQUARED = 0.0625
 FLOPS = 2 * 2 * M * K * N
-S_SQ = 432
+S_SQ = 304
 V_SQH = 128
 S_COLS = 192
 S_COLS_R = 128
 FIRST = 4
 V_SQ1 = 128
 GATE = 128
-S_ROWS = 72
+S_ROWS = 88
+CATCH_ROWS = 0
+LATE = {4: 2, 6: 1}
+CATCH = 11
+HALVES_FROM = 13
+EARLY_FROM = 12
+ROOT_FIRST = 99
+AHEAD_FROM = 11
 
 
 def tile_patch_gradient_magnitude_s1_kernel(tc, patches, d_row, d_col_words, d_col_scales, out_0, out_1):
@@ -109,15 +116,19 @@ def tile_patch_gradient_magnitude_s1_kernel(tc, patches, d_row, d_col_words, d_c
             )
 
         def inter(g, h, lo, hi, e):
-            if (g, h) not in dr_grouped:
+            if (g, h) == (1, 1):
+                dr_grouped[g, h] = dr_raw[0, 1][:].rearrange("p t n -> p (t n)").rearrange("p (n t) -> p n t", t=PACK)
+            elif (g, h) not in dr_grouped:
                 grouped = outs.tile([P, HALF, PACK], BF16, tag="diag", align_bytes=64)
                 dr_grouped[g, h] = grouped
+            if e == "G":
+                rows = dr_raw[g, h][:, :, lo:hi].rearrange("p t n -> p n t")
+                nc.gpsimd.tensor_scalar(out=dr_grouped[g, h][:, lo:hi, :], in0=rows, scalar1=1.0, scalar2=0.0, op0=ALU.mult, op1=ALU.add)
+                return
             dst = dr_grouped[g, h][:, lo:hi, :].rearrange("p (c i) t -> p c t i", i=4)
             src = dr_raw[g, h][:, :, lo:hi].rearrange("p t (c i) -> p c t i", i=4)
             if e == "S":
                 nc.scalar.copy(out=dst, in_=src)
-            elif e == "G":
-                nc.gpsimd.tensor_scalar(out=dst, in0=src, scalar1=1.0, scalar2=0.0, op0=ALU.mult, op1=ALU.add)
             else:
                 nc.vector.tensor_copy(out=dst, in_=src)
 
@@ -283,121 +294,117 @@ def tile_patch_gradient_magnitude_s1_kernel(tc, patches, d_row, d_col_words, d_c
             mm_gr(1, 0)
             mm_gc(1, 1)
             mm_gr(1, 1)
-            turn(4)
-            turn(5)
             square_gr(0, 0)
             square_gr(0, 1)
             square_gc(0, HALF, N - V_SQH, "S")
+            inter(1, 1, S_COLS_R, HALF, "G")
+            inter(1, 1, 0, S_COLS_R, "S")
             diagonal(0, 0)
-            quant_d(0, 1)
-            group_d(1, 1, S_COLS_R)
-            square_gc(0, N - V_SQH, N, "V")
-            quant_d(1, 1)
-            add_squares(0, 0, 2, "G")
-            copy_gc(1, 0, "S")
-            copy_gc(1, 1, "S")
+            copy_gc(1, 0)
             mm_gc(2, 0)
             mm_gc(2, 1)
-            diagonal(0, 1, (0, 2))
-            mm_gr(2, 0)
+            copy_gc(1, 1)
+            square_gc(1, 0, HALF, "V")
+            turn(4)
+            turn(5)
             square_gr(1, 0)
             square_gr(1, 1)
-            copy_x(4, "S")
-            copy_x(5, "S")
-            square_gc(1, 0, N - V_SQ1, "S")
+            diagonal(0, 1, (0, 2))
+            quant_d(0, 1)
+            square_gc(0, N - V_SQH, N, "W")
+            quant_d(1, 1)
+            add_squares(0, 0, 2, "G")
+            square_gc(1, HALF, N - V_SQ1, "S")
+            copy_gc(2, 0, "S")
+            copy_gc(2, 1, "S")
+            mm_gr(2, 0)
             diagonal(1, 0)
             mm_gr(2, 1)
+            copy_x(4, "S")
+            copy_x(5, "S")
             diagonal(1, 1, (0, 2))
-            copy_gc(2, 0)
-            copy_gc(2, 1)
+            square_gc(2, 0, HALF, "V")
+            square_gc(2, HALF, N, "V")
+            mm_gc(3, 0)
+            mm_gc(3, 1)
+            square_gr(2, 0)
+            square_gr(2, 1)
+            mm_gr(3, 0)
+            diagonal(2, 0)
+            copy_gc(3, 0, "S")
             square_gc(1, N - V_SQ1, N, "W")
             quant_x(4, 2)
             add_squares(1, 0, 2, "G")
+            add_squares(2, 0, 2, "G")
+            diagonal(2, 1, (0, 2))
+            root(0, 0, 2, (0, 2))
+            mm_gr(3, 1)
+            turn(6)
+            turn(7)
             def x_pair(s):
                 return [s + 3, s + 4] if s % 2 == 1 and s + 3 < TILES else []
 
 
             last = TILES - 1
-            for s in range(2, 11):
+            def release(s, pair):
+                square_gc(s, N - GATE, N, "W")
+                quant_x(pair, 2)
+                add_squares(s, 0, 2, "G")
+            for s in range(3, last):
                 tiles = x_pair(s)
+                halves = s >= EARLY_FROM
+                place = LATE.get(s, 0) if s < CATCH and not tiles else None
                 mm_gc(s + 1, 0)
-                if s > 2:
-                    copy_gc(s, 1)
-                    copy_gc(s, 0, "S")
-                if s > 2 and not tiles:
-                    square_gc(s - 1, N - GATE, N, "W")
-                    quant_x(s + 2, 2)
-                    add_squares(s - 1, 0, 2, "G")
+                copy_gc(s, 1)
+                if place == 0:
+                    release(s - 1, s + 2)
                 mm_gc(s + 1, 1)
-                square_gr(s, 0)
-                square_gr(s, 1)
-                if s == 2:
-                    square_gc(s, 0, HALF, "S")
-                    diagonal(s, 0)
-                else:
-                    square_gc(s, 0, HALF, "V")
+                early = s >= EARLY_FROM
+                for j in (1, 0) if early else (0, 1):
+                    square_gr(s, j)
+                square_gc(s, 0, HALF, "V")
+                if place == 1:
+                    release(s - 1, s + 2)
                 square_gc(s, HALF, N - GATE if tiles else N, "V")
+                if place == 2:
+                    release(s - 1, s + 2)
                 if not tiles:
                     add_squares(s, 0, 2, "G")
                 mm_gr(s + 1, 0)
+                rows = S_ROWS if s < CATCH else CATCH_ROWS
                 if tiles:
                     copy_x(tiles[0], "S")
-                    copy_x(tiles[1], "S", 0, PASSES, slice(0, S_ROWS))
-                if s > 2:
+                    if rows:
+                        copy_x(tiles[1], "S", 0, PASSES, slice(0, rows))
+                if s == CATCH:
+                    copy_x(tiles[1], "V", 0, PASSES, slice(rows, P))
+                if not early:
                     diagonal(s, 0)
-                diagonal(s, 1, (0, 2))
-                if tiles:
-                    copy_x(tiles[1], "V", 0, PASSES, slice(S_ROWS, P))
-                root(s - 2, 0, 2, (0, 2))
+                if s == CATCH:
+                    release(s, s + 3)
+                    root(s - 2, 0, 2, (0, 2))
+                diagonal(s, 1, (1, 2) if halves else (0, 2))
+                if tiles and s < CATCH:
+                    copy_x(tiles[1], "V", 0, PASSES, slice(rows, P))
+                copy_gc(s + 1, 0, "S")
+                if s + 1 >= EARLY_FROM and s >= AHEAD_FROM:
+                    diagonal(s + 1, 0, (0, 1))
+                root(s - 2 if s < CATCH else s - 1, 0, 2, (0, 2))
+                if s + 1 >= EARLY_FROM and s < AHEAD_FROM:
+                    diagonal(s + 1, 0, (0, 1))
                 mm_gr(s + 1, 1)
                 for m in x_pair(s + 1):
                     turn(m)
-            s = 11
-            mm_gc(s + 1, 0)
-            copy_gc(s, 0)
-            mm_gr(s + 1, 0)
-            copy_gc(s, 1)
-            square_gr(s, 0)
-            square_gr(s, 1)
-            copy_x(14, "S")
-            copy_x(15, "V")
-            square_gc(s, 0, S_SQ, "S")
-            square_gc(s, HALF, N, "V")
-            diagonal(s, 0)
-            square_gc(s, S_SQ, HALF, "W")
-            quant_x(14, 2)
-            add_squares(s, 0, 2, "G")
-            mm_gc(s + 1, 1)
-            root(s - 2, 0, 2, (0, 2))
-            diagonal(s, 1, (0, 2))
-            root(s - 1, 0, 2, (0, 2))
-            mm_gr(s + 1, 1)
-            for s in (12, 13, 14):
-                mm_gc(s + 1, 0)
-                copy_gc(s, 0)
-                mm_gr(s + 1, 0)
-                copy_gc(s, 1)
-                square_gr(s, 0)
-                square_gr(s, 1)
-                square_gc(s, 0, HALF, "V")
-                square_gc(s, HALF, N, "S")
-                add_squares(s, 0, 2, "G")
-                mm_gc(s + 1, 1)
-                diagonal(s, 0, (0, 1) if s >= 13 else None)
-                diagonal(s, 1, (1, 2) if s >= 13 else (0, 2))
-                root(s - 1, 0, 2, (0, 2))
-                mm_gr(s + 1, 1)
-            copy_gc(last, 0)
-            copy_gc(last, 1)
             square_gr(last, 1)
-            square_gc(last, HALF, N, "S")
-            diagonal(last, 0, (0, 1))
+            copy_gc(last, 1)
             square_gr(last, 0)
-            diagonal(last, 1, (1, 2))
             square_gc(last, 0, HALF, "V")
+            diagonal(last, 1, (1, 2))
+            square_gc(last, HALF, N - 256, "S")
+            square_gc(last, N - 256, N, "V")
             root(last - 1, 0, 1, (0, 1))
-            add_squares(last, 1, 2, "V")
-            root(last - 1, 1, 2, (1, 2))
             add_squares(last, 0, 1, "V")
-            root(last, 1, 2, (1, 2))
+            root(last - 1, 1, 2, (1, 2))
+            add_squares(last, 1, 2, "V")
             root(last, 0, 1, (0, 1))
+            root(last, 1, 2, (1, 2))

@@ -29,7 +29,7 @@ S_COLS = 192
 S_COLS_R = 128
 FIRST = 4
 V_SQ1 = 128
-GATE = 128
+GATE = 64
 S_ROWS = 88
 CATCH_ROWS = 0
 LATE = {4: 2, 6: 1}
@@ -38,6 +38,8 @@ HALVES_FROM = 13
 EARLY_FROM = 12
 ROOT_FIRST = 99
 AHEAD_FROM = 11
+SPLIT_FROM = 13
+V_END = 320
 
 
 def tile_patch_gradient_magnitude_s1_kernel(tc, patches, d_row, d_col_words, d_col_scales, out_0, out_1):
@@ -282,8 +284,8 @@ def tile_patch_gradient_magnitude_s1_kernel(tc, patches, d_row, d_col_words, d_c
             mm_gr(0, 0)
             mm_gr(0, 1)
             copy_gc(0, 1, "S")
-            square_gc(0, 0, HALF, "S")
-            copy_x(2, "V")
+            square_gc(0, 0, HALF, "V")
+            copy_x(2, "S")
             copy_x(3, "S")
             inter(0, 1, 0, P, "V")
             quant_x(2, 1)
@@ -296,32 +298,32 @@ def tile_patch_gradient_magnitude_s1_kernel(tc, patches, d_row, d_col_words, d_c
             mm_gr(1, 1)
             square_gr(0, 0)
             square_gr(0, 1)
-            square_gc(0, HALF, N - V_SQH, "S")
+            copy_gc(1, 0, "S")
             inter(1, 1, S_COLS_R, HALF, "G")
             inter(1, 1, 0, S_COLS_R, "S")
             diagonal(0, 0)
-            copy_gc(1, 0)
+            diagonal(0, 1, (0, 2))
             mm_gc(2, 0)
-            mm_gc(2, 1)
-            copy_gc(1, 1)
             square_gc(1, 0, HALF, "V")
+            copy_gc(1, 1)
+            square_gc(0, HALF, N - V_SQH, "V")
             turn(4)
             turn(5)
+            mm_gc(2, 1)
             square_gr(1, 0)
             square_gr(1, 1)
-            diagonal(0, 1, (0, 2))
             quant_d(0, 1)
             square_gc(0, N - V_SQH, N, "W")
             quant_d(1, 1)
             add_squares(0, 0, 2, "G")
             square_gc(1, HALF, N - V_SQ1, "S")
             copy_gc(2, 0, "S")
+            copy_x(4, "S")
+            copy_x(5, "S")
             copy_gc(2, 1, "S")
             mm_gr(2, 0)
             diagonal(1, 0)
             mm_gr(2, 1)
-            copy_x(4, "S")
-            copy_x(5, "S")
             diagonal(1, 1, (0, 2))
             square_gc(2, 0, HALF, "V")
             square_gc(2, HALF, N, "V")
@@ -368,7 +370,10 @@ def tile_patch_gradient_magnitude_s1_kernel(tc, patches, d_row, d_col_words, d_c
                 square_gc(s, HALF, N - GATE if tiles else N, "V")
                 if place == 2:
                     release(s - 1, s + 2)
-                if not tiles:
+                if s >= SPLIT_FROM:
+                    add_squares(s, 0, 1, "G")
+                    add_squares(s, 1, 2, "G")
+                elif not tiles:
                     add_squares(s, 0, 2, "G")
                 mm_gr(s + 1, 0)
                 rows = S_ROWS if s < CATCH else CATCH_ROWS
@@ -379,30 +384,36 @@ def tile_patch_gradient_magnitude_s1_kernel(tc, patches, d_row, d_col_words, d_c
                 if s == CATCH:
                     copy_x(tiles[1], "V", 0, PASSES, slice(rows, P))
                 if not early:
-                    diagonal(s, 0)
+                    diagonal(s, 0, (0, 1) if s == CATCH else None)
                 if s == CATCH:
                     release(s, s + 3)
                     root(s - 2, 0, 2, (0, 2))
-                diagonal(s, 1, (1, 2) if halves else (0, 2))
+                if s > SPLIT_FROM:
+                    root(s - 1, 0, 1, (0, 1))
+                diagonal(s, 1, (1, 2) if s >= CATCH else (0, 2))
                 if tiles and s < CATCH:
                     copy_x(tiles[1], "V", 0, PASSES, slice(rows, P))
                 copy_gc(s + 1, 0, "S")
-                if s + 1 >= EARLY_FROM and s >= AHEAD_FROM:
+                if s + 1 == last:
+                    copy_gc(last, 1)
+                if s + 1 >= EARLY_FROM and s <= SPLIT_FROM:
                     diagonal(s + 1, 0, (0, 1))
-                root(s - 2 if s < CATCH else s - 1, 0, 2, (0, 2))
-                if s + 1 >= EARLY_FROM and s < AHEAD_FROM:
+                if s > SPLIT_FROM:
+                    root(s - 1, 1, 2, (1, 2))
+                else:
+                    root(s - 2 if s < CATCH else s - 1, 0, 2, (0, 2))
+                if s > SPLIT_FROM:
                     diagonal(s + 1, 0, (0, 1))
                 mm_gr(s + 1, 1)
                 for m in x_pair(s + 1):
                     turn(m)
             square_gr(last, 1)
-            copy_gc(last, 1)
             square_gr(last, 0)
             square_gc(last, 0, HALF, "V")
             diagonal(last, 1, (1, 2))
-            square_gc(last, HALF, N - 256, "S")
-            square_gc(last, N - 256, N, "V")
             root(last - 1, 0, 1, (0, 1))
+            square_gc(last, HALF, N - V_END, "S")
+            square_gc(last, N - V_END, N, "V")
             add_squares(last, 0, 1, "V")
             root(last - 1, 1, 2, (1, 2))
             add_squares(last, 1, 2, "V")

@@ -23,23 +23,21 @@ TILES = M // P
 QUAD = 4
 FLOOR_SQUARED = 0.0625
 FLOPS = 2 * 2 * M * K * N
-S_SQ = 304
-V_SQH = 128
-S_COLS = 192
-S_COLS_R = 128
-FIRST = 4
-V_SQ1 = 128
-GATE = 64
-S_ROWS = 88
-CATCH_ROWS = 0
-LATE = {4: 2, 6: 1}
-CATCH = 11
-HALVES_FROM = 13
-EARLY_FROM = 12
-ROOT_FIRST = 99
-AHEAD_FROM = 11
-SPLIT_FROM = 13
-V_END = 320
+
+LEFT, RIGHT = 0, 1
+SCALAR, VECTOR, GPSIMD = "scalar", "vector", "gpsimd"
+BOTH, FIRST_UNIT, SECOND_UNIT = (0, 2), (0, 1), (1, 2)
+
+SPLIT_TILES = 4
+LAST = TILES - 1
+LAST_X_STEP = TILES - 5
+FIRST_WINDOW = 4
+
+SCALAR_COLUMNS_LEFT = 192
+SCALAR_COLUMNS_LAST = 128
+SCALAR_ROWS = 88
+VECTOR_COLUMNS_END = 320
+GATE = 128
 
 
 def tile_patch_gradient_magnitude_s1_kernel(tc, patches, d_row, d_col_words, d_col_scales, out_0, out_1):
@@ -65,7 +63,7 @@ def tile_patch_gradient_magnitude_s1_kernel(tc, patches, d_row, d_col_words, d_c
         dc_scales = [left_scales, right_scales]
 
         x_turned, x_grouped, dr_raw, dr_grouped = {}, {}, {}, {}
-        gc_bank, gr_bank, gc_sb, gc_sq, gr_sq, diag = {}, {}, {}, {}, {}, {}
+        gc_bank, gr_bank, gc_sb, gc_sq, magnitude, diag = {}, {}, {}, {}, {}, {}
 
         def quad_rows(tensor, m):
             first = m // QUAD * QUAD * P
@@ -78,7 +76,7 @@ def tile_patch_gradient_magnitude_s1_kernel(tc, patches, d_row, d_col_words, d_c
             rows = d_row[g * K_PASS : (g + 1) * K_PASS, h * HALF : (h + 1) * HALF]
             raw = outs.tile([P, PACK, HALF], BF16, tag="diag", align_bytes=64)
             dr_raw[g, h] = raw
-            nc.sync.dma_start(out=raw[:], in_=rows.rearrange("(p j) w -> p j w", j=PACK))
+            nc.sync.dma_start(out=raw[:], in_=rows.rearrange("(p t) n -> p t n", t=PACK))
 
         def load_words(h):
             half = slice(2 * h * HALF, 2 * (h + 1) * HALF)
@@ -91,24 +89,26 @@ def tile_patch_gradient_magnitude_s1_kernel(tc, patches, d_row, d_col_words, d_c
                     in_=d_col_scales[:, 4 * q : 4 * q + 4, h * HALF : (h + 1) * HALF].rearrange("g r n -> r g n").bitcast(I32),
                 )
 
+        def move(engine, dst, src):
+            if engine == SCALAR:
+                nc.scalar.copy(out=dst, in_=src)
+            else:
+                nc.vector.tensor_copy(out=dst, in_=src)
+
         def turn(m):
             bank = psum.tile([P, PASSES, 2, P], F32, tag="bank")
             words = x_raw[:, m, :].bitcast(F32)
             for g in range(PASSES):
                 for u in range(2):
-                    nc.tensor.transpose(bank[:, g, u, :], words[:, 256 * g + u : 256 * (g + 1) : 2], ident[:])
+                    nc.tensor.transpose(bank[:, g, u, :], words[:, 2 * P * g + u : 2 * P * (g + 1) : 2], ident[:])
             x_turned[m] = bank
 
-        def copy_x(m, e, lo=0, hi=PASSES, rows=slice(0, P)):
+        def copy_x(m, engine, lo=0, hi=P):
             if m // 2 not in x_grouped:
                 grouped = stage.tile([P, 2, PASSES, P, PACK], BF16, align_bytes=64)
                 x_grouped[m // 2] = grouped
-            dst = x_grouped[m // 2][:, m % 2, lo:hi, rows, :].bitcast(F32)
-            src = x_turned[m][:, lo:hi, :, rows].rearrange("p g u r -> p g r u")
-            if e == "S":
-                nc.scalar.copy(out=dst, in_=src)
-            else:
-                nc.vector.tensor_copy(out=dst, in_=src)
+            dst = x_grouped[m // 2][:, m % 2, :, lo:hi, :].bitcast(F32)
+            move(engine, dst, x_turned[m][:, :, :, lo:hi].rearrange("p g u r -> p g r u"))
 
         def quant_x(m, count):
             nc.vector.quantize_mx(
@@ -117,22 +117,15 @@ def tile_patch_gradient_magnitude_s1_kernel(tc, patches, d_row, d_col_words, d_c
                 in_=x_grouped[m // 2][:, m % 2 : m % 2 + count, :, :, :].rearrange("p a g r t -> p (a g r t)"),
             )
 
-        def inter(g, h, lo, hi, e):
-            if (g, h) == (1, 1):
-                dr_grouped[g, h] = dr_raw[0, 1][:].rearrange("p t n -> p (t n)").rearrange("p (n t) -> p n t", t=PACK)
-            elif (g, h) not in dr_grouped:
+        def regroup(g, h, lo, hi, engine):
+            if (g, h) not in dr_grouped:
                 grouped = outs.tile([P, HALF, PACK], BF16, tag="diag", align_bytes=64)
                 dr_grouped[g, h] = grouped
-            if e == "G":
-                rows = dr_raw[g, h][:, :, lo:hi].rearrange("p t n -> p n t")
-                nc.gpsimd.tensor_scalar(out=dr_grouped[g, h][:, lo:hi, :], in0=rows, scalar1=1.0, scalar2=0.0, op0=ALU.mult, op1=ALU.add)
-                return
-            dst = dr_grouped[g, h][:, lo:hi, :].rearrange("p (c i) t -> p c t i", i=4)
-            src = dr_raw[g, h][:, :, lo:hi].rearrange("p t (c i) -> p c t i", i=4)
-            if e == "S":
-                nc.scalar.copy(out=dst, in_=src)
+            dst, src = dr_grouped[g, h][:, lo:hi, :], dr_raw[g, h][:, :, lo:hi]
+            if engine == GPSIMD:
+                nc.gpsimd.tensor_scalar(out=dst, in0=src.rearrange("p t n -> p n t"), scalar1=1.0, scalar2=0.0, op0=ALU.mult, op1=ALU.add)
             else:
-                nc.vector.tensor_copy(out=dst, in_=src)
+                move(engine, dst.rearrange("p (c i) t -> p c t i", i=4), src.rearrange("p t (c i) -> p c t i", i=4))
 
         def quant_d(g, h):
             cols = slice(h * HALF, (h + 1) * HALF)
@@ -158,16 +151,9 @@ def tile_patch_gradient_magnitude_s1_kernel(tc, patches, d_row, d_col_words, d_c
             return bank
 
         def unit(s, j):
-            if s < FIRST:
-                return 2 * (s % (FIRST // 2)) + j, s // (FIRST // 2)
+            if s < SPLIT_TILES:
+                return 2 * (s % (SPLIT_TILES // 2)) + j, s // (SPLIT_TILES // 2)
             return s, j
-
-        def step_rows(tensor, s, lo, hi):
-            m, h = unit(s, lo)
-            rows = quad_rows(tensor, m)
-            if s < FIRST:
-                return rows[:, m % QUAD : m % QUAD + hi - lo, h * HALF : (h + 1) * HALF]
-            return rows[:, m % QUAD, lo * HALF : hi * HALF].rearrange("p (j n) -> p j n", n=HALF)
 
         def mm_gc(s, j):
             m, h = unit(s, j)
@@ -180,37 +166,39 @@ def tile_patch_gradient_magnitude_s1_kernel(tc, patches, d_row, d_col_words, d_c
             words = [dr_codes[:, g, cols].bitcast(FP8X4) for g in range(PASSES)]
             gr_bank[s, j] = product(m, words, [dr_scales[:, g, cols] for g in range(PASSES)])
 
-        def copy_gc(s, j, e="V"):
+        def copy_gc(s, j, engine):
             if s not in gc_sb:
                 gc = work.tile([P, N], F32)
                 gc_sb[s] = gc
-            dst = gc_sb[s][:, j * HALF : (j + 1) * HALF]
-            if e == "S":
-                nc.scalar.copy(out=dst, in_=gc_bank[s, j][:])
-            else:
-                nc.vector.tensor_copy(out=dst, in_=gc_bank[s, j][:])
+            move(engine, gc_sb[s][:, j * HALF : (j + 1) * HALF], gc_bank[s, j][:])
 
-        def square_gc(s, lo, hi, e):
-            if hi <= lo:
-                return
+        def gc_squared(s):
             if s not in gc_sq:
                 gc2 = work.tile([P, N], F32)
                 gc_sq[s] = gc2
-            gc, dst = gc_sb[s][:, lo:hi], gc_sq[s][:, lo:hi]
-            if e == "S":
-                nc.scalar.activation(out=dst, in_=gc, func=ACT.Square)
-            elif e == "W":
-                nc.vector.tensor_tensor(out=dst, in0=gc, in1=gc, op=ALU.mult)
-            elif e == "V":
-                for j in range(2):
-                    a, b = max(lo, j * HALF), min(hi, (j + 1) * HALF)
-                    if a < b:
-                        nc.vector.tensor_tensor(out=gc_sq[s][:, a:b], in0=gc_sb[s][:, a:b], in1=gc_bank[s, j][:, a - j * HALF : b - j * HALF], op=ALU.mult)
-            else:
-                nc.gpsimd.tensor_tensor(out=dst, in0=gc, in1=gc, op=ALU.mult)
+            return gc_sq[s]
 
-        def store(tensor, tile, s, lo, hi):
-            nc.sync.dma_start(out=step_rows(tensor, s, lo, hi), in_=tile[:, lo * HALF : hi * HALF].rearrange("p (j n) -> p j n", n=HALF))
+        def square_gc(s, lo, hi, engine):
+            dst, gc = gc_squared(s)[:, lo:hi], gc_sb[s][:, lo:hi]
+            if engine == SCALAR:
+                nc.scalar.activation(out=dst, in_=gc, func=ACT.Square)
+            else:
+                j = lo // HALF
+                nc.vector.tensor_tensor(out=dst, in0=gc, in1=gc_bank[s, j][:, lo - j * HALF : hi - j * HALF], op=ALU.mult)
+
+        def gate(s):
+            gc = gc_sb[s][:, N - GATE : N]
+            nc.vector.tensor_tensor(out=gc_squared(s)[:, N - GATE : N], in0=gc, in1=gc, op=ALU.mult)
+
+        def store(tensor, tile, s, units):
+            lo, hi = units
+            m, h = unit(s, lo)
+            rows = quad_rows(tensor, m)
+            if s < SPLIT_TILES:
+                dst = rows[:, m % QUAD : m % QUAD + hi - lo, h * HALF : (h + 1) * HALF]
+            else:
+                dst = rows[:, m % QUAD, lo * HALF : hi * HALF].rearrange("p (j n) -> p j n", n=HALF)
+            nc.sync.dma_start(out=dst, in_=tile[:, lo * HALF : hi * HALF].rearrange("p (j n) -> p j n", n=HALF))
 
         def diagonal(s, j, stored=None):
             if s not in diag:
@@ -219,203 +207,220 @@ def tile_patch_gradient_magnitude_s1_kernel(tc, patches, d_row, d_col_words, d_c
             cols = slice(j * HALF, (j + 1) * HALF)
             nc.vector.tensor_tensor(out=diag[s][:, cols], in0=gc_sb[s][:, cols], in1=gr_bank[s, j][:], op=ALU.add)
             if stored is not None:
-                store(out_1, diag[s], s, stored[0], stored[1])
+                store(out_1, diag[s], s, stored)
 
         def square_gr(s, j):
-            if s not in gr_sq:
-                gr2 = outs.tile([P, N], F32)
-                gr_sq[s] = gr2
-            nc.scalar.activation(out=gr_sq[s][:, j * HALF : (j + 1) * HALF], in_=gr_bank[s, j][:], func=ACT.Square)
+            if s not in magnitude:
+                mag = outs.tile([P, N], F32)
+                magnitude[s] = mag
+            nc.scalar.activation(out=magnitude[s][:, j * HALF : (j + 1) * HALF], in_=gr_bank[s, j][:], func=ACT.Square)
 
-        def add_squares(s, lo, hi, e):
-            engine = nc.gpsimd if e == "G" else nc.vector
-            cols = slice(lo * HALF, hi * HALF)
-            engine.tensor_tensor(out=gr_sq[s][:, cols], in0=gr_sq[s][:, cols], in1=gc_sq[s][:, cols], op=ALU.add)
+        def add_squares(s, units, engine):
+            cols = slice(units[0] * HALF, units[1] * HALF)
+            adder = nc.gpsimd if engine == GPSIMD else nc.vector
+            adder.tensor_tensor(out=magnitude[s][:, cols], in0=magnitude[s][:, cols], in1=gc_sq[s][:, cols], op=ALU.add)
 
-        def root(s, lo, hi, stored=None):
-            cols = slice(lo * HALF, hi * HALF)
-            nc.scalar.activation(out=gr_sq[s][:, cols], in_=gr_sq[s][:, cols], func=ACT.Sqrt, bias=FLOOR_SQUARED)
-            if stored is not None:
-                store(out_0, gr_sq[s], s, stored[0], stored[1])
+        def root(s, units):
+            cols = slice(units[0] * HALF, units[1] * HALF)
+            nc.scalar.activation(out=magnitude[s][:, cols], in_=magnitude[s][:, cols], func=ACT.Sqrt, bias=FLOOR_SQUARED)
+            store(out_0, magnitude[s], s, units)
 
-        def group_d(g, h, s_cols):
-            if s_cols:
-                inter(g, h, 0, s_cols, "S")
-            inter(g, h, s_cols, HALF, "V")
+        def window(s, m):
+            gate(s)
+            quant_x(m, 2)
+            add_squares(s, BOTH, GPSIMD)
 
-        for plane in dc_scales:
-            nc.vector.memset(plane[:].rearrange("p g n -> p (g n)").bitcast(I32), 0)
+        for scales in dc_scales:
+            nc.vector.memset(scales[:].rearrange("p g n -> p (g n)").bitcast(I32), 0)
         nc.gpsimd.memset(one[:], 1.0)
         make_identity(nc, ident[:])
 
         with tc.manual_schedule():
             load_x(0, 2)
-            load_d_row(0, 0)
-            load_scales(0)
-            load_words(0)
-            load_d_row(1, 0)
+            load_d_row(0, LEFT)
+            load_scales(LEFT)
+            load_words(LEFT)
+            load_d_row(1, LEFT)
             load_x(2, 2)
-            load_d_row(0, 1)
-            load_d_row(1, 1)
-            load_scales(1)
-            load_words(1)
+            load_d_row(0, RIGHT)
+            load_d_row(1, RIGHT)
+            load_scales(RIGHT)
+            load_words(RIGHT)
             load_x(4, 2)
             load_x(6, 2)
-            load_x(8, QUAD)
-            load_x(12, QUAD)
+            for m in range(2 * QUAD, TILES, QUAD):
+                load_x(m, QUAD)
             nc.scalar.activation(out=warm[:], in_=one[:], func=ACT.Sqrt, bias=FLOOR_SQUARED)
+
             turn(0)
             turn(1)
-            copy_x(0, "V")
-            inter(0, 0, 0, S_COLS, "S")
-            inter(0, 0, S_COLS, S_COLS + P, "V")
+            copy_x(0, VECTOR)
+            regroup(0, LEFT, 0, SCALAR_COLUMNS_LEFT, SCALAR)
+            regroup(0, LEFT, SCALAR_COLUMNS_LEFT, SCALAR_COLUMNS_LEFT + P, VECTOR)
             quant_x(0, 1)
-            inter(0, 0, S_COLS + P, HALF, "V")
-            copy_x(1, "S")
+            regroup(0, LEFT, SCALAR_COLUMNS_LEFT + P, HALF, VECTOR)
+            copy_x(1, SCALAR)
             mm_gc(0, 0)
             quant_x(1, 1)
-            quant_d(0, 0)
+            quant_d(0, LEFT)
             mm_gc(0, 1)
-            group_d(1, 0, S_COLS)
+            regroup(1, LEFT, 0, SCALAR_COLUMNS_LEFT, SCALAR)
+            regroup(1, LEFT, SCALAR_COLUMNS_LEFT, HALF, VECTOR)
             turn(2)
             turn(3)
-            copy_gc(0, 0, "S")
-            quant_d(1, 0)
+            copy_gc(0, 0, SCALAR)
+            quant_d(1, LEFT)
             mm_gr(0, 0)
             mm_gr(0, 1)
-            copy_gc(0, 1, "S")
-            square_gc(0, 0, HALF, "V")
-            copy_x(2, "S")
-            copy_x(3, "S")
-            inter(0, 1, 0, P, "V")
+
+            copy_gc(0, 1, SCALAR)
+            square_gc(0, 0, HALF, VECTOR)
+            copy_x(2, SCALAR)
+            copy_x(3, SCALAR)
+            regroup(0, RIGHT, 0, P, VECTOR)
             quant_x(2, 1)
-            inter(0, 1, P, 2 * P, "V")
+            regroup(0, RIGHT, P, 2 * P, VECTOR)
             quant_x(3, 1)
-            inter(0, 1, 2 * P, HALF, "V")
-            mm_gc(1, 0)
-            mm_gr(1, 0)
-            mm_gc(1, 1)
-            mm_gr(1, 1)
+            regroup(0, RIGHT, 2 * P, HALF, VECTOR)
+            for j in range(2):
+                mm_gc(1, j)
+                mm_gr(1, j)
             square_gr(0, 0)
             square_gr(0, 1)
-            copy_gc(1, 0, "S")
-            inter(1, 1, S_COLS_R, HALF, "G")
-            inter(1, 1, 0, S_COLS_R, "S")
+            copy_gc(1, 0, SCALAR)
+            dr_grouped[1, RIGHT] = dr_raw[0, RIGHT][:].rearrange("p t n -> p (t n)").rearrange("p (n t) -> p n t", t=PACK)
+            regroup(1, RIGHT, SCALAR_COLUMNS_LAST, HALF, GPSIMD)
+            regroup(1, RIGHT, 0, SCALAR_COLUMNS_LAST, SCALAR)
             diagonal(0, 0)
-            diagonal(0, 1, (0, 2))
+            diagonal(0, 1, BOTH)
+
             mm_gc(2, 0)
-            square_gc(1, 0, HALF, "V")
-            copy_gc(1, 1)
-            square_gc(0, HALF, N - V_SQH, "V")
+            square_gc(1, 0, HALF, VECTOR)
+            copy_gc(1, 1, VECTOR)
+            square_gc(0, HALF, N - GATE, VECTOR)
             turn(4)
             turn(5)
             mm_gc(2, 1)
             square_gr(1, 0)
             square_gr(1, 1)
-            quant_d(0, 1)
-            square_gc(0, N - V_SQH, N, "W")
-            quant_d(1, 1)
-            add_squares(0, 0, 2, "G")
-            square_gc(1, HALF, N - V_SQ1, "S")
-            copy_gc(2, 0, "S")
-            copy_x(4, "S")
-            copy_x(5, "S")
-            copy_gc(2, 1, "S")
+            quant_d(0, RIGHT)
+            gate(0)
+            quant_d(1, RIGHT)
+            add_squares(0, BOTH, GPSIMD)
+            square_gc(1, HALF, N - GATE, SCALAR)
+            copy_gc(2, 0, SCALAR)
+            copy_x(4, SCALAR)
+            copy_x(5, SCALAR)
+            copy_gc(2, 1, SCALAR)
             mm_gr(2, 0)
             diagonal(1, 0)
             mm_gr(2, 1)
-            diagonal(1, 1, (0, 2))
-            square_gc(2, 0, HALF, "V")
-            square_gc(2, HALF, N, "V")
+            diagonal(1, 1, BOTH)
+
+            square_gc(2, 0, HALF, VECTOR)
+            square_gc(2, HALF, N, VECTOR)
             mm_gc(3, 0)
             mm_gc(3, 1)
             square_gr(2, 0)
             square_gr(2, 1)
             mm_gr(3, 0)
             diagonal(2, 0)
-            copy_gc(3, 0, "S")
-            square_gc(1, N - V_SQ1, N, "W")
-            quant_x(4, 2)
-            add_squares(1, 0, 2, "G")
-            add_squares(2, 0, 2, "G")
-            diagonal(2, 1, (0, 2))
-            root(0, 0, 2, (0, 2))
+            copy_gc(3, 0, SCALAR)
+            window(1, 4)
+            add_squares(2, BOTH, GPSIMD)
+            diagonal(2, 1, BOTH)
+            root(0, BOTH)
             mm_gr(3, 1)
             turn(6)
             turn(7)
-            def x_pair(s):
-                return [s + 3, s + 4] if s % 2 == 1 and s + 3 < TILES else []
 
-
-            last = TILES - 1
-            def release(s, pair):
-                square_gc(s, N - GATE, N, "W")
-                quant_x(pair, 2)
-                add_squares(s, 0, 2, "G")
-            for s in range(3, last):
-                tiles = x_pair(s)
-                halves = s >= EARLY_FROM
-                place = LATE.get(s, 0) if s < CATCH and not tiles else None
+            for s in range(3, LAST_X_STEP):
+                odd = s % 2 == 1
+                squares_ahead = None if odd else max(0, 2 - (s - FIRST_WINDOW) // 2)
                 mm_gc(s + 1, 0)
-                copy_gc(s, 1)
-                if place == 0:
-                    release(s - 1, s + 2)
+                copy_gc(s, 1, VECTOR)
+                if squares_ahead == 0:
+                    window(s - 1, s + 2)
                 mm_gc(s + 1, 1)
-                early = s >= EARLY_FROM
-                for j in (1, 0) if early else (0, 1):
-                    square_gr(s, j)
-                square_gc(s, 0, HALF, "V")
-                if place == 1:
-                    release(s - 1, s + 2)
-                square_gc(s, HALF, N - GATE if tiles else N, "V")
-                if place == 2:
-                    release(s - 1, s + 2)
-                if s >= SPLIT_FROM:
-                    add_squares(s, 0, 1, "G")
-                    add_squares(s, 1, 2, "G")
-                elif not tiles:
-                    add_squares(s, 0, 2, "G")
+                square_gr(s, 0)
+                square_gr(s, 1)
+                square_gc(s, 0, HALF, VECTOR)
+                if squares_ahead == 1:
+                    window(s - 1, s + 2)
+                square_gc(s, HALF, N - GATE if odd else N, VECTOR)
+                if squares_ahead == 2:
+                    window(s - 1, s + 2)
+                if not odd:
+                    add_squares(s, BOTH, GPSIMD)
                 mm_gr(s + 1, 0)
-                rows = S_ROWS if s < CATCH else CATCH_ROWS
-                if tiles:
-                    copy_x(tiles[0], "S")
-                    if rows:
-                        copy_x(tiles[1], "S", 0, PASSES, slice(0, rows))
-                if s == CATCH:
-                    copy_x(tiles[1], "V", 0, PASSES, slice(rows, P))
-                if not early:
-                    diagonal(s, 0, (0, 1) if s == CATCH else None)
-                if s == CATCH:
-                    release(s, s + 3)
-                    root(s - 2, 0, 2, (0, 2))
-                if s > SPLIT_FROM:
-                    root(s - 1, 0, 1, (0, 1))
-                diagonal(s, 1, (1, 2) if s >= CATCH else (0, 2))
-                if tiles and s < CATCH:
-                    copy_x(tiles[1], "V", 0, PASSES, slice(rows, P))
-                copy_gc(s + 1, 0, "S")
-                if s + 1 == last:
-                    copy_gc(last, 1)
-                if s + 1 >= EARLY_FROM and s <= SPLIT_FROM:
-                    diagonal(s + 1, 0, (0, 1))
-                if s > SPLIT_FROM:
-                    root(s - 1, 1, 2, (1, 2))
-                else:
-                    root(s - 2 if s < CATCH else s - 1, 0, 2, (0, 2))
-                if s > SPLIT_FROM:
-                    diagonal(s + 1, 0, (0, 1))
+                if odd:
+                    copy_x(s + 3, SCALAR)
+                    copy_x(s + 4, SCALAR, 0, SCALAR_ROWS)
+                diagonal(s, 0)
+                diagonal(s, 1, BOTH)
+                if odd:
+                    copy_x(s + 4, VECTOR, SCALAR_ROWS, P)
+                copy_gc(s + 1, 0, SCALAR)
+                root(s - 2, BOTH)
                 mm_gr(s + 1, 1)
-                for m in x_pair(s + 1):
-                    turn(m)
-            square_gr(last, 1)
-            square_gr(last, 0)
-            square_gc(last, 0, HALF, "V")
-            diagonal(last, 1, (1, 2))
-            root(last - 1, 0, 1, (0, 1))
-            square_gc(last, HALF, N - V_END, "S")
-            square_gc(last, N - V_END, N, "V")
-            add_squares(last, 0, 1, "V")
-            root(last - 1, 1, 2, (1, 2))
-            add_squares(last, 1, 2, "V")
-            root(last, 0, 1, (0, 1))
-            root(last, 1, 2, (1, 2))
+                if not odd:
+                    turn(s + 4)
+                    turn(s + 5)
+
+            s = LAST_X_STEP
+            mm_gr(s + 1, 0)
+            mm_gc(s + 1, 0)
+            copy_gc(s, 1, VECTOR)
+            copy_x(s + 3, SCALAR)
+            mm_gc(s + 1, 1)
+            square_gr(s, 0)
+            square_gr(s, 1)
+            square_gc(s, 0, HALF, VECTOR)
+            square_gc(s, HALF, N - GATE, VECTOR)
+            copy_x(s + 4, VECTOR)
+            diagonal(s, 0, FIRST_UNIT)
+            window(s, s + 3)
+            root(s - 2, BOTH)
+            diagonal(s, 1, SECOND_UNIT)
+            copy_gc(s + 1, 0, SCALAR)
+            diagonal(s + 1, 0, FIRST_UNIT)
+            root(s - 1, BOTH)
+            mm_gr(s + 1, 1)
+
+            for s in range(LAST_X_STEP + 1, LAST):
+                mm_gr(s + 1, 0)
+                mm_gc(s + 1, 0)
+                copy_gc(s, 1, VECTOR)
+                mm_gc(s + 1, 1)
+                square_gr(s, 1)
+                square_gr(s, 0)
+                square_gc(s, 0, HALF, VECTOR)
+                square_gc(s, HALF, N, VECTOR)
+                for units in (BOTH,) if s < LAST - 2 else (FIRST_UNIT, SECOND_UNIT):
+                    add_squares(s, units, GPSIMD)
+                if s < LAST - 1:
+                    diagonal(s, 1, SECOND_UNIT)
+                    copy_gc(s + 1, 0, SCALAR)
+                    diagonal(s + 1, 0, FIRST_UNIT)
+                    root(s - 1, BOTH)
+                else:
+                    root(s - 1, FIRST_UNIT)
+                    diagonal(s, 1, SECOND_UNIT)
+                    copy_gc(s + 1, 0, SCALAR)
+                    copy_gc(s + 1, 1, VECTOR)
+                    root(s - 1, SECOND_UNIT)
+                    diagonal(s + 1, 0, FIRST_UNIT)
+                mm_gr(s + 1, 1)
+
+            square_gr(LAST, 1)
+            square_gr(LAST, 0)
+            square_gc(LAST, 0, HALF, VECTOR)
+            diagonal(LAST, 1, SECOND_UNIT)
+            root(LAST - 1, FIRST_UNIT)
+            square_gc(LAST, HALF, N - VECTOR_COLUMNS_END, SCALAR)
+            square_gc(LAST, N - VECTOR_COLUMNS_END, N, VECTOR)
+            add_squares(LAST, FIRST_UNIT, VECTOR)
+            root(LAST - 1, SECOND_UNIT)
+            add_squares(LAST, SECOND_UNIT, VECTOR)
+            root(LAST, FIRST_UNIT)
+            root(LAST, SECOND_UNIT)

@@ -83,10 +83,10 @@ def tile_patch_gradient_magnitude_s1_kernel(tc, patches, d_row, d_col_words, d_c
             nc.sync.dma_start(out=dc_words[:, h, :, :].bitcast(I32), in_=d_col_words[:, :, half].rearrange("g p w -> p g w").bitcast(I32))
 
         def load_scales(h):
-            for q in range(4):
+            for r in range(4):
                 nc.sync.dma_start(
-                    out=dc_scales[h][32 * q : 32 * q + 4, :, :].bitcast(I32),
-                    in_=d_col_scales[:, 4 * q : 4 * q + 4, h * HALF : (h + 1) * HALF].rearrange("g r n -> r g n").bitcast(I32),
+                    out=dc_scales[h][r:P:32, :, :].bitcast(I32),
+                    in_=d_col_scales[:, r:16:4, h * HALF : (h + 1) * HALF].rearrange("g q n -> q g n").bitcast(I32),
                 )
 
         def move(engine, dst, src):

@@ -33,7 +33,8 @@ LAST = TILES - 1
 LAST_X_STEP = TILES - 5
 FIRST_WINDOW = 4
 
-SCALAR_COLUMNS_LEFT = 192
+SCALAR_COLUMNS_FIRST = 128
+SCALAR_COLUMNS_SECOND = 192
 SCALAR_COLUMNS_LAST = 128
 SCALAR_ROWS = 88
 VECTOR_COLUMNS_END = 320
@@ -78,9 +79,9 @@ def tile_patch_gradient_magnitude_s1_kernel(tc, patches, d_row, d_col_words, d_c
             dr_raw[g, h] = raw
             nc.sync.dma_start(out=raw[:], in_=rows.rearrange("(p t) n -> p t n", t=PACK))
 
-        def load_words(h):
-            half = slice(2 * h * HALF, 2 * (h + 1) * HALF)
-            nc.sync.dma_start(out=dc_words[:, h, :, :].bitcast(I32), in_=d_col_words[:, :, half].rearrange("g p w -> p g w").bitcast(I32))
+        def load_words(h, lo=0, hi=PASSES):
+            words = d_col_words[lo:hi, :, 2 * h * HALF : 2 * (h + 1) * HALF]
+            nc.sync.dma_start(out=dc_words[:, h, lo:hi, :].bitcast(I32), in_=words.rearrange("g p w -> p g w").bitcast(I32))
 
         def load_scales(h):
             for r in range(4):
@@ -236,12 +237,15 @@ def tile_patch_gradient_magnitude_s1_kernel(tc, patches, d_row, d_col_words, d_c
         make_identity(nc, ident[:])
 
         with tc.manual_schedule():
-            load_x(0, 2)
+            load_x(0, 1)
+            load_x(1, 1)
             load_d_row(0, LEFT)
             load_scales(LEFT)
-            load_words(LEFT)
+            for g in range(PASSES):
+                load_words(LEFT, g, g + 1)
             load_d_row(1, LEFT)
-            load_x(2, 2)
+            load_x(2, 1)
+            load_x(3, 1)
             load_d_row(0, RIGHT)
             load_d_row(1, RIGHT)
             load_scales(RIGHT)
@@ -255,17 +259,16 @@ def tile_patch_gradient_magnitude_s1_kernel(tc, patches, d_row, d_col_words, d_c
             turn(0)
             turn(1)
             copy_x(0, VECTOR)
-            regroup(0, LEFT, 0, SCALAR_COLUMNS_LEFT, SCALAR)
-            regroup(0, LEFT, SCALAR_COLUMNS_LEFT, SCALAR_COLUMNS_LEFT + P, VECTOR)
-            quant_x(0, 1)
-            regroup(0, LEFT, SCALAR_COLUMNS_LEFT + P, HALF, VECTOR)
             copy_x(1, SCALAR)
+            quant_x(0, 1)
+            regroup(0, LEFT, 0, SCALAR_COLUMNS_FIRST, SCALAR)
+            regroup(0, LEFT, SCALAR_COLUMNS_FIRST, HALF, VECTOR)
             mm_gc(0, 0)
             quant_x(1, 1)
             quant_d(0, LEFT)
             mm_gc(0, 1)
-            regroup(1, LEFT, 0, SCALAR_COLUMNS_LEFT, SCALAR)
-            regroup(1, LEFT, SCALAR_COLUMNS_LEFT, HALF, VECTOR)
+            regroup(1, LEFT, 0, SCALAR_COLUMNS_SECOND, SCALAR)
+            regroup(1, LEFT, SCALAR_COLUMNS_SECOND, HALF, VECTOR)
             turn(2)
             turn(3)
             copy_gc(0, 0, SCALAR)

@@ -19,26 +19,25 @@ PACK = 4
 K_PASS = P * PACK
 PASSES = K // K_PASS
 HALF = 512
+BANKS = 8
 TILES = M // P
 QUAD = 4
+RAW_TILES = 16
 FLOOR_SQUARED = 0.0625
 FLOPS = 2 * 2 * M * K * N
 
 LEFT, RIGHT = 0, 1
 SCALAR, VECTOR, GPSIMD = "scalar", "vector", "gpsimd"
-BOTH, FIRST_UNIT, SECOND_UNIT = (0, 2), (0, 1), (1, 2)
+TURN, GC, GR, SUM = "turn", "gc", "gr", "sum"
+BOTH, FIRST_UNIT, SECOND_UNIT = (0, N), (0, HALF), (HALF, N)
 
 SPLIT_TILES = 4
+SPLIT_STEPS = SPLIT_TILES // 2
 LAST = TILES - 1
-LAST_X_STEP = TILES - 5
-FIRST_WINDOW = 4
-
 SCALAR_COLUMNS_FIRST = 128
-SCALAR_COLUMNS_SECOND = 192
-SCALAR_COLUMNS_LAST = 128
-SCALAR_ROWS = 88
-VECTOR_COLUMNS_END = 320
 GATE = 128
+PART = K
+GATED = (0, 1, 3, 5, 7, 9, 11)
 
 
 def tile_patch_gradient_magnitude_s1_kernel(tc, patches, d_row, d_col_words, d_col_scales, out_0, out_1):
@@ -48,12 +47,12 @@ def tile_patch_gradient_magnitude_s1_kernel(tc, patches, d_row, d_col_words, d_c
         stage = ctx.enter_context(tc.tile_pool(name="stage", bufs=2))
         work = ctx.enter_context(tc.tile_pool(name="work", bufs=4))
         outs = ctx.enter_context(tc.tile_pool(name="outs", bufs=TILES))
-        psum = ctx.enter_context(tc.psum_pool(name="psum", bufs=8))
+        psum = ctx.enter_context(tc.psum_pool(name="psum", bufs=BANKS))
 
         ident = keep.tile([P, P], F32)
         one = keep.tile([P, 1], F32)
         warm = keep.tile([P, 1], F32)
-        x_raw = keep.tile([P, TILES, K], BF16, align_bytes=64)
+        x_raw = keep.tile([P, RAW_TILES, K], BF16, align_bytes=64)
         x_codes = keep.tile([P, TILES, PASSES * P], U32, align_bytes=64)
         x_scales = keep.tile([P, TILES, PASSES * P], U8, align_bytes=64)
         dr_codes = keep.tile([P, PASSES, N], U32, align_bytes=64)
@@ -63,15 +62,16 @@ def tile_patch_gradient_magnitude_s1_kernel(tc, patches, d_row, d_col_words, d_c
         right_scales = keep.tile([P, PASSES, HALF], U8, align_bytes=64)
         dc_scales = [left_scales, right_scales]
 
-        x_turned, x_grouped, dr_raw, dr_grouped = {}, {}, {}, {}
-        gc_bank, gr_bank, gc_sb, gc_sq, magnitude, diag = {}, {}, {}, {}, {}, {}
+        x_grouped, dr_raw, dr_grouped = {}, {}, {}
+        banks, gc_sb, gc_sq, magnitude, diag = {}, {}, {}, {}, {}
 
         def quad_rows(tensor, m):
             first = m // QUAD * QUAD * P
             return tensor[first : first + QUAD * P, :].rearrange("(p a) k -> p a k", a=QUAD)
 
         def load_x(m, count):
-            nc.sync.dma_start(out=x_raw[:, m : m + count, :], in_=quad_rows(patches, m)[:, m % QUAD : m % QUAD + count, :])
+            at = m % RAW_TILES
+            nc.sync.dma_start(out=x_raw[:, at : at + count, :], in_=quad_rows(patches, m)[:, m % QUAD : m % QUAD + count, :])
 
         def load_d_row(g, h):
             rows = d_row[g * K_PASS : (g + 1) * K_PASS, h * HALF : (h + 1) * HALF]
@@ -96,140 +96,194 @@ def tile_patch_gradient_magnitude_s1_kernel(tc, patches, d_row, d_col_words, d_c
             else:
                 nc.vector.tensor_copy(out=dst, in_=src)
 
+        def unit(s, j):
+            if s < SPLIT_TILES:
+                return 2 * (s % SPLIT_STEPS) + j, s // SPLIT_STEPS
+            return s, j
+
+        def place(m, h):
+            if m < SPLIT_TILES:
+                return m // 2 + h * SPLIT_STEPS, m % 2
+            return m, h
+
         def turn(m):
             bank = psum.tile([P, PASSES, 2, P], F32, tag="bank")
-            words = x_raw[:, m, :].bitcast(F32)
+            words = x_raw[:, m % RAW_TILES, :].bitcast(F32)
             for g in range(PASSES):
                 for u in range(2):
                     nc.tensor.transpose(bank[:, g, u, :], words[:, 2 * P * g + u : 2 * P * (g + 1) : 2], ident[:])
-            x_turned[m] = bank
+            return bank
 
-        def copy_x(m, engine, lo=0, hi=P):
-            if m // 2 not in x_grouped:
-                grouped = stage.tile([P, 2, PASSES, P, PACK], BF16, align_bytes=64)
-                x_grouped[m // 2] = grouped
-            dst = x_grouped[m // 2][:, m % 2, :, lo:hi, :].bitcast(F32)
-            move(engine, dst, x_turned[m][:, :, :, lo:hi].rearrange("p g u r -> p g r u"))
-
-        def quant_x(m, count):
-            nc.vector.quantize_mx(
-                out=x_codes[:, m : m + count, :].rearrange("p a w -> p (a w)").bitcast(FP8X4),
-                scales=x_scales[:, m : m + count, :].rearrange("p a w -> p (a w)"),
-                in_=x_grouped[m // 2][:, m % 2 : m % 2 + count, :, :, :].rearrange("p a g r t -> p (a g r t)"),
-            )
-
-        def regroup(g, h, lo, hi, engine):
-            if (g, h) not in dr_grouped:
-                grouped = outs.tile([P, HALF, PACK], BF16, tag="diag", align_bytes=64)
-                dr_grouped[g, h] = grouped
-            dst, src = dr_grouped[g, h][:, lo:hi, :], dr_raw[g, h][:, :, lo:hi]
-            if engine == GPSIMD:
-                nc.gpsimd.tensor_scalar(out=dst, in0=src.rearrange("p t n -> p n t"), scalar1=1.0, scalar2=0.0, op0=ALU.mult, op1=ALU.add)
-            else:
-                move(engine, dst.rearrange("p (c i) t -> p c t i", i=4), src.rearrange("p t (c i) -> p c t i", i=4))
-
-        def quant_d(g, h):
+        def product(kind, s, j):
+            m, h = unit(s, j)
             cols = slice(h * HALF, (h + 1) * HALF)
-            nc.vector.quantize_mx(
-                out=dr_codes[:, g, cols].bitcast(FP8X4),
-                scales=dr_scales[:, g, cols],
-                in_=dr_grouped[g, h][:].rearrange("p n t -> p (n t)"),
-            )
-
-        def product(m, words, scales):
+            col_passes = [(g, dc_words[:, h, g, :].bitcast(FP4X4), dc_scales[h][:, g, :]) for g in range(PASSES)]
+            row_passes = [(g, dr_codes[:, g, cols].bitcast(FP8X4), dr_scales[:, g, cols]) for g in range(PASSES)]
+            passes = {GC: col_passes, GR: row_passes, SUM: col_passes + row_passes}[kind]
             bank = psum.tile([P, HALF], F32, tag="bank")
-            for g in range(PASSES):
+            for i, (g, words, scales) in enumerate(passes):
                 rows = slice(g * P, (g + 1) * P)
                 nc.tensor.matmul_mx(
                     out=bank[:],
                     lhsT=x_codes[:, m, rows].bitcast(FP8X4),
                     lhsT_scale=x_scales[:, m, rows],
-                    rhs=words[g],
-                    rhs_scale=scales[g],
-                    start=(g == 0),
-                    stop=(g == PASSES - 1),
+                    rhs=words,
+                    rhs_scale=scales,
+                    start=(i == 0),
+                    stop=(i == len(passes) - 1),
                 )
             return bank
 
-        def unit(s, j):
-            if s < SPLIT_TILES:
-                return 2 * (s % (SPLIT_TILES // 2)) + j, s // (SPLIT_TILES // 2)
-            return s, j
+        jobs = [(TURN, 0), (TURN, 1), (GC, 0, 0), (GC, 0, 1), (TURN, 2), (TURN, 3), (GR, 0, 0), (GR, 0, 1)]
+        jobs.extend([(GC, 1, 0), (GR, 1, 0), (GC, 1, 1), (GR, 1, 1), (GC, 2, 0), (TURN, 4), (TURN, 5), (GC, 2, 1), (GR, 2, 0), (GR, 2, 1)])
+        for s in range(3, TILES):
+            jobs.extend([(GC, s, 0), (GC, s, 1), (GR, s, 0)] if s < 12 else [(GR, s, 0), (GC, s, 0), (GC, s, 1)])
+            jobs.append((GR, s, 1))
+            if s % 2 == 1 and s + 4 < TILES:
+                jobs.extend([(TURN, s + 3), (TURN, s + 4)])
+        given, emptied, readers, quantised = [], [], {}, set()
 
-        def mm_gc(s, j):
-            m, h = unit(s, j)
-            words = [dc_words[:, h, g, :].bitcast(FP4X4) for g in range(PASSES)]
-            gc_bank[s, j] = product(m, words, [dc_scales[h][:, g, :] for g in range(PASSES)])
+        def feed():
+            while len(given) < len(jobs) and len(given) - len(emptied) < BANKS:
+                job = jobs[len(given)]
+                if job[0] == TURN:
+                    banks[job] = turn(job[1])
+                else:
+                    m, h = unit(job[1], job[2])
+                    if m not in quantised or (job[0] != GC and not all((g, h) in quantised for g in range(PASSES))):
+                        return
+                    banks[job] = product(job[0], job[1], job[2])
+                given.append(job)
 
-        def mm_gr(s, j):
-            m, h = unit(s, j)
-            cols = slice(h * HALF, (h + 1) * HALF)
-            words = [dr_codes[:, g, cols].bitcast(FP8X4) for g in range(PASSES)]
-            gr_bank[s, j] = product(m, words, [dr_scales[:, g, cols] for g in range(PASSES)])
+        def was_read(job, of):
+            readers[job] = readers.get(job, 0) + 1
+            if readers[job] == of:
+                emptied.append(job)
+            feed()
 
-        def copy_gc(s, j, engine):
+        def copy_x(m, engine, lo=0, hi=P):
+            if m not in x_grouped:
+                pair = stage.tile([P, 2 * PART], BF16, align_bytes=64)
+                x_grouped[m], x_grouped[m + 1], x_grouped[m, "pair"] = pair[:, :PART], pair[:, PART:], pair
+            dst = x_grouped[m].bitcast(F32).rearrange("p (g r u) -> p g r u", g=PASSES, u=2)[:, :, lo:hi, :]
+            move(engine, dst, banks[TURN, m][:, :, :, lo:hi].rearrange("p g u r -> p g r u"))
+            was_read((TURN, m), 1 if hi - lo == P else 2)
+
+        def quant_x(m, count):
+            nc.vector.quantize_mx(
+                out=x_codes[:, m : m + count, :].rearrange("p a w -> p (a w)").bitcast(FP8X4),
+                scales=x_scales[:, m : m + count, :].rearrange("p a w -> p (a w)"),
+                in_=x_grouped[m] if count == 1 else x_grouped[m, "pair"][:],
+            )
+            for a in range(count):
+                quantised.add(m + a)
+            feed()
+
+        def regroup(g, h, lo, hi, engine):
+            if (g, h) not in dr_grouped:
+                grouped = outs.tile([P, PACK * HALF], BF16, tag="diag", align_bytes=64)
+                dr_grouped[g, h] = grouped[:]
+            dst, src = dr_grouped[g, h].rearrange("p (n t) -> p n t", t=PACK)[:, lo:hi, :], dr_raw[g, h][:, :, lo:hi]
+            if engine == GPSIMD:
+                nc.gpsimd.tensor_scalar(out=dst, in0=src.rearrange("p t n -> p n t"), scalar1=1.0, scalar2=0.0, op0=ALU.mult, op1=ALU.add)
+            else:
+                move(engine, dst.rearrange("p (c i) t -> p c t i", i=4), src.rearrange("p t (c i) -> p c t i", i=4))
+
+        def quant_d(g, h, parts):
+            for lo, hi in parts:
+                cols = slice(h * HALF + lo, h * HALF + hi)
+                nc.vector.quantize_mx(out=dr_codes[:, g, cols].bitcast(FP8X4), scales=dr_scales[:, g, cols], in_=dr_grouped[g, h][:, PACK * lo : PACK * hi])
+            quantised.add((g, h))
+            feed()
+
+        def gc_copy(s, j):
             if s not in gc_sb:
                 gc = work.tile([P, N], F32)
                 gc_sb[s] = gc
-            move(engine, gc_sb[s][:, j * HALF : (j + 1) * HALF], gc_bank[s, j][:])
+            return gc_sb[s][:, j * HALF : (j + 1) * HALF]
 
-        def gc_squared(s):
+        def diag_of(s, j):
+            if s not in diag:
+                dg = outs.tile([P, N], F32, tag="diag", align_bytes=64)
+                diag[s] = dg
+            return diag[s][:, j * HALF : (j + 1) * HALF]
+
+        def copy_gc(s, j, engine, of=2):
+            move(engine, gc_copy(s, j), banks[GC, s, j][:])
+            was_read((GC, s, j), of)
+
+        def squares(s):
             if s not in gc_sq:
                 gc2 = work.tile([P, N], F32)
                 gc_sq[s] = gc2
             return gc_sq[s]
 
-        def square_gc(s, lo, hi, engine):
-            dst, gc = gc_squared(s)[:, lo:hi], gc_sb[s][:, lo:hi]
+        def square_gc(s, j, engine, lo=0, hi=HALF, of=2):
+            hi = min(hi, HALF - GATE) if s in GATED and j == 1 else hi
+            dst, bank = squares(s)[:, j * HALF + lo : j * HALF + hi], banks[GC, s, j][:, lo:hi]
             if engine == SCALAR:
-                nc.scalar.activation(out=dst, in_=gc, func=ACT.Square)
+                nc.scalar.activation(out=dst, in_=bank, func=ACT.Square)
             else:
-                j = lo // HALF
-                nc.vector.tensor_tensor(out=dst, in0=gc, in1=gc_bank[s, j][:, lo - j * HALF : hi - j * HALF], op=ALU.mult)
+                nc.vector.tensor_tensor(out=dst, in0=gc_copy(s, j)[:, lo:hi], in1=bank, op=ALU.mult)
+            was_read((GC, s, j), of)
 
-        def gate(s):
-            gc = gc_sb[s][:, N - GATE : N]
-            nc.vector.tensor_tensor(out=gc_squared(s)[:, N - GATE : N], in0=gc, in1=gc, op=ALU.mult)
-
-        def store(tensor, tile, s, units):
-            lo, hi = units
-            m, h = unit(s, lo)
-            rows = quad_rows(tensor, m)
-            if s < SPLIT_TILES:
-                dst = rows[:, m % QUAD : m % QUAD + hi - lo, h * HALF : (h + 1) * HALF]
-            else:
-                dst = rows[:, m % QUAD, lo * HALF : hi * HALF].rearrange("p (j n) -> p j n", n=HALF)
-            nc.sync.dma_start(out=dst, in_=tile[:, lo * HALF : hi * HALF].rearrange("p (j n) -> p j n", n=HALF))
-
-        def diagonal(s, j, stored=None):
-            if s not in diag:
-                dg = outs.tile([P, N], F32, tag="diag", align_bytes=64)
-                diag[s] = dg
-            cols = slice(j * HALF, (j + 1) * HALF)
-            nc.vector.tensor_tensor(out=diag[s][:, cols], in0=gc_sb[s][:, cols], in1=gr_bank[s, j][:], op=ALU.add)
+        def copy_sum(s, j, stored=None):
+            nc.vector.tensor_copy(out=diag_of(s, j), in_=banks[SUM, s, j][:])
+            was_read((SUM, s, j), 1)
             if stored is not None:
                 store(out_1, diag[s], s, stored)
 
-        def square_gr(s, j):
+        def square_copy(s, j, lo=0, hi=HALF):
+            hi = min(hi, HALF - GATE) if s in GATED and j == 1 else hi
+            nc.scalar.activation(out=squares(s)[:, j * HALF + lo : j * HALF + hi], in_=gc_copy(s, j)[:, lo:hi], func=ACT.Square)
+            was_read((GC, s, j), 2 if lo > 0 or hi >= HALF - GATE else 9)
+
+        def gate(s):
+            gc = gc_copy(s, 1)[:, HALF - GATE :]
+            nc.vector.tensor_tensor(out=squares(s)[:, N - GATE :], in0=gc, in1=gc, op=ALU.mult)
+
+        def store(tensor, tile, s, cols, queue=nc.sync):
+            lo, hi = cols
+            m, h = unit(s, 0)
+            rows = quad_rows(tensor, m)
+            if s < SPLIT_TILES:
+                dst = rows[:, m % QUAD : m % QUAD + 2, h * HALF : (h + 1) * HALF]
+                nc.sync.dma_start(out=dst, in_=tile[:].rearrange("p (j n) -> p j n", n=HALF))
+            else:
+                queue.dma_start(out=rows[:, m % QUAD, lo:hi], in_=tile[:, lo:hi])
+
+        def diagonal(s, j, stored=None):
+            nc.vector.tensor_tensor(out=diag_of(s, j), in0=gc_copy(s, j), in1=banks[GR, s, j][:], op=ALU.add)
+            was_read((GR, s, j), 2)
+            if stored is not None:
+                store(out_1, diag[s], s, stored)
+
+        def square_gr(s, j, of=2):
             if s not in magnitude:
                 mag = outs.tile([P, N], F32)
                 magnitude[s] = mag
-            nc.scalar.activation(out=magnitude[s][:, j * HALF : (j + 1) * HALF], in_=gr_bank[s, j][:], func=ACT.Square)
+            nc.scalar.activation(out=magnitude[s][:, j * HALF : (j + 1) * HALF], in_=banks[GR, s, j][:], func=ACT.Square)
+            was_read((GR, s, j), of)
 
         def add_squares(s, units, engine):
-            cols = slice(units[0] * HALF, units[1] * HALF)
+            cols = slice(units[0], units[1])
             adder = nc.gpsimd if engine == GPSIMD else nc.vector
             adder.tensor_tensor(out=magnitude[s][:, cols], in0=magnitude[s][:, cols], in1=gc_sq[s][:, cols], op=ALU.add)
 
-        def root(s, units):
-            cols = slice(units[0] * HALF, units[1] * HALF)
+        def root(s, units, queue=None):
+            cols = slice(units[0], units[1])
             nc.scalar.activation(out=magnitude[s][:, cols], in_=magnitude[s][:, cols], func=ACT.Sqrt, bias=FLOOR_SQUARED)
-            store(out_0, magnitude[s], s, units)
+            if queue is None:
+                store(out_0, magnitude[s], s, units)
 
-        def window(s, m):
-            gate(s)
-            quant_x(m, 2)
-            add_squares(s, BOTH, GPSIMD)
+        def empty_gc(m, h):
+            s, j = place(m, h)
+            square_gc(s, j, SCALAR)
+            copy_gc(s, j, VECTOR)
+
+        def empty_gr(s, j):
+            square_gr(s, j)
+            diagonal(s, j, BOTH if j == 1 else None)
 
         for scales in dc_scales:
             nc.vector.memset(scales[:].rearrange("p g n -> p (g n)").bitcast(I32), 0)
@@ -256,28 +310,20 @@ def tile_patch_gradient_magnitude_s1_kernel(tc, patches, d_row, d_col_words, d_c
                 load_x(m, QUAD)
             nc.scalar.activation(out=warm[:], in_=one[:], func=ACT.Sqrt, bias=FLOOR_SQUARED)
 
-            turn(0)
-            turn(1)
+            feed()
             copy_x(0, VECTOR)
             copy_x(1, SCALAR)
             quant_x(0, 1)
-            regroup(0, LEFT, 0, SCALAR_COLUMNS_FIRST, SCALAR)
-            regroup(0, LEFT, SCALAR_COLUMNS_FIRST, HALF, VECTOR)
-            mm_gc(0, 0)
+            regroup(0, LEFT, 0, 128, SCALAR)
+            regroup(0, LEFT, 128, HALF, VECTOR)
             quant_x(1, 1)
-            quant_d(0, LEFT)
-            mm_gc(0, 1)
-            regroup(1, LEFT, 0, SCALAR_COLUMNS_SECOND, SCALAR)
-            regroup(1, LEFT, SCALAR_COLUMNS_SECOND, HALF, VECTOR)
-            turn(2)
-            turn(3)
+            quant_d(0, LEFT, [(0, HALF)])
+            regroup(1, LEFT, 0, 192, SCALAR)
+            regroup(1, LEFT, 192, HALF, VECTOR)
             copy_gc(0, 0, SCALAR)
-            quant_d(1, LEFT)
-            mm_gr(0, 0)
-            mm_gr(0, 1)
-
+            quant_d(1, LEFT, [(0, HALF)])
             copy_gc(0, 1, SCALAR)
-            square_gc(0, 0, HALF, VECTOR)
+            square_gc(0, 0, VECTOR)
             copy_x(2, SCALAR)
             copy_x(3, SCALAR)
             regroup(0, RIGHT, 0, P, VECTOR)
@@ -285,145 +331,139 @@ def tile_patch_gradient_magnitude_s1_kernel(tc, patches, d_row, d_col_words, d_c
             regroup(0, RIGHT, P, 2 * P, VECTOR)
             quant_x(3, 1)
             regroup(0, RIGHT, 2 * P, HALF, VECTOR)
-            for j in range(2):
-                mm_gc(1, j)
-                mm_gr(1, j)
             square_gr(0, 0)
             square_gr(0, 1)
             copy_gc(1, 0, SCALAR)
-            dr_grouped[1, RIGHT] = dr_raw[0, RIGHT][:].rearrange("p t n -> p (t n)").rearrange("p (n t) -> p n t", t=PACK)
-            regroup(1, RIGHT, SCALAR_COLUMNS_LAST, HALF, GPSIMD)
-            regroup(1, RIGHT, 0, SCALAR_COLUMNS_LAST, SCALAR)
+            dr_grouped[1, RIGHT] = dr_raw[0, RIGHT][:].rearrange("p t n -> p (t n)")
+            regroup(1, RIGHT, 128, HALF, GPSIMD)
+            regroup(1, RIGHT, 0, 128, SCALAR)
             diagonal(0, 0)
             diagonal(0, 1, BOTH)
-
-            mm_gc(2, 0)
-            square_gc(1, 0, HALF, VECTOR)
+            square_gc(1, 0, VECTOR)
             copy_gc(1, 1, VECTOR)
-            square_gc(0, HALF, N - GATE, VECTOR)
-            turn(4)
-            turn(5)
-            mm_gc(2, 1)
+            square_gc(0, 1, VECTOR)
             square_gr(1, 0)
             square_gr(1, 1)
-            quant_d(0, RIGHT)
+            quant_d(0, RIGHT, [(0, HALF)])
             gate(0)
-            quant_d(1, RIGHT)
+            quant_d(1, RIGHT, [(0, HALF)])
             add_squares(0, BOTH, GPSIMD)
-            square_gc(1, HALF, N - GATE, SCALAR)
+            square_copy(1, 1)
             copy_gc(2, 0, SCALAR)
             copy_x(4, SCALAR)
             copy_x(5, SCALAR)
             copy_gc(2, 1, SCALAR)
-            mm_gr(2, 0)
             diagonal(1, 0)
-            mm_gr(2, 1)
             diagonal(1, 1, BOTH)
-
-            square_gc(2, 0, HALF, VECTOR)
-            square_gc(2, HALF, N, VECTOR)
-            mm_gc(3, 0)
-            mm_gc(3, 1)
+            square_gc(2, 0, VECTOR)
+            square_gc(2, 1, VECTOR)
             square_gr(2, 0)
             square_gr(2, 1)
-            mm_gr(3, 0)
             diagonal(2, 0)
             copy_gc(3, 0, SCALAR)
-            window(1, 4)
+            gate(1)
+            quant_x(4, 2)
+            add_squares(1, BOTH, GPSIMD)
             add_squares(2, BOTH, GPSIMD)
             diagonal(2, 1, BOTH)
             root(0, BOTH)
-            mm_gr(3, 1)
-            turn(6)
-            turn(7)
 
-            for s in range(3, LAST_X_STEP):
+            def window(s, m):
+                gate(s)
+                quant_x(m, 2)
+                add_squares(s, BOTH, GPSIMD)
+
+            for s in range(3, 11):
                 odd = s % 2 == 1
-                squares_ahead = None if odd else max(0, 2 - (s - FIRST_WINDOW) // 2)
-                mm_gc(s + 1, 0)
-                copy_gc(s, 1, VECTOR)
-                if squares_ahead == 0:
+                summed = False
+                squares_ahead = None if odd else max(0, 2 - (s - 4) // 2)
+                if summed:
+                    square_gr(s, 1)
+                    square_gc(s, 1, SCALAR, of=1)
+                    square_gr(s, 0)
                     window(s - 1, s + 2)
-                mm_gc(s + 1, 1)
-                square_gr(s, 0)
-                square_gr(s, 1)
-                square_gc(s, 0, HALF, VECTOR)
-                if squares_ahead == 1:
-                    window(s - 1, s + 2)
-                square_gc(s, HALF, N - GATE if odd else N, VECTOR)
-                if squares_ahead == 2:
-                    window(s - 1, s + 2)
-                if not odd:
+                    square_gc(s, 0, VECTOR)
                     add_squares(s, BOTH, GPSIMD)
-                mm_gr(s + 1, 0)
-                if odd:
-                    copy_x(s + 3, SCALAR)
-                    copy_x(s + 4, SCALAR, 0, SCALAR_ROWS)
-                diagonal(s, 0)
-                diagonal(s, 1, BOTH)
-                if odd:
-                    copy_x(s + 4, VECTOR, SCALAR_ROWS, P)
+                    diagonal(s, 0)
+                    copy_sum(s, 1, BOTH)
+                else:
+                    copy_gc(s, 1, VECTOR)
+                    if squares_ahead == 0:
+                        window(s - 1, s + 2)
+                    square_gr(s, 0)
+                    square_gr(s, 1)
+                    square_gc(s, 0, VECTOR)
+                    if squares_ahead == 1:
+                        window(s - 1, s + 2)
+                    square_gc(s, 1, VECTOR)
+                    if squares_ahead == 2:
+                        window(s - 1, s + 2)
+                    if not odd:
+                        add_squares(s, BOTH, GPSIMD)
+                    if odd:
+                        copy_x(s + 3, SCALAR)
+                        copy_x(s + 4, SCALAR, 0, 88)
+                    diagonal(s, 0)
+                    diagonal(s, 1, BOTH)
+                    if odd:
+                        copy_x(s + 4, VECTOR, 88, P)
                 copy_gc(s + 1, 0, SCALAR)
                 root(s - 2, BOTH)
-                mm_gr(s + 1, 1)
-                if not odd:
-                    turn(s + 4)
-                    turn(s + 5)
 
-            s = LAST_X_STEP
-            mm_gr(s + 1, 0)
-            mm_gc(s + 1, 0)
+            def store_root(s, cols):
+                store(out_0, magnitude[s], s, cols, nc.scalar)
+
+            s = 11
             copy_gc(s, 1, VECTOR)
             copy_x(s + 3, SCALAR)
-            mm_gc(s + 1, 1)
             square_gr(s, 0)
             square_gr(s, 1)
-            square_gc(s, 0, HALF, VECTOR)
-            square_gc(s, HALF, N - GATE, VECTOR)
+            square_gc(s, 0, VECTOR)
+            square_gc(s, 1, VECTOR)
             copy_x(s + 4, VECTOR)
             diagonal(s, 0, FIRST_UNIT)
             window(s, s + 3)
-            root(s - 2, BOTH)
+            root(s - 2, BOTH, SCALAR)
             diagonal(s, 1, SECOND_UNIT)
             copy_gc(s + 1, 0, SCALAR)
+            store_root(s - 2, BOTH)
             diagonal(s + 1, 0, FIRST_UNIT)
-            root(s - 1, BOTH)
-            mm_gr(s + 1, 1)
-
-            for s in range(LAST_X_STEP + 1, LAST):
-                mm_gr(s + 1, 0)
-                mm_gc(s + 1, 0)
+            root(s - 1, BOTH, SCALAR)
+            for s in range(12, LAST):
                 copy_gc(s, 1, VECTOR)
-                mm_gc(s + 1, 1)
                 square_gr(s, 1)
+                store_root(s - 2, BOTH)
                 square_gr(s, 0)
-                square_gc(s, 0, HALF, VECTOR)
-                square_gc(s, HALF, N, VECTOR)
+                square_gc(s, 0, VECTOR)
+                square_gc(s, 1, VECTOR)
                 for units in (BOTH,) if s < LAST - 2 else (FIRST_UNIT, SECOND_UNIT):
                     add_squares(s, units, GPSIMD)
                 if s < LAST - 1:
                     diagonal(s, 1, SECOND_UNIT)
                     copy_gc(s + 1, 0, SCALAR)
                     diagonal(s + 1, 0, FIRST_UNIT)
-                    root(s - 1, BOTH)
+                    root(s - 1, BOTH, SCALAR)
                 else:
-                    root(s - 1, FIRST_UNIT)
+                    root(s - 1, FIRST_UNIT, SCALAR)
                     diagonal(s, 1, SECOND_UNIT)
                     copy_gc(s + 1, 0, SCALAR)
+                    store_root(s - 1, FIRST_UNIT)
                     copy_gc(s + 1, 1, VECTOR)
-                    root(s - 1, SECOND_UNIT)
+                    root(s - 1, SECOND_UNIT, SCALAR)
                     diagonal(s + 1, 0, FIRST_UNIT)
-                mm_gr(s + 1, 1)
-
             square_gr(LAST, 1)
+            store_root(LAST - 2, SECOND_UNIT)
             square_gr(LAST, 0)
-            square_gc(LAST, 0, HALF, VECTOR)
+            square_gc(LAST, 0, VECTOR)
             diagonal(LAST, 1, SECOND_UNIT)
-            root(LAST - 1, FIRST_UNIT)
-            square_gc(LAST, HALF, N - VECTOR_COLUMNS_END, SCALAR)
-            square_gc(LAST, N - VECTOR_COLUMNS_END, N, VECTOR)
+            root(LAST - 1, FIRST_UNIT, SCALAR)
+            square_copy(LAST, 1, 0, 192)
+            square_gc(LAST, 1, VECTOR, 192, HALF)
             add_squares(LAST, FIRST_UNIT, VECTOR)
-            root(LAST - 1, SECOND_UNIT)
+            root(LAST - 1, SECOND_UNIT, SCALAR)
+            store_root(LAST - 1, FIRST_UNIT)
             add_squares(LAST, SECOND_UNIT, VECTOR)
             root(LAST, FIRST_UNIT)
-            root(LAST, SECOND_UNIT)
+            store_root(LAST - 1, SECOND_UNIT)
+            root(LAST, SECOND_UNIT, SCALAR)
+            store_root(LAST, SECOND_UNIT)

@@ -114,14 +114,19 @@ def tile_patch_gradient_magnitude_s1_kernel(tc, patches, d_row, d_col_words, d_c
                     nc.tensor.transpose(bank[:, g, u, :], words[:, 2 * P * g + u : 2 * P * (g + 1) : 2], ident[:])
             return bank
 
-        def product(kind, s, j):
+        def product(kind, s, j, only=None):
             m, h = unit(s, j)
             cols = slice(h * HALF, (h + 1) * HALF)
             col_passes = [(g, dc_words[:, h, g, :].bitcast(FP4X4), dc_scales[h][:, g, :]) for g in range(PASSES)]
             row_passes = [(g, dr_codes[:, g, cols].bitcast(FP8X4), dr_scales[:, g, cols]) for g in range(PASSES)]
             passes = {GC: col_passes, GR: row_passes, SUM: col_passes + row_passes}[kind]
-            bank = psum.tile([P, HALF], F32, tag="bank")
+            if (kind, s, j) in banks:
+                bank = banks[kind, s, j]
+            else:
+                bank = psum.tile([P, HALF], F32, tag="bank")
             for i, (g, words, scales) in enumerate(passes):
+                if only is not None and i != only:
+                    continue
                 rows = slice(g * P, (g + 1) * P)
                 nc.tensor.matmul_mx(
                     out=bank[:],
@@ -134,11 +139,16 @@ def tile_patch_gradient_magnitude_s1_kernel(tc, patches, d_row, d_col_words, d_c
                 )
             return bank
 
-        jobs = [(TURN, 0), (TURN, 1), (GC, 0, 0), (GC, 0, 1), (TURN, 2), (TURN, 3), (GR, 0, 0), (GR, 0, 1)]
+        SUMMED = (12, 14)
+        jobs = [(TURN, 0), (TURN, 1), (GC, 0, 0), (GC, 0, 1), (GR, 0, 0, 0), (TURN, 2), (TURN, 3), (GR, 0, 1, 0), (GR, 0, 0, 1), (GR, 0, 1, 1)]
         jobs.extend([(GC, 1, 0), (GR, 1, 0), (GC, 1, 1), (GR, 1, 1), (GC, 2, 0), (TURN, 4), (TURN, 5), (GC, 2, 1), (GR, 2, 0), (GR, 2, 1)])
         for s in range(3, TILES):
             jobs.extend([(GC, s, 0), (GC, s, 1), (GR, s, 0)] if s < 12 else [(GR, s, 0), (GC, s, 0), (GC, s, 1)])
+            if s in SUMMED:
+                jobs.append((SUM, s, 0))
             jobs.append((GR, s, 1))
+            if s == LAST:
+                jobs.append((SUM, s, 1))
             if s % 2 == 1 and s + 4 < TILES:
                 jobs.extend([(TURN, s + 3), (TURN, s + 4)])
         given, emptied, readers, quantised = [], [], {}, set()
@@ -150,10 +160,12 @@ def tile_patch_gradient_magnitude_s1_kernel(tc, patches, d_row, d_col_words, d_c
                     banks[job] = turn(job[1])
                 else:
                     m, h = unit(job[1], job[2])
-                    if m not in quantised or (job[0] != GC and not all((g, h) in quantised for g in range(PASSES))):
+                    if m not in quantised or (job[0] != GC and not all((g, h) in quantised for g in job[3:] or range(PASSES))):
                         return
-                    banks[job] = product(job[0], job[1], job[2])
+                    banks[job[:3]] = product(*job)
                 given.append(job)
+                if job[3:] == (1,):
+                    emptied.append(job)
 
         def was_read(job, of):
             readers[job] = readers.get(job, 0) + 1
@@ -164,7 +176,8 @@ def tile_patch_gradient_magnitude_s1_kernel(tc, patches, d_row, d_col_words, d_c
         def copy_x(m, engine, lo=0, hi=P):
             if m not in x_grouped:
                 pair = stage.tile([P, 2 * PART], BF16, align_bytes=64)
-                x_grouped[m], x_grouped[m + 1], x_grouped[m, "pair"] = pair[:, :PART], pair[:, PART:], pair
+                even = m - m % 2
+                x_grouped[even], x_grouped[even + 1], x_grouped[even, "pair"] = pair[:, :PART], pair[:, PART:], pair
             dst = x_grouped[m].bitcast(F32).rearrange("p (g r u) -> p g r u", g=PASSES, u=2)[:, :, lo:hi, :]
             move(engine, dst, banks[TURN, m][:, :, :, lo:hi].rearrange("p g u r -> p g r u"))
             was_read((TURN, m), 1 if hi - lo == P else 2)
@@ -318,19 +331,19 @@ def tile_patch_gradient_magnitude_s1_kernel(tc, patches, d_row, d_col_words, d_c
             regroup(0, LEFT, 128, HALF, VECTOR)
             quant_x(1, 1)
             quant_d(0, LEFT, [(0, HALF)])
-            regroup(1, LEFT, 0, 192, SCALAR)
-            regroup(1, LEFT, 192, HALF, VECTOR)
-            copy_gc(0, 0, SCALAR)
+            regroup(1, LEFT, 0, 224, SCALAR)
+            regroup(1, LEFT, 224, HALF, VECTOR)
+            copy_gc(0, 0, VECTOR)
             quant_d(1, LEFT, [(0, HALF)])
             copy_gc(0, 1, SCALAR)
             square_gc(0, 0, VECTOR)
             copy_x(2, SCALAR)
             copy_x(3, SCALAR)
-            regroup(0, RIGHT, 0, P, VECTOR)
             quant_x(2, 1)
-            regroup(0, RIGHT, P, 2 * P, VECTOR)
+            regroup(0, RIGHT, 0, 96, SCALAR)
+            regroup(0, RIGHT, 96, 224, VECTOR)
             quant_x(3, 1)
-            regroup(0, RIGHT, 2 * P, HALF, VECTOR)
+            regroup(0, RIGHT, 224, HALF, VECTOR)
             square_gr(0, 0)
             square_gr(0, 1)
             copy_gc(1, 0, SCALAR)
@@ -348,8 +361,8 @@ def tile_patch_gradient_magnitude_s1_kernel(tc, patches, d_row, d_col_words, d_c
             gate(0)
             quant_d(1, RIGHT, [(0, HALF)])
             add_squares(0, BOTH, GPSIMD)
-            square_copy(1, 1)
             copy_gc(2, 0, SCALAR)
+            square_copy(1, 1)
             copy_x(4, SCALAR)
             copy_x(5, SCALAR)
             copy_gc(2, 1, SCALAR)
@@ -373,97 +386,126 @@ def tile_patch_gradient_magnitude_s1_kernel(tc, patches, d_row, d_col_words, d_c
                 quant_x(m, 2)
                 add_squares(s, BOTH, GPSIMD)
 
-            for s in range(3, 11):
-                odd = s % 2 == 1
-                summed = False
-                squares_ahead = None if odd else max(0, 2 - (s - 4) // 2)
-                if summed:
-                    square_gr(s, 1)
-                    square_gc(s, 1, SCALAR, of=1)
-                    square_gr(s, 0)
-                    window(s - 1, s + 2)
-                    square_gc(s, 0, VECTOR)
-                    add_squares(s, BOTH, GPSIMD)
-                    diagonal(s, 0)
-                    copy_sum(s, 1, BOTH)
+            def first_gc(s, engine):
+                if s in SUMMED:
+                    square_gc(s, 0, SCALAR, of=1)
                 else:
-                    copy_gc(s, 1, VECTOR)
-                    if squares_ahead == 0:
-                        window(s - 1, s + 2)
-                    square_gr(s, 0)
-                    square_gr(s, 1)
+                    copy_gc(s, 0, engine)
+
+            for s in range(3, 9):
+                odd = s % 2 == 1
+                squares_ahead = None if odd else max(0, 2 - (s - 4) // 2)
+                copy_gc(s, 1, VECTOR)
+                if squares_ahead == 0:
+                    window(s - 1, s + 2)
+                square_gr(s, 0, 1 if s in SUMMED else 2)
+                square_gr(s, 1)
+                if s not in SUMMED:
                     square_gc(s, 0, VECTOR)
-                    if squares_ahead == 1:
-                        window(s - 1, s + 2)
-                    square_gc(s, 1, VECTOR)
-                    if squares_ahead == 2:
-                        window(s - 1, s + 2)
-                    if not odd:
-                        add_squares(s, BOTH, GPSIMD)
-                    if odd:
-                        copy_x(s + 3, SCALAR)
+                if squares_ahead == 1:
+                    window(s - 1, s + 2)
+                square_gc(s, 1, VECTOR)
+                if squares_ahead == 2:
+                    window(s - 1, s + 2)
+                if not odd:
+                    add_squares(s, BOTH, GPSIMD)
+                if odd:
+                    copy_x(s + 3, SCALAR)
+                    if s + 1 not in SUMMED:
                         copy_x(s + 4, SCALAR, 0, 88)
+                if s in SUMMED:
+                    copy_sum(s, 0)
+                else:
                     diagonal(s, 0)
-                    diagonal(s, 1, BOTH)
-                    if odd:
-                        copy_x(s + 4, VECTOR, 88, P)
-                copy_gc(s + 1, 0, SCALAR)
+                diagonal(s, 1, BOTH)
+                if odd:
+                    copy_x(s + 4, VECTOR, 0 if s + 1 in SUMMED else 88, P)
+                first_gc(s + 1, SCALAR)
                 root(s - 2, BOTH)
 
-            def store_root(s, cols):
-                store(out_0, magnitude[s], s, cols, nc.scalar)
-
-            s = 11
+            s = 9
             copy_gc(s, 1, VECTOR)
+            square_gr(s, 0)
+            square_gr(s, 1)
+            square_gc(s, 0, VECTOR)
+            copy_x(s + 4, VECTOR, 88, P)
+            square_gc(s, 1, VECTOR)
             copy_x(s + 3, SCALAR)
+            copy_x(s + 4, SCALAR, 0, 88)
+            diagonal(s, 0)
+            diagonal(s, 1, BOTH)
+            window(s, s + 3)
+            copy_gc(s + 1, 0, SCALAR)
+            root(s - 2, BOTH)
+            s = 10
+            copy_gc(s, 1, VECTOR)
             square_gr(s, 0)
             square_gr(s, 1)
             square_gc(s, 0, VECTOR)
             square_gc(s, 1, VECTOR)
+            add_squares(s, BOTH, GPSIMD)
+            root(s - 2, BOTH)
+            diagonal(s, 0)
+            copy_gc(s + 1, 0, VECTOR)
+            diagonal(s, 1, BOTH)
+            root(s - 1, BOTH)
+            s = 11
+            copy_gc(s, 1, VECTOR)
+            copy_x(s + 3, SCALAR)
             copy_x(s + 4, VECTOR)
-            diagonal(s, 0, FIRST_UNIT)
+            square_gr(s, 0)
+            square_gr(s, 1)
+            square_gc(s, 0, VECTOR)
+            square_gc(s, 1, VECTOR)
             window(s, s + 3)
-            root(s - 2, BOTH, SCALAR)
-            diagonal(s, 1, SECOND_UNIT)
+            root(s - 1, BOTH)
+            first_gc(s + 1, SCALAR)
+            diagonal(s, 0)
+            copy_gc(s + 1, 1, VECTOR)
+            diagonal(s, 1, BOTH)
+            s = 12
+            square_gr(s, 0, 1)
+            square_gr(s, 1)
+            square_gc(s, 1, VECTOR)
+            add_squares(s, BOTH, GPSIMD)
+            copy_sum(s, 0, FIRST_UNIT)
             copy_gc(s + 1, 0, SCALAR)
-            store_root(s - 2, BOTH)
+            diagonal(s, 1, SECOND_UNIT)
+            root(s - 1, BOTH)
             diagonal(s + 1, 0, FIRST_UNIT)
-            root(s - 1, BOTH, SCALAR)
-            for s in range(12, LAST):
-                copy_gc(s, 1, VECTOR)
-                square_gr(s, 1)
-                store_root(s - 2, BOTH)
-                square_gr(s, 0)
-                square_gc(s, 0, VECTOR)
-                square_gc(s, 1, VECTOR)
-                for units in (BOTH,) if s < LAST - 2 else (FIRST_UNIT, SECOND_UNIT):
-                    add_squares(s, units, GPSIMD)
-                if s < LAST - 1:
-                    diagonal(s, 1, SECOND_UNIT)
-                    copy_gc(s + 1, 0, SCALAR)
-                    diagonal(s + 1, 0, FIRST_UNIT)
-                    root(s - 1, BOTH, SCALAR)
-                else:
-                    root(s - 1, FIRST_UNIT, SCALAR)
-                    diagonal(s, 1, SECOND_UNIT)
-                    copy_gc(s + 1, 0, SCALAR)
-                    store_root(s - 1, FIRST_UNIT)
-                    copy_gc(s + 1, 1, VECTOR)
-                    root(s - 1, SECOND_UNIT, SCALAR)
-                    diagonal(s + 1, 0, FIRST_UNIT)
-            square_gr(LAST, 1)
-            store_root(LAST - 2, SECOND_UNIT)
-            square_gr(LAST, 0)
-            square_gc(LAST, 0, VECTOR)
-            diagonal(LAST, 1, SECOND_UNIT)
-            root(LAST - 1, FIRST_UNIT, SCALAR)
-            square_copy(LAST, 1, 0, 192)
-            square_gc(LAST, 1, VECTOR, 192, HALF)
-            add_squares(LAST, FIRST_UNIT, VECTOR)
-            root(LAST - 1, SECOND_UNIT, SCALAR)
-            store_root(LAST - 1, FIRST_UNIT)
-            add_squares(LAST, SECOND_UNIT, VECTOR)
-            root(LAST, FIRST_UNIT)
-            store_root(LAST - 1, SECOND_UNIT)
-            root(LAST, SECOND_UNIT, SCALAR)
-            store_root(LAST, SECOND_UNIT)
+            s = 13
+            copy_gc(s, 1, VECTOR)
+            square_gr(s, 1)
+            square_gr(s, 0)
+            square_gc(s, 0, VECTOR)
+            add_squares(s, FIRST_UNIT, GPSIMD)
+            diagonal(s, 1, SECOND_UNIT)
+            root(s - 1, BOTH)
+            square_gc(s, 1, VECTOR)
+            add_squares(s, SECOND_UNIT, GPSIMD)
+            first_gc(s + 1, SCALAR)
+            s = 14
+            copy_gc(s, 1, VECTOR)
+            copy_sum(s, 0, FIRST_UNIT)
+            square_gr(s, 0, 1)
+            add_squares(s, FIRST_UNIT, GPSIMD)
+            root(s - 1, FIRST_UNIT)
+            diagonal(s, 1, SECOND_UNIT)
+            square_gr(s, 1)
+            square_gc(s, 1, VECTOR)
+            add_squares(s, SECOND_UNIT, GPSIMD)
+            copy_gc(s + 1, 0, VECTOR)
+            root(s - 1, SECOND_UNIT)
+            s = LAST
+            square_gr(s, 1, 1)
+            diagonal(s, 0, FIRST_UNIT)
+            root(s - 1, FIRST_UNIT)
+            square_gc(s, 0, VECTOR)
+            copy_sum(s, 1, SECOND_UNIT)
+            square_gr(s, 0)
+            square_gc(s, 1, SCALAR, of=1)
+            add_squares(s, FIRST_UNIT, VECTOR)
+            root(s - 1, SECOND_UNIT)
+            add_squares(s, SECOND_UNIT, VECTOR)
+            root(s, FIRST_UNIT)
+            root(s, SECOND_UNIT)

@@ -67,7 +67,7 @@ def tile_patch_gradient_magnitude_s1_kernel(tc, patches, d_row, d_col_words, d_c
 
         def quad_rows(tensor, m):
             first = m // QUAD * QUAD * P
-            return tensor[first : first + QUAD * P, :].rearrange("(p a) k -> p a k", a=QUAD)
+            return tensor[first : first + QUAD * P, :].rearrange("(a p) k -> p a k", a=QUAD)
 
         def load_x(m, count):
             at = m % RAW_TILES

@@ -62,6 +62,7 @@ def tile_patch_gradient_magnitude_s1_kernel(tc, patches, d_row, d_col_words, d_c
         right_scales = keep.tile([P, PASSES, HALF], U8, align_bytes=64)
         dc_scales = [left_scales, right_scales]
 
+        first_pair = stage.tile([P, 2 * PART], BF16, tag="pair", align_bytes=64)
         x_grouped, dr_raw, dr_grouped = {}, {}, {}
         banks, gc_sb, gc_sq, magnitude, diag = {}, {}, {}, {}, {}
 
@@ -106,12 +107,12 @@ def tile_patch_gradient_magnitude_s1_kernel(tc, patches, d_row, d_col_words, d_c
                 return m // 2 + h * SPLIT_STEPS, m % 2
             return m, h
 
-        def turn(m):
+        def turn(m, passes=range(PASSES)):
             bank = psum.tile([P, PASSES, 2, P], F32, tag="bank")
-            words = x_raw[:, m % RAW_TILES, :].bitcast(F32)
-            for g in range(PASSES):
+            for g in passes:
+                words = x_raw[:, m % RAW_TILES, g * K_PASS : (g + 1) * K_PASS].bitcast(F32)
                 for u in range(2):
-                    nc.tensor.transpose(bank[:, g, u, :], words[:, 2 * P * g + u : 2 * P * (g + 1) : 2], ident[:])
+                    nc.tensor.transpose(bank[:, g, u, :], words[:, u : 2 * P : 2], ident[:])
             return bank
 
         def product(kind, s, j, only=None):
@@ -139,11 +140,20 @@ def tile_patch_gradient_magnitude_s1_kernel(tc, patches, d_row, d_col_words, d_c
                 )
             return bank
 
-        SUMMED = (12, 14)
-        jobs = [(TURN, 0), (TURN, 1), (GC, 0, 0), (GC, 0, 1), (GR, 0, 0, 0), (TURN, 2), (TURN, 3), (GR, 0, 1, 0), (GR, 0, 0, 1), (GR, 0, 1, 1)]
+        SUMMED = (11, 12, 14)
+        jobs = [(TURN, 0, 0), (TURN, 0, 1), (TURN, 1), (GC, 0, 0), (GC, 0, 1), (GR, 0, 0, 0), (TURN, 2), (TURN, 3), (GR, 0, 1, 0), (GR, 0, 0, 1), (GR, 0, 1, 1)]
         jobs.extend([(GC, 1, 0), (GR, 1, 0), (GC, 1, 1), (GR, 1, 1), (GC, 2, 0), (TURN, 4), (TURN, 5), (GC, 2, 1), (GR, 2, 0), (GR, 2, 1)])
         for s in range(3, TILES):
-            jobs.extend([(GC, s, 0), (GC, s, 1), (GR, s, 0)] if s < 12 else [(GR, s, 0), (GC, s, 0), (GC, s, 1)])
+            late = {
+                12: [(GC, s, 0), (GC, s, 1), (GR, s, 0), (GR, s, 1), (SUM, s, 0)],
+                13: [(GC, s, 0), (GR, s, 1), (GC, s, 1), (GR, s, 0)],
+                14: [(GC, s, 0), (GC, s, 1), (GR, s, 1), (GR, s, 0), (SUM, s, 0)],
+                15: [(GR, s, 1), (GC, s, 0), (GR, s, 0), (GC, s, 1), (SUM, s, 1)],
+            }
+            if s in late:
+                jobs.extend(late[s])
+                continue
+            jobs.extend([(GC, s, 0), (GC, s, 1), (GR, s, 0)])
             if s in SUMMED:
                 jobs.append((SUM, s, 0))
             jobs.append((GR, s, 1))
@@ -157,10 +167,10 @@ def tile_patch_gradient_magnitude_s1_kernel(tc, patches, d_row, d_col_words, d_c
             while len(given) < len(jobs) and len(given) - len(emptied) < BANKS:
                 job = jobs[len(given)]
                 if job[0] == TURN:
-                    banks[job] = turn(job[1])
+                    banks[job] = turn(job[1]) if len(job) == 2 else turn(job[1], job[2:])
                 else:
                     m, h = unit(job[1], job[2])
-                    if m not in quantised or (job[0] != GC and not all((g, h) in quantised for g in job[3:] or range(PASSES))):
+                    if (("x0", job[3]) if m == 0 and job[3:] else m) not in quantised or (job[0] != GC and not all((g, h) in quantised for g in job[3:] or range(PASSES))):
                         return
                     banks[job[:3]] = product(*job)
                 given.append(job)
@@ -181,6 +191,18 @@ def tile_patch_gradient_magnitude_s1_kernel(tc, patches, d_row, d_col_words, d_c
             dst = x_grouped[m].bitcast(F32).rearrange("p (g r u) -> p g r u", g=PASSES, u=2)[:, :, lo:hi, :]
             move(engine, dst, banks[TURN, m][:, :, :, lo:hi].rearrange("p g u r -> p g r u"))
             was_read((TURN, m), 1 if hi - lo == P else 2)
+
+        def copy_x_pass(g, engine):
+            dst = first_pair[:, g * K_PASS : (g + 1) * K_PASS].bitcast(F32).rearrange("p (r u) -> p r u", u=2)
+            move(engine, dst, banks[TURN, 0, g][:, g, :, :].rearrange("p u r -> p r u"))
+            was_read((TURN, 0, g), 1)
+
+        def quant_x_pass(g):
+            rows = slice(g * P, (g + 1) * P)
+            nc.vector.quantize_mx(out=x_codes[:, 0, rows].bitcast(FP8X4), scales=x_scales[:, 0, rows], in_=first_pair[:, g * K_PASS : (g + 1) * K_PASS])
+            if g == 1:
+                quantised.add(0)
+            quantised.add(("x0", g))
 
         def quant_x(m, count):
             nc.vector.quantize_mx(
@@ -303,6 +325,7 @@ def tile_patch_gradient_magnitude_s1_kernel(tc, patches, d_row, d_col_words, d_c
         nc.gpsimd.memset(one[:], 1.0)
         make_identity(nc, ident[:])
 
+        x_grouped[1] = first_pair[:, PART:]
         with tc.manual_schedule():
             load_x(0, 1)
             load_x(1, 1)
@@ -324,9 +347,12 @@ def tile_patch_gradient_magnitude_s1_kernel(tc, patches, d_row, d_col_words, d_c
             nc.scalar.activation(out=warm[:], in_=one[:], func=ACT.Sqrt, bias=FLOOR_SQUARED)
 
             feed()
-            copy_x(0, VECTOR)
+            copy_x_pass(0, VECTOR)
+            copy_x_pass(1, SCALAR)
+            quant_x_pass(0)
+            quant_x_pass(1)
+            feed()
             copy_x(1, SCALAR)
-            quant_x(0, 1)
             regroup(0, LEFT, 0, 128, SCALAR)
             regroup(0, LEFT, 128, HALF, VECTOR)
             quant_x(1, 1)
@@ -444,35 +470,33 @@ def tile_patch_gradient_magnitude_s1_kernel(tc, patches, d_row, d_col_words, d_c
             square_gc(s, 0, VECTOR)
             square_gc(s, 1, VECTOR)
             add_squares(s, BOTH, GPSIMD)
+            diagonal(s, 0, FIRST_UNIT)
             root(s - 2, BOTH)
-            diagonal(s, 0)
-            copy_gc(s + 1, 0, VECTOR)
-            diagonal(s, 1, BOTH)
+            diagonal(s, 1, SECOND_UNIT)
+            first_gc(s + 1, SCALAR)
             root(s - 1, BOTH)
             s = 11
             copy_gc(s, 1, VECTOR)
-            copy_x(s + 3, SCALAR)
+            copy_x(s + 3, VECTOR)
             copy_x(s + 4, VECTOR)
-            square_gr(s, 0)
-            square_gr(s, 1)
-            square_gc(s, 0, VECTOR)
-            square_gc(s, 1, VECTOR)
-            window(s, s + 3)
-            root(s - 1, BOTH)
-            first_gc(s + 1, SCALAR)
-            diagonal(s, 0)
-            copy_gc(s + 1, 1, VECTOR)
-            diagonal(s, 1, BOTH)
-            s = 12
             square_gr(s, 0, 1)
             square_gr(s, 1)
             square_gc(s, 1, VECTOR)
-            add_squares(s, BOTH, GPSIMD)
+            window(s, s + 3)
             copy_sum(s, 0, FIRST_UNIT)
-            copy_gc(s + 1, 0, SCALAR)
+            root(s - 1, BOTH)
+            diagonal(s, 1, SECOND_UNIT)
+            first_gc(s + 1, SCALAR)
+            s = 12
+            copy_gc(s, 1, VECTOR)
+            square_gr(s, 0, 1)
+            square_gr(s, 1)
+            copy_sum(s, 0, FIRST_UNIT)
+            square_gc(s, 1, VECTOR)
+            add_squares(s, BOTH, GPSIMD)
+            copy_gc(s + 1, 0, VECTOR)
             diagonal(s, 1, SECOND_UNIT)
             root(s - 1, BOTH)
-            diagonal(s + 1, 0, FIRST_UNIT)
             s = 13
             copy_gc(s, 1, VECTOR)
             square_gr(s, 1)
@@ -480,32 +504,34 @@ def tile_patch_gradient_magnitude_s1_kernel(tc, patches, d_row, d_col_words, d_c
             square_gc(s, 0, VECTOR)
             add_squares(s, FIRST_UNIT, GPSIMD)
             diagonal(s, 1, SECOND_UNIT)
-            root(s - 1, BOTH)
+            diagonal(s, 0, FIRST_UNIT)
             square_gc(s, 1, VECTOR)
             add_squares(s, SECOND_UNIT, GPSIMD)
             first_gc(s + 1, SCALAR)
+            root(s - 1, BOTH)
             s = 14
             copy_gc(s, 1, VECTOR)
-            copy_sum(s, 0, FIRST_UNIT)
+            square_gr(s, 1)
+            copy_sum(s, 0)
+            diagonal(s, 1, BOTH)
             square_gr(s, 0, 1)
             add_squares(s, FIRST_UNIT, GPSIMD)
-            root(s - 1, FIRST_UNIT)
-            diagonal(s, 1, SECOND_UNIT)
-            square_gr(s, 1)
             square_gc(s, 1, VECTOR)
             add_squares(s, SECOND_UNIT, GPSIMD)
+            root(s - 1, FIRST_UNIT, SCALAR)
             copy_gc(s + 1, 0, VECTOR)
-            root(s - 1, SECOND_UNIT)
             s = LAST
             square_gr(s, 1, 1)
-            diagonal(s, 0, FIRST_UNIT)
+            root(s - 2, SECOND_UNIT, SCALAR)
+            store(out_0, magnitude[s - 2], s - 2, BOTH)
+            diagonal(s, 0)
+            square_gc(s, 1, SCALAR, of=1)
             root(s - 1, FIRST_UNIT)
             square_gc(s, 0, VECTOR)
-            copy_sum(s, 1, SECOND_UNIT)
+            copy_sum(s, 1, BOTH)
             square_gr(s, 0)
-            square_gc(s, 1, SCALAR, of=1)
-            add_squares(s, FIRST_UNIT, VECTOR)
-            root(s - 1, SECOND_UNIT)
             add_squares(s, SECOND_UNIT, VECTOR)
-            root(s, FIRST_UNIT)
+            root(s - 1, SECOND_UNIT)
+            add_squares(s, FIRST_UNIT, VECTOR)
             root(s, SECOND_UNIT)
+            root(s, FIRST_UNIT)

from contextlib import ExitStack

import concourse.mybir as mybir
from concourse.masks import make_identity

F32 = mybir.dt.float32
BF16 = mybir.dt.bfloat16
U32 = mybir.dt.uint32
I32 = mybir.dt.int32
U8 = mybir.dt.uint8
FP8X4 = mybir.dt.float8_e4m3fn_x4
FP4X4 = mybir.dt.float4_e2m1fn_x4
ACT = mybir.ActivationFunctionType
ALU = mybir.AluOpType

M, K, N = 2048, 1024, 1024
P = 128
PACK = 4
K_PASS = P * PACK
PASSES = K // K_PASS
HALF = 512
BANKS = 8
TILES = M // P
QUAD = 4
RAW_TILES = 16
FLOOR_SQUARED = 0.0625
FLOPS = 2 * 2 * M * K * N

LEFT, RIGHT = 0, 1
SCALAR, VECTOR, GPSIMD = "scalar", "vector", "gpsimd"
TURN, GC, GR, SUM = "turn", "gc", "gr", "sum"
BOTH, FIRST_UNIT, SECOND_UNIT = (0, N), (0, HALF), (HALF, N)

SPLIT_TILES = 4
SPLIT_STEPS = SPLIT_TILES // 2
LAST = TILES - 1
SCALAR_COLUMNS_FIRST = 128
GATE = 128
PART = K
GATED = (0, 1, 3, 5, 7, 9, 11)


def tile_patch_gradient_magnitude_s1_kernel(tc, patches, d_row, d_col_words, d_col_scales, out_0, out_1):
    nc = tc.nc
    with ExitStack() as ctx:
        keep = ctx.enter_context(tc.tile_pool(name="keep", bufs=1))
        stage = ctx.enter_context(tc.tile_pool(name="stage", bufs=2))
        work = ctx.enter_context(tc.tile_pool(name="work", bufs=4))
        outs = ctx.enter_context(tc.tile_pool(name="outs", bufs=TILES))
        psum = ctx.enter_context(tc.psum_pool(name="psum", bufs=BANKS))

        ident = keep.tile([P, P], F32)
        one = keep.tile([P, 1], F32)
        warm = keep.tile([P, 1], F32)
        x_raw = keep.tile([P, RAW_TILES, K], BF16, align_bytes=64)
        x_codes = keep.tile([P, TILES, PASSES * P], U32, align_bytes=64)
        x_scales = keep.tile([P, TILES, PASSES * P], U8, align_bytes=64)
        dr_codes = keep.tile([P, PASSES, N], U32, align_bytes=64)
        dr_scales = keep.tile([P, PASSES, N], U8, align_bytes=64)
        dc_words = keep.tile([P, 2, PASSES, 2 * HALF], U8, align_bytes=64)
        left_scales = keep.tile([P, PASSES, HALF], U8, align_bytes=64)
        right_scales = keep.tile([P, PASSES, HALF], U8, align_bytes=64)
        dc_scales = [left_scales, right_scales]

        first_pair = stage.tile([P, 2 * PART], BF16, tag="pair", align_bytes=64)
        x_grouped, dr_raw, dr_grouped = {}, {}, {}
        banks, gc_sb, gc_sq, magnitude, diag = {}, {}, {}, {}, {}

        def quad_rows(tensor, m):
            first = m // QUAD * QUAD * P
            return tensor[first : first + QUAD * P, :].rearrange("(a p) k -> p a k", a=QUAD)

        def load_x(m, count):
            at = m % RAW_TILES
            nc.sync.dma_start(out=x_raw[:, at : at + count, :], in_=quad_rows(patches, m)[:, m % QUAD : m % QUAD + count, :])

        def load_d_row(g, h):
            rows = d_row[g * K_PASS : (g + 1) * K_PASS, h * HALF : (h + 1) * HALF]
            raw = outs.tile([P, PACK, HALF], BF16, tag="diag", align_bytes=64)
            dr_raw[g, h] = raw
            nc.sync.dma_start(out=raw[:], in_=rows.rearrange("(p t) n -> p t n", t=PACK))

        def load_words(h, lo=0, hi=PASSES):
            words = d_col_words[lo:hi, :, 2 * h * HALF : 2 * (h + 1) * HALF]
            nc.sync.dma_start(out=dc_words[:, h, lo:hi, :].bitcast(I32), in_=words.rearrange("g p w -> p g w").bitcast(I32))

        def load_scales(h):
            for r in range(4):
                nc.sync.dma_start(
                    out=dc_scales[h][r:P:32, :, :].bitcast(I32),
                    in_=d_col_scales[:, r:16:4, h * HALF : (h + 1) * HALF].rearrange("g q n -> q g n").bitcast(I32),
                )

        def move(engine, dst, src):
            if engine == SCALAR:
                nc.scalar.copy(out=dst, in_=src)
            else:
                nc.vector.tensor_copy(out=dst, in_=src)

        def unit(s, j):
            if s < SPLIT_TILES:
                return 2 * (s % SPLIT_STEPS) + j, s // SPLIT_STEPS
            return s, j

        def place(m, h):
            if m < SPLIT_TILES:
                return m // 2 + h * SPLIT_STEPS, m % 2
            return m, h

        def turn(m, passes=range(PASSES)):
            bank = psum.tile([P, PASSES, 2, P], F32, tag="bank")
            for g in passes:
                words = x_raw[:, m % RAW_TILES, g * K_PASS : (g + 1) * K_PASS].bitcast(F32)
                for u in range(2):
                    nc.tensor.transpose(bank[:, g, u, :], words[:, u : 2 * P : 2], ident[:])
            return bank

        def product(kind, s, j, only=None):
            m, h = unit(s, j)
            cols = slice(h * HALF, (h + 1) * HALF)
            col_passes = [(g, dc_words[:, h, g, :].bitcast(FP4X4), dc_scales[h][:, g, :]) for g in range(PASSES)]
            row_passes = [(g, dr_codes[:, g, cols].bitcast(FP8X4), dr_scales[:, g, cols]) for g in range(PASSES)]
            passes = {GC: col_passes, GR: row_passes, SUM: col_passes + row_passes}[kind]
            if (kind, s, j) in banks:
                bank = banks[kind, s, j]
            else:
                bank = psum.tile([P, HALF], F32, tag="bank")
            for i, (g, words, scales) in enumerate(passes):
                if only is not None and i != only:
                    continue
                rows = slice(g * P, (g + 1) * P)
                nc.tensor.matmul_mx(
                    out=bank[:],
                    lhsT=x_codes[:, m, rows].bitcast(FP8X4),
                    lhsT_scale=x_scales[:, m, rows],
                    rhs=words,
                    rhs_scale=scales,
                    start=(i == 0),
                    stop=(i == len(passes) - 1),
                )
            return bank

        SUMMED = (11, 12, 14)
        jobs = [(TURN, 0, 0), (TURN, 0, 1), (TURN, 1), (GC, 0, 0), (GC, 0, 1), (GR, 0, 0, 0), (TURN, 2), (TURN, 3), (GR, 0, 1, 0), (GR, 0, 0, 1), (GR, 0, 1, 1)]
        jobs.extend([(GC, 1, 0), (GR, 1, 0), (GC, 1, 1), (GR, 1, 1), (GC, 2, 0), (TURN, 4), (TURN, 5), (GC, 2, 1), (GR, 2, 0), (GR, 2, 1)])
        for s in range(3, TILES):
            late = {
                12: [(GC, s, 0), (GC, s, 1), (GR, s, 0), (GR, s, 1), (SUM, s, 0)],
                13: [(GC, s, 0), (GR, s, 1), (GC, s, 1), (GR, s, 0)],
                14: [(GC, s, 0), (GC, s, 1), (GR, s, 1), (GR, s, 0), (SUM, s, 0)],
                15: [(GR, s, 1), (GC, s, 0), (GR, s, 0), (GC, s, 1), (SUM, s, 1)],
            }
            if s in late:
                jobs.extend(late[s])
                continue
            jobs.extend([(GC, s, 0), (GC, s, 1), (GR, s, 0)])
            if s in SUMMED:
                jobs.append((SUM, s, 0))
            jobs.append((GR, s, 1))
            if s == LAST:
                jobs.append((SUM, s, 1))
            if s % 2 == 1 and s + 4 < TILES:
                jobs.extend([(TURN, s + 3), (TURN, s + 4)])
        given, emptied, readers, quantised = [], [], {}, set()

        def feed():
            while len(given) < len(jobs) and len(given) - len(emptied) < BANKS:
                job = jobs[len(given)]
                if job[0] == TURN:
                    banks[job] = turn(job[1]) if len(job) == 2 else turn(job[1], job[2:])
                else:
                    m, h = unit(job[1], job[2])
                    if (("x0", job[3]) if m == 0 and job[3:] else m) not in quantised or (job[0] != GC and not all((g, h) in quantised for g in job[3:] or range(PASSES))):
                        return
                    banks[job[:3]] = product(*job)
                given.append(job)
                if job[3:] == (1,):
                    emptied.append(job)

        def was_read(job, of):
            readers[job] = readers.get(job, 0) + 1
            if readers[job] == of:
                emptied.append(job)
            feed()

        def copy_x(m, engine, lo=0, hi=P):
            if m not in x_grouped:
                pair = stage.tile([P, 2 * PART], BF16, align_bytes=64)
                even = m - m % 2
                x_grouped[even], x_grouped[even + 1], x_grouped[even, "pair"] = pair[:, :PART], pair[:, PART:], pair
            dst = x_grouped[m].bitcast(F32).rearrange("p (g r u) -> p g r u", g=PASSES, u=2)[:, :, lo:hi, :]
            move(engine, dst, banks[TURN, m][:, :, :, lo:hi].rearrange("p g u r -> p g r u"))
            was_read((TURN, m), 1 if hi - lo == P else 2)

        def copy_x_pass(g, engine):
            dst = first_pair[:, g * K_PASS : (g + 1) * K_PASS].bitcast(F32).rearrange("p (r u) -> p r u", u=2)
            move(engine, dst, banks[TURN, 0, g][:, g, :, :].rearrange("p u r -> p r u"))
            was_read((TURN, 0, g), 1)

        def quant_x_pass(g):
            rows = slice(g * P, (g + 1) * P)
            nc.vector.quantize_mx(out=x_codes[:, 0, rows].bitcast(FP8X4), scales=x_scales[:, 0, rows], in_=first_pair[:, g * K_PASS : (g + 1) * K_PASS])
            if g == 1:
                quantised.add(0)
            quantised.add(("x0", g))

        def quant_x(m, count):
            nc.vector.quantize_mx(
                out=x_codes[:, m : m + count, :].rearrange("p a w -> p (a w)").bitcast(FP8X4),
                scales=x_scales[:, m : m + count, :].rearrange("p a w -> p (a w)"),
                in_=x_grouped[m] if count == 1 else x_grouped[m, "pair"][:],
            )
            for a in range(count):
                quantised.add(m + a)
            feed()

        def regroup(g, h, lo, hi, engine):
            if (g, h) not in dr_grouped:
                grouped = outs.tile([P, PACK * HALF], BF16, tag="diag", align_bytes=64)
                dr_grouped[g, h] = grouped[:]
            dst, src = dr_grouped[g, h].rearrange("p (n t) -> p n t", t=PACK)[:, lo:hi, :], dr_raw[g, h][:, :, lo:hi]
            if engine == GPSIMD:
                nc.gpsimd.tensor_scalar(out=dst, in0=src.rearrange("p t n -> p n t"), scalar1=1.0, scalar2=0.0, op0=ALU.mult, op1=ALU.add)
            else:
                move(engine, dst.rearrange("p (c i) t -> p c t i", i=4), src.rearrange("p t (c i) -> p c t i", i=4))

        def quant_d(g, h, parts):
            for lo, hi in parts:
                cols = slice(h * HALF + lo, h * HALF + hi)
                nc.vector.quantize_mx(out=dr_codes[:, g, cols].bitcast(FP8X4), scales=dr_scales[:, g, cols], in_=dr_grouped[g, h][:, PACK * lo : PACK * hi])
            quantised.add((g, h))
            feed()

        def gc_copy(s, j):
            if s not in gc_sb:
                gc = work.tile([P, N], F32)
                gc_sb[s] = gc
            return gc_sb[s][:, j * HALF : (j + 1) * HALF]

        def diag_of(s, j):
            if s not in diag:
                dg = outs.tile([P, N], F32, tag="diag", align_bytes=64)
                diag[s] = dg
            return diag[s][:, j * HALF : (j + 1) * HALF]

        def copy_gc(s, j, engine, of=2):
            move(engine, gc_copy(s, j), banks[GC, s, j][:])
            was_read((GC, s, j), of)

        def squares(s):
            if s not in gc_sq:
                gc2 = work.tile([P, N], F32)
                gc_sq[s] = gc2
            return gc_sq[s]

        def square_gc(s, j, engine, lo=0, hi=HALF, of=2):
            hi = min(hi, HALF - GATE) if s in GATED and j == 1 else hi
            dst, bank = squares(s)[:, j * HALF + lo : j * HALF + hi], banks[GC, s, j][:, lo:hi]
            if engine == SCALAR:
                nc.scalar.activation(out=dst, in_=bank, func=ACT.Square)
            else:
                nc.vector.tensor_tensor(out=dst, in0=gc_copy(s, j)[:, lo:hi], in1=bank, op=ALU.mult)
            was_read((GC, s, j), of)

        def copy_sum(s, j, stored=None):
            nc.vector.tensor_copy(out=diag_of(s, j), in_=banks[SUM, s, j][:])
            was_read((SUM, s, j), 1)
            if stored is not None:
                store(out_1, diag[s], s, stored)

        def square_copy(s, j, lo=0, hi=HALF):
            hi = min(hi, HALF - GATE) if s in GATED and j == 1 else hi
            nc.scalar.activation(out=squares(s)[:, j * HALF + lo : j * HALF + hi], in_=gc_copy(s, j)[:, lo:hi], func=ACT.Square)
            was_read((GC, s, j), 2 if lo > 0 or hi >= HALF - GATE else 9)

        def gate(s):
            gc = gc_copy(s, 1)[:, HALF - GATE :]
            nc.vector.tensor_tensor(out=squares(s)[:, N - GATE :], in0=gc, in1=gc, op=ALU.mult)

        def store(tensor, tile, s, cols, queue=nc.sync):
            lo, hi = cols
            m, h = unit(s, 0)
            rows = quad_rows(tensor, m)
            if s < SPLIT_TILES:
                dst = rows[:, m % QUAD : m % QUAD + 2, h * HALF : (h + 1) * HALF]
                nc.sync.dma_start(out=dst, in_=tile[:].rearrange("p (j n) -> p j n", n=HALF))
            else:
                queue.dma_start(out=rows[:, m % QUAD, lo:hi], in_=tile[:, lo:hi])

        def diagonal(s, j, stored=None):
            nc.vector.tensor_tensor(out=diag_of(s, j), in0=gc_copy(s, j), in1=banks[GR, s, j][:], op=ALU.add)
            was_read((GR, s, j), 2)
            if stored is not None:
                store(out_1, diag[s], s, stored)

        def square_gr(s, j, of=2):
            if s not in magnitude:
                mag = outs.tile([P, N], F32)
                magnitude[s] = mag
            nc.scalar.activation(out=magnitude[s][:, j * HALF : (j + 1) * HALF], in_=banks[GR, s, j][:], func=ACT.Square)
            was_read((GR, s, j), of)

        def add_squares(s, units, engine):
            cols = slice(units[0], units[1])
            adder = nc.gpsimd if engine == GPSIMD else nc.vector
            adder.tensor_tensor(out=magnitude[s][:, cols], in0=magnitude[s][:, cols], in1=gc_sq[s][:, cols], op=ALU.add)

        def root(s, units, queue=None):
            cols = slice(units[0], units[1])
            nc.scalar.activation(out=magnitude[s][:, cols], in_=magnitude[s][:, cols], func=ACT.Sqrt, bias=FLOOR_SQUARED)
            if queue is None:
                store(out_0, magnitude[s], s, units)

        def empty_gc(m, h):
            s, j = place(m, h)
            square_gc(s, j, SCALAR)
            copy_gc(s, j, VECTOR)

        def empty_gr(s, j):
            square_gr(s, j)
            diagonal(s, j, BOTH if j == 1 else None)

        for scales in dc_scales:
            nc.vector.memset(scales[:].rearrange("p g n -> p (g n)").bitcast(I32), 0)
        nc.gpsimd.memset(one[:], 1.0)
        make_identity(nc, ident[:])

        x_grouped[1] = first_pair[:, PART:]
        with tc.manual_schedule():
            load_x(0, 1)
            load_x(1, 1)
            load_d_row(0, LEFT)
            load_scales(LEFT)
            for g in range(PASSES):
                load_words(LEFT, g, g + 1)
            load_d_row(1, LEFT)
            load_x(2, 1)
            load_x(3, 1)
            load_d_row(0, RIGHT)
            load_d_row(1, RIGHT)
            load_scales(RIGHT)
            load_words(RIGHT)
            load_x(4, 2)
            load_x(6, 2)
            for m in range(2 * QUAD, TILES, QUAD):
                load_x(m, QUAD)
            nc.scalar.activation(out=warm[:], in_=one[:], func=ACT.Sqrt, bias=FLOOR_SQUARED)

            feed()
            copy_x_pass(0, VECTOR)
            copy_x_pass(1, SCALAR)
            quant_x_pass(0)
            quant_x_pass(1)
            feed()
            copy_x(1, SCALAR)
            regroup(0, LEFT, 0, 128, SCALAR)
            regroup(0, LEFT, 128, HALF, VECTOR)
            quant_x(1, 1)
            quant_d(0, LEFT, [(0, HALF)])
            regroup(1, LEFT, 0, 224, SCALAR)
            regroup(1, LEFT, 224, HALF, VECTOR)
            copy_gc(0, 0, VECTOR)
            quant_d(1, LEFT, [(0, HALF)])
            copy_gc(0, 1, SCALAR)
            square_gc(0, 0, VECTOR)
            copy_x(2, SCALAR)
            copy_x(3, SCALAR)
            quant_x(2, 1)
            regroup(0, RIGHT, 0, 96, SCALAR)
            regroup(0, RIGHT, 96, 224, VECTOR)
            quant_x(3, 1)
            regroup(0, RIGHT, 224, HALF, VECTOR)
            square_gr(0, 0)
            square_gr(0, 1)
            copy_gc(1, 0, SCALAR)
            dr_grouped[1, RIGHT] = dr_raw[0, RIGHT][:].rearrange("p t n -> p (t n)")
            regroup(1, RIGHT, 128, HALF, GPSIMD)
            regroup(1, RIGHT, 0, 128, SCALAR)
            diagonal(0, 0)
            diagonal(0, 1, BOTH)
            square_gc(1, 0, VECTOR)
            copy_gc(1, 1, VECTOR)
            square_gc(0, 1, VECTOR)
            square_gr(1, 0)
            square_gr(1, 1)
            quant_d(0, RIGHT, [(0, HALF)])
            gate(0)
            quant_d(1, RIGHT, [(0, HALF)])
            add_squares(0, BOTH, GPSIMD)
            copy_gc(2, 0, SCALAR)
            square_copy(1, 1)
            copy_x(4, SCALAR)
            copy_x(5, SCALAR)
            copy_gc(2, 1, SCALAR)
            diagonal(1, 0)
            diagonal(1, 1, BOTH)
            square_gc(2, 0, VECTOR)
            square_gc(2, 1, VECTOR)
            square_gr(2, 0)
            square_gr(2, 1)
            diagonal(2, 0)
            copy_gc(3, 0, SCALAR)
            gate(1)
            quant_x(4, 2)
            add_squares(1, BOTH, GPSIMD)
            add_squares(2, BOTH, GPSIMD)
            diagonal(2, 1, BOTH)
            root(0, BOTH)

            def window(s, m):
                gate(s)
                quant_x(m, 2)
                add_squares(s, BOTH, GPSIMD)

            def first_gc(s, engine):
                if s in SUMMED:
                    square_gc(s, 0, SCALAR, of=1)
                else:
                    copy_gc(s, 0, engine)

            for s in range(3, 9):
                odd = s % 2 == 1
                squares_ahead = None if odd else max(0, 2 - (s - 4) // 2)
                copy_gc(s, 1, VECTOR)
                if squares_ahead == 0:
                    window(s - 1, s + 2)
                square_gr(s, 0, 1 if s in SUMMED else 2)
                square_gr(s, 1)
                if s not in SUMMED:
                    square_gc(s, 0, VECTOR)
                if squares_ahead == 1:
                    window(s - 1, s + 2)
                square_gc(s, 1, VECTOR)
                if squares_ahead == 2:
                    window(s - 1, s + 2)
                if not odd:
                    add_squares(s, BOTH, GPSIMD)
                if odd:
                    copy_x(s + 3, SCALAR)
                    if s + 1 not in SUMMED:
                        copy_x(s + 4, SCALAR, 0, 88)
                if s in SUMMED:
                    copy_sum(s, 0)
                else:
                    diagonal(s, 0)
                diagonal(s, 1, BOTH)
                if odd:
                    copy_x(s + 4, VECTOR, 0 if s + 1 in SUMMED else 88, P)
                first_gc(s + 1, SCALAR)
                root(s - 2, BOTH)

            s = 9
            copy_gc(s, 1, VECTOR)
            square_gr(s, 0)
            square_gr(s, 1)
            square_gc(s, 0, VECTOR)
            copy_x(s + 4, VECTOR, 88, P)
            square_gc(s, 1, VECTOR)
            copy_x(s + 3, SCALAR)
            copy_x(s + 4, SCALAR, 0, 88)
            diagonal(s, 0)
            diagonal(s, 1, BOTH)
            window(s, s + 3)
            copy_gc(s + 1, 0, SCALAR)
            root(s - 2, BOTH)
            s = 10
            copy_gc(s, 1, VECTOR)
            square_gr(s, 0)
            square_gr(s, 1)
            square_gc(s, 0, VECTOR)
            square_gc(s, 1, VECTOR)
            add_squares(s, BOTH, GPSIMD)
            diagonal(s, 0, FIRST_UNIT)
            root(s - 2, BOTH)
            diagonal(s, 1, SECOND_UNIT)
            first_gc(s + 1, SCALAR)
            root(s - 1, BOTH)
            s = 11
            copy_gc(s, 1, VECTOR)
            copy_x(s + 3, VECTOR)
            copy_x(s + 4, VECTOR)
            square_gr(s, 0, 1)
            square_gr(s, 1)
            square_gc(s, 1, VECTOR)
            window(s, s + 3)
            copy_sum(s, 0, FIRST_UNIT)
            root(s - 1, BOTH)
            diagonal(s, 1, SECOND_UNIT)
            first_gc(s + 1, SCALAR)
            s = 12
            copy_gc(s, 1, VECTOR)
            square_gr(s, 0, 1)
            square_gr(s, 1)
            copy_sum(s, 0, FIRST_UNIT)
            square_gc(s, 1, VECTOR)
            add_squares(s, BOTH, GPSIMD)
            copy_gc(s + 1, 0, VECTOR)
            diagonal(s, 1, SECOND_UNIT)
            root(s - 1, BOTH)
            s = 13
            copy_gc(s, 1, VECTOR)
            square_gr(s, 1)
            square_gr(s, 0)
            square_gc(s, 0, VECTOR)
            add_squares(s, FIRST_UNIT, GPSIMD)
            diagonal(s, 1, SECOND_UNIT)
            diagonal(s, 0, FIRST_UNIT)
            square_gc(s, 1, VECTOR)
            add_squares(s, SECOND_UNIT, GPSIMD)
            first_gc(s + 1, SCALAR)
            root(s - 1, BOTH)
            s = 14
            copy_gc(s, 1, VECTOR)
            square_gr(s, 1)
            copy_sum(s, 0)
            diagonal(s, 1, BOTH)
            square_gr(s, 0, 1)
            add_squares(s, FIRST_UNIT, GPSIMD)
            square_gc(s, 1, VECTOR)
            add_squares(s, SECOND_UNIT, GPSIMD)
            root(s - 1, FIRST_UNIT, SCALAR)
            copy_gc(s + 1, 0, VECTOR)
            s = LAST
            square_gr(s, 1, 1)
            root(s - 2, SECOND_UNIT, SCALAR)
            store(out_0, magnitude[s - 2], s - 2, BOTH)
            diagonal(s, 0)
            square_gc(s, 1, SCALAR, of=1)
            root(s - 1, FIRST_UNIT)
            square_gc(s, 0, VECTOR)
            copy_sum(s, 1, BOTH)
            square_gr(s, 0)
            add_squares(s, SECOND_UNIT, VECTOR)
            root(s - 1, SECOND_UNIT)
            add_squares(s, FIRST_UNIT, VECTOR)
            root(s, SECOND_UNIT)
            root(s, FIRST_UNIT)
